import numpy as np, ml_dtypes
CORES = [40,41,42,43,44,45,46,47]
N = 8
import mx_ref
BF = ml_dtypes.bfloat16
def gcols(t, e):
    v = np.concatenate([t.reshape(8, 16, -1, 4), np.zeros((8, 16, 1, 4), BF)], axis=2)
    return np.ascontiguousarray(np.stack([v[g][:, e[g]] for g in range(8)])).reshape(128, -1)
def gpick(z, e):
    return np.concatenate([z[16 * g:16 * g + 16][:, e[g]] for g in range(8)])
def tile(rs):
    return np.stack(rs, axis=2).reshape(128, -1).astype(BF)
def pick(q, e):
    c = np.concatenate([q[0].reshape(128, -1, 4), np.zeros((128, 1, 4), np.uint8)], axis=1); s = np.concatenate([q[1], np.ones((16, 1), np.uint8)], axis=1)
    return (np.ascontiguousarray(c[:, e].reshape(128, -1)), np.ascontiguousarray(s[:, e]))
def join(*qs):
    return (np.concatenate([q[0] for q in qs], axis=1), np.concatenate([q[1] for q in qs], axis=1))
def put(q, e, v):
    c, s = q[0].reshape(128, -1, 4).copy(), q[1].copy(); c[:, e] = v[0].reshape(128, -1, 4); s[:, e] = v[1]
    return (c.reshape(128, -1), s)
def pk(c, s):
    return (np.ascontiguousarray(c), mx_ref.live(s))
def emit(q):
    return q[0], q[1]
def packed(v, rng):
    q = [mx_ref.quantize(np.ascontiguousarray(v[r])) for r in range(N)]
    return np.stack([a for a, b in q]), np.stack([mx_ref.plane(b, rng) for a, b in q])
def values_of_codes():
    e, c = np.zeros((128, 128, 4), np.float32), np.zeros((128, 2, 4), np.uint8)
    e[np.arange(128), np.arange(128), 0] = 1
    c[:127, :, 0] = np.arange(256).reshape(2, 128).T[:127]
    return mx_ref.matmul(mx_ref.quantize(e.reshape(128, 512).astype(BF)), (c.reshape(128, 8), np.full((16, 2), 127, np.uint8))).T.reshape(-1).astype(np.float64)
CODE_VALUE, SCALE_VALUE = values_of_codes(), 2.0 ** (np.arange(256) - 127.0)
def decode(q):
    return (CODE_VALUE[q[0]].reshape(16, 8, -1, 4) * SCALE_VALUE[q[1]][:, None, :, None] + 0.0).reshape(128, -1).astype(np.float32)
def f(rng, *shape):
    return mx_ref.flush((rng.standard_normal(shape, dtype=np.float32) * np.exp2(rng.integers(-2, 3, shape[:-1] + (1,)))).astype(BF))
def wide(rng, *shape, cols=0):
    v = rng.standard_normal(shape, dtype=np.float32) * np.exp2(rng.integers(-12, 13, shape)).astype(np.float32)
    if cols: v *= np.repeat(np.exp2(rng.integers(-cols, cols + 1, shape[:-2] + (1, shape[-1] // 4))) * (rng.random(shape[:-2] + (1, shape[-1] // 4)) > 0.0625), 4, axis=-1).astype(np.float32)
    return mx_ref.flush(v.astype(BF))
C, A, K = 256, 64, 128
STEP = [1, 2, 4]
MANY = np.repeat(np.array([2, 1, 0]), [A, K, A])
def numbers_of(rng):
    return {"x": np.array(f(rng, N, 128, 4 * C)), "u": np.array(f(rng, N, 128, 512)), "v": np.array(f(rng, N, 128, 512))}
def layers(rng, still=[]):
    w = np.array(f(rng, N, 128, 2048)).reshape(N, 8, 16, 4, 8, 16, 4)
    for i in still:
        w[:, :, i] = 0
        w[:, :, :, :, :, i] = 0
    return w
def weights(rng, w):
    c, p = packed(np.ascontiguousarray(w).reshape(N, 128, 2048), rng)
    return {"wc": c, "ws": p}
def numbers_to(x, u, v):
    return {"x": x.astype(np.float32).reshape(N, 128, 4 * C).astype(BF), "u": u.reshape(N, 128, 512), "v": v}
def setup_inputs(rng):
    return {**numbers_of(rng), **weights(rng, layers(rng))}
def setup_inputs_ties(rng):
    d = numbers_of(rng)
    x = d["x"].astype(np.float32).reshape(N, 8, 16, C, 4)
    x[:, :, 0] = 0
    x[:, :, 0, :, 0] = np.exp2(rng.integers(0, 3, (N, 8, C)))
    u = d["u"].reshape(N, 128, 128, 4)
    u[:, :, ::16] = 0
    o = rng.permutation(N)
    g = rng.permutation(8)[:2]
    for r in range(N):
        for h in range(0, 128, 16): u[r, h, h, 0] = 0.0 if r == o[0] else -1.0 if r == o[1] else 1.0
        if r != o[0] and r ^ 1 != o[0]:
            for i in range(2):
                s = np.ones(C)
                s[A * (r % 2):A * (r % 2) + A] = 0
                s[C - 1 - i * (r % 2)] = 2
                x[r, g[i], 0, :, 0] = np.exp2(2 - s if r == o[1] else s)
    return {**numbers_to(x, u, d["v"]), **weights(rng, layers(rng, [0]))}
def setup_inputs_near(rng):
    d = numbers_of(rng)
    x = d["x"].astype(np.float32).reshape(N, 8, 16, C, 4)
    x[:, :, 0] = 0
    x[:, :, 8:] = 0
    u = d["u"].reshape(N, 128, 128, 4)
    u[:, :, ::16] = 0
    o = rng.permutation(N) % 4
    for r in range(N):
        s = rng.integers(0, 256, (8, C))
        if o[r] < 3:
            for t in range(8): x[r, :, 8 + t // 4, :, t % 4] = ((s >> t) & 1) * 2.0 ** (t - 23)
        if o[r] < 2:
            x[r, :, 0, :, 0] = rng.integers(0, 2, (8, C)) * 2.0 - 1.0
            x[r, :, 11, :, 0] = 2.0 ** -10
        if o[r] == 2:
            for g in range(8): x[r, g, 0, rng.permutation(C)[:2], 0] = np.array([2.0 ** 29, -2.0 ** 29])
        if o[r] == 3:
            x[r, :, 10, :, 0] = rng.integers(-7, 8, (8, C)) * 2.0 ** -30
            for g in rng.permutation(8)[:4]:
                a = rng.permutation(C) % 16
                x[r, g, 10, :, 0] = np.where(a < 8, a + 8, -a) * 2.0 ** -30
                x[r, g, 15, :, 0] = 1.96875 * 2.0 ** -14
        k = 1.0 if o[r] == 0 else 2.0 ** -30
        for h in range(0, 128, 16):
            if o[r] < 2:
                u[r, h, h, 0] = k
                u[r, h + 11, h, 0] = k
            if o[r] == 2: u[r, h, h, 0] = 1.0
            if o[r] < 3: u[r, h + 8:h + 10, h] = k
            else: u[r, h + 10, h, 0] = k
    return {**numbers_to(x, u, d["v"]), **weights(rng, layers(rng, [0, 8, 9, 10, 11, 12, 13, 14, 15]))}
def setup_inputs_huge(rng):
    d = numbers_of(rng)
    h, o = rng.permutation(8), rng.permutation(N)
    x = (0.75 + 0.25 * rng.random((N, 8, 1, C, 1))) * (0.9 + 0.1 * rng.random((N, 8, 16, C, 4))) * 2.0 ** 30
    c = rng.integers(0, 2, (N, 1, 1, C, 1))
    x[:, h[4:6]] *= 0.0625 + 0.9375 * c
    x[:, h[6:]] *= 1.0 - 0.9375 * c
    x[o[0]] = (0.95 + 0.05 * rng.random((8, 16, C, 4))) * 2.0 ** 30
    u = d["u"].reshape(N, 128, 128, 4)
    u[:, :, ::16] = 0
    for r in range(N):
        k = rng.permutation(8)
        for g in range(8):
            e = float(k[g] % 2 * 2 - 1)
            if r == o[0]: u[r, :, 16 * g] = 2.0 ** 30 * e
            else:
                for i in (h[:4] if k[g] < 4 else h[4:]):
                    t = -e if i in h[6:] else e
                    u[r, 16 * i:16 * i + 16, 16 * g] = (2.0 ** 30 * (1 - 0.1 * rng.random((16, 4))) * t).astype(np.float32).astype(BF)
    w = np.zeros((N, 128, 4, 128, 4), np.float32)
    i = np.arange(128)
    for b in range(4): w[:, i, b, i, b] = -4
    return {**numbers_to(x, u, d["v"]), **weights(rng, w.astype(BF))}
def setup_inputs_edges(rng):
    d = numbers_of(rng)
    s = (8, 16, C, 4)
    x = (2 * rng.integers(4, 8, (N,) + s) + 1) * 0.125 * (rng.integers(0, 2, (N,) + s) * 2.0 - 1.0) * np.exp2(rng.integers(-2, 2, (1, 8, 1, C, 1)))
    x[:, :, 0] = 0
    x[:, :, 0, :, 0] = 1.96875 * 2.0 ** 12
    x[:, :, 8:] = 0
    for t in range(9): x[:, :, 8 + t // 4, :, t % 4] = (np.arange(C) >> t) & 1
    u = d["u"].reshape(N, 128, 128, 4)
    u[:, :, ::16] = 0
    w = layers(rng, [0, 8, 9, 10, 11, 12, 13, 14, 15])
    k, e = rng.permutation(8) % N, rng.integers(0, 2, 8)
    for r in range(N):
        for t in range(2):
            c = ((r >> t) & 1) * 2.0 - 1.0
            x[r, :, 11, :, t] = c
            for g in range(8): w[r, g, 11, 0, g, 0, t] = -4096.0 * c
        for g in range(8):
            if (bin(r & int(k[g])).count("1") + int(e[g])) % 2 == 1:
                for t in range(9): u[r, 16 * g + 8 + t // 4, 16 * g, t % 4] = 2.0 ** t
    return {**numbers_to(x, u, d["v"]), **weights(rng, w)}
def setup_inputs_spread(rng):
    d = setup_inputs(rng)
    d["x"] = wide(rng, N, 128, 4 * C, cols=6)
    return d
def check_inputs(d):
    b = []
    for k in ("x", "u", "v"):
        a = np.abs(d[k].astype(np.float32))
        if not (np.isfinite(a).all() and ((a == 0) | (a >= 2.0 ** -30) & (a <= 2.0 ** 30)).all()): b.append("a value of " + k)
    none, least, most = [emit(mx_ref.quantize(np.full((128, 16), k, np.float32).astype(BF)))[1][0, 0] for k in (0.0, 2.0 ** -30, 2.0 ** 30)]
    for r in range(N):
        if ((d["wc"][r] == 0x7F) | (d["wc"][r] == 0xFF)).any(): b.append("wc: a code that is no number")
        s = mx_ref.live(d["ws"][r])
        if ((s != none) & ((s < least) | (s > most))).any(): b.append("ws: a scale out of range")
        if ((s == none)[:, None, :, None] & ((d["wc"][r].reshape(16, 8, -1, 4) & 0x7F) != 0)).any(): b.append("wc: a code that isn't zero beside the scale of zeros")
    return b
def reference(x, u, v, wc, ws):
    qu = [mx_ref.quantize(u[r]) for r in range(N)]
    lay = [pk(wc[r], ws[r]) for r in range(N)]
    now = [x[r] for r in range(N)]
    last = np.zeros((N, 8, C), np.int64)
    for h in STEP:
        own, times_of = [], np.zeros((N, 8, C), np.int64)
        for r in range(N):
            q = mx_ref.quantize(now[r])
            own.append(decode(q).astype(BF))
            s = mx_ref.matmul(qu[r], q)[::16] + np.float32(0.0)
            np.put_along_axis(times_of[r], np.argsort(-s, axis=1, kind="stable"), np.stack([MANY] * 8), axis=1)
        first = np.full((N, 8, C), K)
        part, packs = [], []
        for r in range(N):
            both = np.minimum(times_of[r], times_of[r ^ h])
            e = np.zeros((8, K), np.int64)
            for g in range(8):
                e[g] = np.flatnonzero(both[g])[:K]
                shared = np.repeat(np.arange(C), both[g])
                last[r, g] = np.concatenate([shared, np.repeat(np.arange(C), times_of[r, g] - both[g])])
                first[r, g, np.searchsorted(shared, e[g])] = np.arange(K)
            part.append(gcols(own[r], e))
            packs.append(mx_ref.quantize(part[r]))
        for r in range(N):
            z = mx_ref.quantize((part[r].astype(np.float32) - decode(packs[r ^ h])).astype(BF))
            a = gcols(own[r], last[r]).astype(np.float32)
            made = []
            for b in range(4):
                p = mx_ref.matmul(pick(lay[r], np.arange(128 * b, 128 * b + 128)), z) * np.float32(0.015625)
                made.append(a[:, b::4] + gpick(np.concatenate([p, np.zeros((128, 1), np.float32)], axis=1), first[r]))
            now[r] = tile(made)
    y, nl = np.zeros((N, 128, C), np.float32), np.zeros((N, 8, C), np.float32)
    oc, osc = np.zeros((N, 128, 4 * C), np.uint8), np.zeros((N, 16, C), np.uint8)
    for r in range(N):
        q = mx_ref.quantize(now[r])
        y[r] = mx_ref.matmul(mx_ref.quantize(v[r]), q)
        nl[r] = last[r]
        oc[r], osc[r] = emit(q)
    return {"y": y, "nl": nl, "oc": oc, "osc": osc}

@@ -1,0 +1,459 @@
+from concourse.bass import DstId, RemoteDMATransfer
+from concourse.mybir import dt, AluOpType, AxisListType, ActivationFunctionType
+
+A = AluOpType
+AF = ActivationFunctionType
+C = 256
+STEPS = [1, 2, 4]
+M0 = 12582912.0
+BIG = 1.0e29
+FAR = 8192.0
+CODE = "float8_e4m3fn_x4"
+MW = [256, 192, 128, 128]
+MO = [0, 256, 448, 576]
+BOTH = (15, 14)
+
+
+def sb(n, d):
+    return ("sbuf", [128, n], d)
+
+
+SCRATCH = {
+    "xin": sb(1024, "bfloat16"), "ut": sb(512, "bfloat16"), "vt": sb(512, "bfloat16"),
+    "xt": sb(1024, "bfloat16"),
+    "wq": sb(512, CODE), "wsc": sb(512, "uint8"),
+    "uq": sb(128, CODE), "us": sb(128, "uint8"), "uq2": sb(128, CODE), "us2": sb(128, "uint8"),
+    "vq": sb(128, CODE), "vs": sb(128, "uint8"),
+    "eq": sb(512, CODE), "es": sb(512, "uint8"), "oq": sb(128, CODE), "osb": sb(128, "uint8"),
+    "mq": sb(704, CODE), "ms": sb(704, "uint8"), "mt": sb(4 * 704, "bfloat16"),
+    "fq": sb(128, CODE), "fs": sb(128, "uint8"), "zq": sb(128, CODE), "zs": sb(128, "uint8"),
+    "ft": sb(512, "bfloat16"), "zt": sb(512, "bfloat16"), "fp": sb(512, "bfloat16"), "f64": sb(512, "bfloat16"),
+    "win": sb(4 * 384, "bfloat16"), "tp": sb(1024, "bfloat16"),
+    "et": sb(528, "bfloat16"), "ot": sb(512, "bfloat16"),
+    "pi": sb(4, "int32"), "pf": sb(8, "float32"),
+    "yy": sb(256, "bfloat16"), "g16": sb(128, "bfloat16"), "src": sb(512, "bfloat16"),
+    "bigm": sb(256, "float32"), "kres": sb(256, "float32"), "diag": sb(256, "bfloat16"),
+    "keep": sb(256, "bfloat16"), "hold": sb(256, "bfloat16"), "m32": sb(64, "float32"),
+    "k0": sb(32, "float32"), "cidx": sb(52, "float32"), "uoff": sb(8, "uint16"),
+    "m1": sb(256, "float32"), "tq": sb(256, "float32"), "sg": sb(512, "bfloat16"), "junk": sb(2048, "bfloat16"),
+    "r1": sb(16, "float32"), "dsc": sb(256, "bfloat16"), "cm": sb(256, "bfloat16"), "csc": sb(256, "bfloat16"),
+    "u1": sb(32, "float32"), "u2": sb(32, "float32"), "i32": sb(32, "float32"), "o32": sb(32, "float32"),
+    "rk": sb(16, "float32"), "gm": sb(48, "float32"), "gl": sb(48, "float32"),
+    "own": sb(160, "float32"), "w": sb(512, "float32"),
+    "offe": sb(16, "uint16"), "le": sb(768, "bfloat16"), "lek": sb(128, "bfloat16"), "el": sb(8, "uint16"),
+    "offn": sb(32, "uint16"), "ln": sb(1536, "bfloat16"), "isa": sb(256, "bfloat16"), "ks": sb(256, "bfloat16"),
+    "kw": sb(256, "bfloat16"), "lm": sb(256, "bfloat16"), "lw": sb(256, "bfloat16"), "nlist": sb(16, "uint16"),
+    "nlo": sb(256, "float32"), "yo": sb(256, "float32"),
+    "ps": ("psum", [128, 4096], "float32"),
+}
+for _k in range(4):
+    SCRATCH["xq%d" % _k] = sb(256, CODE)
+    SCRATCH["xs%d" % _k] = sb(256, "uint8")
+for _k in range(3):
+    SCRATCH["pq%d" % _k] = sb(256, CODE)
+    SCRATCH["pz%d" % _k] = sb(256, "uint8")
+
+POOL = {"v": 60, "a": 30, "p": 20, "g": 6}
+NDMA = 16
+SEMAPHORES = (["%s%d" % (q, k) for q in POOL for k in range(POOL[q])] + ["d%d" % k for k in range(NDMA)]
+              + ["aq0", "aq1", "aq2", "af0", "af1", "af2", "gone"])
+
+
+def emit(g, T, ops):
+    queue = {"v": g.vector, "a": g.scalar, "p": g.tensor, "g": g, "s": g.sync}
+    writer, readers = {}, {}
+    deps = []
+    for n, (q, fn, rd, wr, ext, dma) in enumerate(ops):
+        d = set()
+        for t in rd:
+            if t in writer:
+                d.add(writer[t])
+            if t[0] == "P":
+                d.update(k for k in readers.get(t, []) if ops[k][0] != q)
+        for t in wr:
+            if t in writer and not (q == "p" and ops[writer[t]][0] == "p"):
+                d.add(writer[t])
+            d.update(readers.get(t, []))
+        d.discard(n)
+        deps.append(d)
+        for t in rd:
+            readers.setdefault(t, []).append(n)
+        for t in wr:
+            writer[t] = n
+            readers[t] = []
+    known = {q: 0 for q in queue}
+    issued = {q: 0 for q in queue}
+    closure, waits, needed = [], [], set()
+    for n, op in enumerate(ops):
+        q = op[0]
+        mine = []
+        for k in sorted(deps[n], reverse=True):
+            if not known[q] >> k & 1:
+                mine.append(k)
+                known[q] |= closure[k]
+                needed.add(k)
+        waits.append(mine)
+        if op[5] or q == "g":
+            closure.append(known[q] | 1 << n)
+        else:
+            issued[q] |= 1 << n
+            closure.append(known[q] | issued[q])
+    count = {q: 0 for q in POOL}
+    mark, ndma, open_dma = {}, 0, []
+    for n, (q, fn, rd, wr, ext, dma) in enumerate(ops):
+        for k in waits[n]:
+            queue[q].wait_ge(*mark[k])
+        for s, val in ext:
+            queue[q].wait_ge(T.sem[s], val)
+        ins = fn()
+        if dma:
+            mark[n] = (T.sem["d%d" % ndma], 16)
+            ndma += 1
+            ins.then_inc(*mark[n])
+            if n not in needed:
+                open_dma.append((q, mark[n]))
+        elif n in needed:
+            k = count[q]
+            count[q] += 1
+            sem = T.sem["%s%d" % (q, k % POOL[q])]
+            mark[n] = (sem, k // POOL[q] + 1)
+            ins.then_inc(sem, 1)
+    for q, m in open_dma:
+        queue[q].wait_ge(*m)
+
+
+def rank_program(g, core, T, topo):
+    rank = T.rank_of(core)
+    if rank is None:
+        return
+    V, S, PE = g.vector, g.scalar, g.tensor
+    ops = []
+
+    def op(q, fn, rd, wr, ext=(), dma=False):
+        ops.append((q, fn, list(rd), list(wr), list(ext), dma))
+
+    def ts(out, in0, s1, s2, o0, o1, rd, wr, ext=()):
+        if o1 is None:
+            op("v", lambda: V.tensor_scalar(out, in0, s1, None, o0), rd, wr, ext)
+        else:
+            op("v", lambda: V.tensor_scalar(out, in0, s1, s2, o0, o1), rd, wr, ext)
+
+    def tt(out, a, b, o, rd, wr, ext=()):
+        op("v", lambda: V.tensor_tensor(out, a, b, o), rd, wr, ext)
+
+    def cp(out, a, rd, wr):
+        op("v", lambda: V.tensor_copy(out, a), rd, wr)
+
+    def scan(out, d0, d1, o0, o1, rd, wr, first=0.0):
+        op("v", lambda: V.tensor_tensor_scan(out, d0, d1, first, o0, o1), rd, wr)
+
+    def tr(out, a, rd, wr):
+        op("v", lambda: V.transpose(out, a), rd, wr)
+
+    def red(out, a, rd, wr):
+        op("v", lambda: V.tensor_reduce(out, a, AxisListType.X, A.add), rd, wr)
+
+    def fill(ap, val, wr):
+        op("v", lambda: V.memset(ap, val), [], wr)
+
+    def quant(qo, so, a, rd, wr):
+        op("v", lambda: V.quantize_mx(qo, so, a), rd, wr)
+
+    def act(out, a, fn, rd, wr, **kw):
+        op("a", lambda: S.activation(out, a, fn, **kw), rd, wr)
+
+    def mm(bank, n, lq, ls, rq, rs, rd, start=True, stop=True, ext=()):
+        op("p", lambda: PE.matmul_mx(T.ps[:, 512 * bank:512 * bank + n], lq, ls, rq, rs, start, stop),
+           rd, ["P%d" % bank], ext)
+
+    def bank(k, a, b):
+        return T.ps[:, 512 * k + a:512 * k + b]
+
+    def dma(q, out, a, rd, wr):
+        eng = {"s": g.sync, "a": g.scalar, "g": g}[q]
+        op(q, lambda: eng.dma_start(out, a), rd, wr, (), True)
+
+    def iota(out, pat, base, mult, wr, small=True):
+        if small:
+            op("g", lambda: g.iota(out, pat, base, mult, allow_small_or_imprecise_dtypes=True), [], wr)
+        else:
+            op("g", lambda: g.iota(out, pat, base, mult), [], wr)
+
+    def slot(c, n):
+        k, t = (0, 0) if c == 0 else divmod(16 - c, 4)
+        return T.mt[:, 4 * MO[k] + t:4 * (MO[k] + n):4]
+
+    def blocks(k):
+        return ["m%d" % c for c in range(16) if (c == 0 and k == 0) or (c > 0 and (16 - c) // 4 == k)]
+
+    def maskof(es):
+        return sum(1 << e for e in es)
+
+    def weave(first, second):
+        for k in range(max(len(first), len(second))):
+            ops.extend(first[k:k + 1])
+            ops.extend(second[k:k + 1])
+
+    def taken(start):
+        got = ops[start:]
+        del ops[start:]
+        return got
+
+    gone = [0]
+
+    dma("s", T.xin[:], T.x[:], [], ["x0"])
+    dma("a", T.ut[:], T.u[:], [], ["ut"])
+    dma("s", T.wq[:].bitcast(dt.uint8), T.wc[:], ["x0"], ["wq"])
+    dma("s", T.wsc[:], T.ws[:], [], ["wsc"])
+    dma("s", T.vt[:], T.v[:], [], ["vt"])
+
+    iota(T.pi[:, 0:1], [[0, 1]], 0, 1, ["pi0"], False)
+    iota(T.yy[:], [[0, 16], [1, 16]], 0, 0, ["yy"])
+    iota(T.g16[:], [[16, 8], [0, 16]], 0, 0, ["g16"])
+    iota(T.src[:, 256:512], [[1, 16], [16, 16]], 0, 0, ["srcb"])
+    for k, (a, b) in enumerate([(208, 256), (144, 192), (80, 128), (16, 128)]):
+        fill(T.mt[:, 4 * (MO[k] + a):4 * (MO[k] + b)], 0.0, blocks(k))
+    fill(T.et[:], 0.0, ["et"])
+    fill(T.r1[:, 0:1], 0.0, ["r0"])
+    for k, bits in enumerate([15, 112, 16]):
+        ts(T.pi[:, 1 + k:2 + k], T.pi[:, 0:1], bits, None, A.bitwise_and, None, ["pi0"], ["pi%d" % (k + 1)])
+    cp(T.pf[:, 0:3], T.pi[:, 1:4], ["pi1", "pi2", "pi3"], ["pf"])
+    rr, gp, par = T.pf[:, 0:1], T.pf[:, 1:2], T.pf[:, 2:3]
+    ts(T.pf[:, 3:4], par, 65536.0, rr, A.mult, A.subtract, ["pf"], ["pf3"])
+    ts(T.pf[:, 4:5], par, -65536.0, rr, A.mult, A.subtract, ["pf"], ["pf4"])
+    ts(T.pf[:, 3:4], T.pf[:, 3:4], 15.5, None, A.add, None, ["pf3"], ["pf3"])
+    ts(T.pf[:, 4:5], T.pf[:, 4:5], 15.5 + 16 * 65536.0, None, A.add, None, ["pf4"], ["pf4"])
+    ts(T.uoff[:], T.yy[:, 0:8], 16.0, None, A.mult, None, ["yy"], ["uoff"])
+    ts(T.bigm[:], T.yy[:], rr, BIG, A.not_equal, A.mult, ["yy", "pf"], ["bigm"])
+    ts(T.kres[:], T.yy[:], 0.0, 5 * BIG, A.is_equal, A.mult, ["yy"], ["kres"])
+    ts(T.diag[:], T.yy[:], rr, None, A.is_equal, None, ["yy", "pf"], ["diag"])
+    ts(T.keep[:], T.yy[:], 0.0, None, A.not_equal, None, ["yy"], ["keep"])
+    ts(T.k0[:, 0:16], T.yy[:, 0:16], 16.0, T.pf[:, 3:4], A.mult, A.add, ["yy", "pf3"], ["k0a"])
+    ts(T.k0[:, 16:32], T.yy[:, 0:16], 16.0, T.pf[:, 4:5], A.mult, A.add, ["yy", "pf4"], ["k0b"])
+    for t in range(4):
+        ts(T.ot[:, t:512:4], T.g16[:], gp, None, A.is_equal, None, ["g16", "pf"], ["ot%d" % t])
+    quant(T.uq[:], T.us[:], T.ut[:], ["ut"], ["uq"])
+    tt(T.et[:, 3:515:4], T.ot[:, 0:512:4], T.diag[:, 0:128], A.mult, ["ot0", "diag"], ["et"])
+    op("v", lambda: V.tensor_copy(T.uq2[:].bitcast(dt.uint32), T.uq[:].bitcast(dt.uint32).indirect(T.uoff[:])),
+       ["uq", "uoff"], ["uq2"])
+    act(T.us2[:], T.us[:].indirect(T.uoff[:]), AF.Copy, ["uq", "uoff"], ["us2"])
+    quant(T.oq[:], T.osb[:], T.ot[:], ["ot0", "ot1", "ot2", "ot3"], ["oq"])
+    for b in range(4):
+        quant(T.eq[:, 128 * b:128 * b + 128], T.es[:, 128 * b:128 * b + 128], T.et[:, 3 - b:515 - b], ["et"], ["eq%d" % b])
+
+    def later_constants():
+        ts(T.hold[:], T.yy[:], rr, 65536.0, A.is_le, A.mult, ["yy", "pf"], ["hold"])
+        ts(T.m32[:, 32:64], T.g16[:, 0:32], par, None, A.is_equal, None, ["g16", "pf"], ["same"])
+        ts(T.m32[:, 0:32], T.yy[:, 0:32], rr, None, A.is_gt, None, ["yy", "pf"], ["lt"])
+        ts(T.pf[:, 5:6], rr, 16.0, None, A.mult, None, ["pf"], ["pf5"])
+        tt(T.m32[:, 0:32], T.m32[:, 0:32], T.m32[:, 32:64], A.mult, ["lt", "same"], ["lt"])
+        ts(T.cidx[:, 0:16], T.yy[:, 0:16], T.pf[:, 5:6], 256.0, A.add, A.add, ["yy", "pf5"], ["cidx"])
+        fill(T.cidx[:, 32:52], -M0, ["negm"])
+        fill(T.w[:, 0:1], M0, ["w0"])
+        ts(T.cidx[:, 16:32], T.cidx[:, 0:16], 2.0, 256.0, A.mult, A.add, ["cidx"], ["cidx2"])
+        ts(T.src[:, 0:256], T.src[:, 256:512], -256.0, None, A.add, None, ["srcb"], ["srca"])
+
+    quant(T.xq0[:], T.xs0[:], T.xin[:], ["x0"], ["xq0"])
+
+    for rnd, h in enumerate(STEPS):
+        mate = T.cores[rank ^ h]
+        rid, pid, _ = topo.addr(mate)
+        eng = topo.engines(core, mate)
+        xq, xs, pq, pz = T["xq%d" % rnd], T["xs%d" % rnd], T["pq%d" % rnd], T["pz%d" % rnd]
+        X = "xq%d" % rnd
+
+        quarter, eighth = len(eng) // 4, len(eng) // 8
+        cuts = [0, quarter, 2 * quarter, 3 * quarter, 3 * quarter + eighth, 4 * quarter]
+        trs = []
+        for k in range(5):
+            if k < 4:
+                s_, d_ = xq[:, 64 * k:64 * k + 64].bitcast(dt.uint8), pq[:, 64 * k:64 * k + 64].bitcast(dt.uint8)
+            else:
+                s_, d_ = xs[:], pz[:]
+            trs.append(RemoteDMATransfer(dst_ids=[DstId(rid=rid, pnc=pid)], dma_engine_mask=maskof(eng[cuts[k]:cuts[k + 1]]),
+                                         remote_sem=T.sem["aq%d" % rnd], src=s_, dst=d_))
+        nq = cuts[5]
+        op("g", lambda trs=trs: g.remote_dma_fused(trs, local_sem=T.sem.gone), [X], [])
+        gone[0] += nq
+
+        mm(0, C, T.uq2[:], T.us2[:], xq[:], xs[:], ["uq2", "us2", X])
+        mm(1, C, T.uq2[:], T.us2[:], xq[:], xs[:], ["uq2", "us2", X])
+        for b in range(4):
+            mm(3 + b, C, T.eq[:, 128 * b:128 * b + 128], T.es[:, 128 * b:128 * b + 128], xq[:], xs[:], ["eq%d" % b, X])
+        tt(T.m1[:], bank(0, 0, C), T.bigm[:], A.add, ["P0", "bigm"], ["m1"])
+        scan(T.tq[:], T.kres[:], T.m1[:], A.add, A.min, ["kres", "m1"], ["tq"])
+        for k, c in enumerate(BOTH):
+            sg = T.sg[:, 256 * k:256 * k + 16 * c]
+            act(sg, bank(1, 0, 16 * c), AF.Sign, ["P1", "tq"], ["sg%d" % k], bias=T.tq[:, 16 * c + 15:16 * c + 16], scale=-1.0)
+        for k, c in enumerate(BOTH):
+            sg = T.sg[:, 256 * k:256 * k + 16 * c]
+            act(slot(c, 16 * c), sg, AF.Sign, ["sg%d" % k], ["m%d" % c, "r%d" % c], bias=1.0, scale=-1.0, accum_out=T.r1[:, c:c + 1])
+
+        def compare(c):
+            ts(slot(c, 16 * c), bank(0, 0, 16 * c), T.tq[:, 16 * c + 15:16 * c + 16], None, A.is_ge, None, ["P0", "tq"], ["m%d" % c])
+
+        def rowsum(c):
+            act(T.junk[:, 8 * c * (c - 1):8 * c * (c + 1)], slot(c, 16 * c), AF.Copy, ["m%d" % c], ["r%d" % c], accum_out=T.r1[:, c:c + 1])
+
+        def colsum(k):
+            a, b = MO[k], MO[k] + MW[k]
+            quant(T.mq[:, a:b], T.ms[:, a:b], T.mt[:, 4 * a:4 * b], blocks(k), ["mq%d" % k])
+            mm(2, MW[k], T.oq[:], T.osb[:], T.mq[:, a:b], T.ms[:, a:b], ["oq", "mq%d" % k], k == 0, k == 3)
+
+        tt(slot(0, C), bank(0, 0, C), T.tq[:], A.is_gt, ["P0", "tq"], ["m0"])
+        for c in range(13, 8, -1):
+            compare(c)
+        scan(T.dsc[:], T.keep[:], slot(0, C), A.mult, A.add, ["keep", "m0"], ["dsc"])
+        colsum(0)
+        colsum(1)
+        for c in range(8, 0, -1):
+            compare(c)
+        colsum(2)
+        colsum(3)
+        for c in range(13, 0, -1):
+            rowsum(c)
+        for k in range(2):
+            tt(T.u1[:, 16 * k:16 * k + 16], T.k0[:, 16 * k:16 * k + 16], T.dsc[:, 15:256:16], A.subtract,
+               ["k0a", "k0b", "dsc"], ["u1%d" % k])
+        tt(T.cm[:], bank(2, 0, C), T.diag[:], A.mult, ["P2", "diag"], ["cm"])
+        for k in range(2):
+            tt(T.u2[:, 16 * k:16 * k + 16], T.u1[:, 16 * k:16 * k + 16], T.r1[:], A.subtract,
+               ["u1%d" % k] + ["r%d" % c for c in range(16)], ["u2%d" % k])
+        scan(T.csc[:], T.keep[:], T.cm[:], A.mult, A.add, ["keep", "cm"], ["csc"])
+        for k in range(2):
+            tt(T.i32[:, 16 * k:16 * k + 16], T.u2[:, 16 * k:16 * k + 16], T.csc[:, 15:256:16], A.add,
+               ["u2%d" % k, "csc"], ["i32%d" % k])
+        tr(T.o32[:], T.i32[:], ["i320", "i321"], ["o32"])
+        tt(T.rk[:], T.o32[:, 0:16], T.o32[:, 16:32], A.min, ["o32"], ["rk"])
+        gm, gl = T.gm[:, 16 * rnd:16 * rnd + 16], T.gl[:, 16 * rnd:16 * rnd + 16]
+        G = "gm%d" % rnd
+        ts(gm, T.rk[:], 1.0 / 128, M0, A.mult, A.add, ["rk"], [G])
+        op("g", lambda gm=gm, gl=gl, rnd=rnd, pid=pid, rid=rid, m=maskof(eng):
+           g.remote_dma(gl, gm, T.sem["af%d" % rnd], T.sem.gone, pid, rid, m), [G], [])
+        gone[0] += len(eng)
+
+        tb = [7, 1, 0, 2]
+        for b in range(4):
+            mm(tb[b], C, T.eq[:, 128 * b:128 * b + 128], T.es[:, 128 * b:128 * b + 128], pq[:], pz[:], ["eq%d" % b],
+               ext=[("aq%d" % rnd, nq)] if b == 0 else [])
+        for b in range(4):
+            act(T.win[:, 384 * b:384 * b + C], bank(3 + b, 0, C), AF.Copy, ["P%d" % (3 + b)], ["wt%d" % b], scale=64.0)
+        if rnd == 0:
+            later_constants()
+        o = T.own
+        pa, pb, of = o[:, 16:32], o[:, 32:48], o[:, 128:129]
+        scan(o[:, 0:16], gm, T.cidx[:, 32:48], A.add, A.add, [G, "negm"], ["cfl"])
+        ts(pa, gm, M0, None, A.is_le, None, [G], ["pa"])
+        ts(pb, gm, M0 + 2, None, A.is_lt, None, [G], ["pb"])
+        ts(o[:, 64:96], T.m32[:, 0:32], o[:, 15:16], None, A.mult, None, ["lt", "cfl"], ["fx"])
+        tt(pa, pa, T.cidx[:, 0:16], A.mult, ["pa", "cidx"], ["pa"])
+        tr(o[:, 96:128], o[:, 64:96], ["fx"], ["fxt"])
+        tt(pb, pb, T.cidx[:, 16:32], A.mult, ["pb", "cidx2"], ["pb"])
+        red(of, o[:, 96:128], ["fxt"], ["of"])
+        tt(pa, pa, gm, A.subtract, ["pa", G], ["pa"])
+        ts(pb, pb, of, None, A.add, None, ["pb", "of"], ["pb"])
+        ts(pa, pa, of, M0, A.add, A.add, ["pa", "of"], ["pa"])
+        for b in range(2):
+            cp(T.tp[:, C * b:C * b + C], bank(tb[b], 0, C), ["P%d" % tb[b]], ["tp%d" % b])
+        for b in range(2, 4):
+            act(T.tp[:, C * b:C * b + C], bank(tb[b], 0, C), AF.Copy, ["P%d" % tb[b]], ["tp%d" % b])
+        if rnd == 1:
+            quant(T.vq[:], T.vs[:], T.vt[:], ["vt"], ["vq"])
+
+        w = T.w
+        mm_, hh, nh, cs, pen = w[:, 1:17], w[:, 20:36], w[:, 36:52], w[:, 52:68], w[:, 68:84]
+        oh, om, mt_, sc = w[:, 84:85], w[:, 85:86], w[:, 86:87], w[:, 87:88]
+        tt(mm_, gm, gl, A.min, [G], ["mm"], ext=[("af%d" % rnd, len(eng))])
+        ts(hh, mm_, M0, None, A.is_gt, None, ["mm"], ["hh"])
+        ts(nh, mm_, M0, FAR, A.is_le, A.mult, ["mm"], ["nh"])
+        scan(cs, hh, hh, A.add, A.max, ["hh"], ["cs"])
+        tt(pen, nh, T.cidx[:, 0:16], A.min, ["nh", "cidx"], ["pen"])
+        ts(w[:, 96:128], T.m32[:, 0:32], w[:, 67:68], None, A.mult, None, ["lt", "cs"], ["hx"])
+        tt(pen, pen, cs, A.add, ["pen", "cs"], ["pen"])
+        at = len(ops)
+        tr(w[:, 128:160], w[:, 96:128], ["hx"], ["hxt"])
+        red(oh, w[:, 128:160], ["hxt"], ["oh"])
+        ts(T.offe[:], pen, oh, -1.0, A.add, A.add, ["pen", "oh"], ["offe"])
+        cp(T.le[:].indirect(T.offe[:]), T.src[:, 256:512], ["offe", "srcb"], ["le"])
+        scan(T.lek[:], T.hold[:, 0:128], T.le[:, 0:128], A.add, A.min, ["hold", "le"], ["lek"])
+        cp(T.el[:], T.lek[:, 15:128:16], ["lek"], ["el"])
+        list_e = taken(at)
+
+        cmx, cml, crl, sb_ = w[:, 160:176], w[:, 161:177], w[:, 180:196], w[:, 196:212]
+        scan(w[:, 160:177], w[:, 0:17], T.cidx[:, 32:49], A.add, A.add, ["mm", "w0", "negm"], ["cml"])
+        ts(w[:, 256:320], T.m32[:], w[:, 176:177], None, A.mult, None, ["lt", "same", "cml"], ["mx"])
+        tr(w[:, 320:384], w[:, 256:320], ["mx"], ["mxt"])
+        red(om, w[:, 320:352], ["mxt"], ["om"])
+        red(mt_, w[:, 352:384], ["mxt"], ["mtot"])
+        ts(sb_, mm_, M0 + 2, FAR, A.is_lt, A.mult, ["mm"], ["sb"])
+        weave(list_e, taken(at))
+        ts(sc, om, -2.0, mt_, A.mult, A.add, ["om", "mtot"], ["sc"])
+        tt(w[:, 224:240], cmx, nh, A.add, ["cml", "nh"], ["x1a"])
+        scan(crl, gm, mm_, A.add, A.subtract, [G, "mm", "sc"], ["crl"], sc)
+        tt(w[:, 240:256], cml, sb_, A.add, ["cml", "sb"], ["x1b"])
+        tt(w[:, 384:400], crl, pa, A.add, ["crl", "pa"], ["x2a"])
+        tt(w[:, 400:416], crl, pb, A.add, ["crl", "pb"], ["x2b"])
+        tt(w[:, 224:256], w[:, 224:256], w[:, 384:416], A.min, ["x1a", "x1b", "x2a", "x2b"], ["x1a", "x1b"])
+        ts(T.offn[:, 0:16], w[:, 224:240], om, None, A.add, None, ["x1a", "om"], ["offa"])
+        ts(T.offn[:, 16:32], w[:, 240:256], om, -1.0, A.add, A.add, ["x1b", "om"], ["offb"])
+
+        for b in range(4):
+            act(T.ft[:, b:512:4], T.tp[:, C * b:C * b + C].indirect(T.el[:]), AF.Copy, ["tp%d" % b, "el"], ["ft%d" % b])
+        for b in range(4):
+            act(T.fp[:, 128 * b:128 * b + 128], T.win[:, 384 * b:384 * b + C].indirect(T.el[:]), AF.Copy,
+                ["wt%d" % b, "el"], ["fp%d" % b], scale=1.0 / 64)
+        act(T.f64[:], T.fp[:], AF.Copy, ["fp0", "fp1", "fp2", "fp3"], ["f64"], scale=64.0)
+        quant(T.fq[:], T.fs[:], T.ft[:], ["ft0", "ft1", "ft2", "ft3"], ["fq"])
+        for b in range(4):
+            mm(3 + b, 128, T.eq[:, 128 * b:128 * b + 128], T.es[:, 128 * b:128 * b + 128], T.fq[:], T.fs[:], ["eq%d" % b, "fq"])
+        cp(T.ln[:].indirect(T.offn[:]), T.src[:], ["offa", "offb", "srca", "srcb"], ["ln"])
+
+        for b in range(4):
+            tt(T.zt[:, b:512:4], T.fp[:, 128 * b:128 * b + 128], bank(3 + b, 0, 128), A.subtract,
+               ["fp%d" % b, "P%d" % (3 + b)], ["zt%d" % b])
+        ts(T.isa[:], T.ln[:, 0:C], 0.0, None, A.is_lt, None, ["ln"], ["isa"])
+        quant(T.zq[:], T.zs[:], T.zt[:], ["zt0", "zt1", "zt2", "zt3"], ["zq"])
+        for b in range(4):
+            mm(tb[b], 128, T.wq[:, 128 * b:128 * b + 128], T.wsc[:, 128 * b:128 * b + 128], T.zq[:], T.zs[:], ["wq", "wsc", "zq"])
+
+        def made(k):
+            tt(T.win[:, 384 * k + C:384 * k + 384], bank(tb[k], 0, 128), T.f64[:, 128 * k:128 * k + 128], A.add,
+               ["P%d" % tb[k], "f64"], ["wg%d" % k])
+
+        scan(T.ks[:], T.isa[:], T.src[:, 0:C], A.add, A.max, ["isa", "srca"], ["ks"], -1.0)
+        tt(T.lm[:], T.ln[:, 0:C], T.diag[:], A.mult, ["ln", "diag"], ["lm"])
+        scan(T.kw[:], T.hold[:], T.ks[:], A.add, A.min, ["hold", "ks"], ["kw"])
+        scan(T.lw[:], T.keep[:], T.lm[:], A.mult, A.add, ["keep", "lm"], ["lw"])
+        lw, kw = T.lw[:, 15:256:16], T.kw[:, 15:256:16]
+        q2, nm, z2 = w[:, 432:448], w[:, 448:464], w[:, 464:480]
+        made(0)
+        ts(q2, lw, 0.0, 256.0, A.is_ge, A.mult, ["lw"], ["q2"])
+        made(1)
+        tt(z2, kw, q2, A.add, ["kw", "q2"], ["z2"])
+        tt(nm, lw, q2, A.subtract, ["lw", "q2"], ["nm"])
+        ts(z2, z2, 127.0, -1024.0, A.is_gt, A.mult, ["z2"], ["z2"])
+        tt(z2, z2, kw, A.add, ["z2", "kw"], ["z2"])
+        tt(z2, z2, nm, A.max, ["z2", "nm"], ["z2"])
+        ts(T.nlist[:], z2, 256.0, None, A.add, None, ["z2"], ["nlist"])
+        made(2)
+        made(3)
+
+        for b in (0, 1):
+            act(T.xt[:, b:1024:4], T.win[:, 384 * b:384 * b + 384].indirect(T.nlist[:]), AF.Copy,
+                ["wt%d" % b, "wg%d" % b, "nlist"], ["xt%d" % b], scale=1.0 / 64)
+        for b in (2, 3):
+            ts(T.xt[:, b:1024:4], T.win[:, 384 * b:384 * b + 384].indirect(T.nlist[:]), 1.0 / 64, None, A.mult, None,
+               ["wt%d" % b, "wg%d" % b, "nlist"], ["xt%d" % b])
+        quant(T["xq%d" % (rnd + 1)][:], T["xs%d" % (rnd + 1)][:], T.xt[:], ["xt0", "xt1", "xt2", "xt3"], ["xq%d" % (rnd + 1)])
+
+    mm(3, C, T.vq[:], T.vs[:], T.xq3[:], T.xs3[:], ["vq", "xq3"])
+    dma("s", T.oc[:], T.xq3[:].bitcast(dt.uint8), ["xq3"], [])
+    ts(T.isa[:], T.isa[:], 256.0, None, A.mult, None, ["isa"], ["isa"])
+    tt(T.nlo[:], T.ln[:, 0:C], T.isa[:], A.add, ["ln", "isa"], ["nlo"])
+    act(T.yo[:], bank(3, 0, C), AF.Copy, ["P3"], ["yo"])
+    dma("a", T.y[:], T.yo[:], ["yo"], [])
+    for k in range(4):
+        dma("s" if k < 3 else "a", T.osc[4 * k:4 * k + 4, :], T.xs3[32 * k:32 * k + 4, :], ["xq3"], [])
+    dma("s", T.nl[:], T.nlo[0:128:16, :], ["nlo"], [])
+    emit(g, T, ops)
+    g.wait_ge(T.sem.gone, gone[0])

@@ -4,14 +4,16 @@ from concourse.mybir import dt, AluOpType, AxisListType, ActivationFunctionType
 A = AluOpType
 AF = ActivationFunctionType
 C = 256
+SH = 192
+WN = C + 2 * SH
 STEPS = [1, 2, 4]
 M0 = 12582912.0
-BIG = 1.0e29
+BIG = 2.0 ** 88
 FAR = 8192.0
 CODE = "float8_e4m3fn_x4"
 MW = [256, 192, 128, 128]
 MO = [0, 256, 448, 576]
-BOTH = (15, 14)
+BOTH = (15, 14, 13)
 
 
 def sb(n, d):
@@ -27,22 +29,22 @@ SCRATCH = {
     "eq": sb(512, CODE), "es": sb(512, "uint8"), "oq": sb(128, CODE), "osb": sb(128, "uint8"),
     "mq": sb(704, CODE), "ms": sb(704, "uint8"), "mt": sb(4 * 704, "bfloat16"),
     "fq": sb(128, CODE), "fs": sb(128, "uint8"), "zq": sb(128, CODE), "zs": sb(128, "uint8"),
-    "ft": sb(512, "bfloat16"), "zt": sb(512, "bfloat16"), "fp": sb(512, "bfloat16"), "f64": sb(512, "bfloat16"),
-    "win": sb(4 * 384, "bfloat16"), "tp": sb(1024, "bfloat16"),
+    "ft": sb(512, "bfloat16"), "zt": sb(512, "bfloat16"), "fp": sb(4 * SH, "bfloat16"),
+    "win": sb(4 * WN, "bfloat16"), "tp": sb(1024, "bfloat16"), "idw": sb(WN, "float32"),
     "et": sb(528, "bfloat16"), "ot": sb(512, "bfloat16"),
-    "pi": sb(4, "int32"), "pf": sb(8, "float32"),
-    "yy": sb(256, "bfloat16"), "g16": sb(128, "bfloat16"), "src": sb(512, "bfloat16"),
+    "pi": sb(4, "int32"), "pf": sb(12, "float32"),
+    "yy": sb(256, "bfloat16"), "g16": sb(128, "bfloat16"), "src": sb(256, "bfloat16"),
     "bigm": sb(256, "float32"), "kres": sb(256, "float32"), "diag": sb(256, "bfloat16"),
-    "keep": sb(256, "bfloat16"), "hold": sb(256, "bfloat16"), "m32": sb(64, "float32"),
-    "k0": sb(32, "float32"), "cidx": sb(52, "float32"), "uoff": sb(8, "uint16"),
-    "m1": sb(256, "float32"), "tq": sb(256, "float32"), "sg": sb(512, "bfloat16"), "junk": sb(2048, "bfloat16"),
+    "keep": sb(256, "bfloat16"), "hold": sb(512, "bfloat16"), "m32": sb(64, "float32"),
+    "k0": sb(32, "float32"), "cidx": sb(72, "float32"), "uoff": sb(8, "uint16"),
+    "m1": sb(256, "float32"), "tq": sb(256, "float32"), "sg": sb(768, "bfloat16"), "junk": sb(2048, "bfloat16"),
     "r1": sb(16, "float32"), "dsc": sb(256, "bfloat16"), "cm": sb(256, "bfloat16"), "csc": sb(256, "bfloat16"),
     "u1": sb(32, "float32"), "u2": sb(32, "float32"), "i32": sb(32, "float32"), "o32": sb(32, "float32"),
     "rk": sb(16, "float32"), "gm": sb(48, "float32"), "gl": sb(48, "float32"),
     "own": sb(160, "float32"), "w": sb(512, "float32"),
-    "offe": sb(16, "uint16"), "le": sb(768, "bfloat16"), "lek": sb(128, "bfloat16"), "el": sb(8, "uint16"),
-    "offn": sb(32, "uint16"), "ln": sb(1536, "bfloat16"), "isa": sb(256, "bfloat16"), "ks": sb(256, "bfloat16"),
-    "kw": sb(256, "bfloat16"), "lm": sb(256, "bfloat16"), "lw": sb(256, "bfloat16"), "nlist": sb(16, "uint16"),
+    "offe": sb(16, "uint16"), "le": sb(1024, "bfloat16"), "lek": sb(SH, "bfloat16"), "el": sb(12, "uint16"),
+    "offn": sb(16, "uint16"), "ln": sb(1024, "bfloat16"), "fl": sb(272, "bfloat16"), "ks": sb(512, "bfloat16"),
+    "kw": sb(512, "bfloat16"), "nlist": sb(16, "uint16"),
     "nlo": sb(256, "float32"), "yo": sb(256, "float32"),
     "ps": ("psum", [128, 4096], "float32"),
 }
@@ -210,50 +212,56 @@ def rank_program(g, core, T, topo):
     iota(T.pi[:, 0:1], [[0, 1]], 0, 1, ["pi0"], False)
     iota(T.yy[:], [[0, 16], [1, 16]], 0, 0, ["yy"])
     iota(T.g16[:], [[16, 8], [0, 16]], 0, 0, ["g16"])
-    iota(T.src[:, 256:512], [[1, 16], [16, 16]], 0, 0, ["srcb"])
-    for k, (a, b) in enumerate([(208, 256), (144, 192), (80, 128), (16, 128)]):
-        fill(T.mt[:, 4 * (MO[k] + a):4 * (MO[k] + b)], 0.0, blocks(k))
     fill(T.et[:], 0.0, ["et"])
-    fill(T.r1[:, 0:1], 0.0, ["r0"])
     for k, bits in enumerate([15, 112, 16]):
         ts(T.pi[:, 1 + k:2 + k], T.pi[:, 0:1], bits, None, A.bitwise_and, None, ["pi0"], ["pi%d" % (k + 1)])
+    fill(T.r1[:, 0:1], 0.0, ["r0"])
     cp(T.pf[:, 0:3], T.pi[:, 1:4], ["pi1", "pi2", "pi3"], ["pf"])
     rr, gp, par = T.pf[:, 0:1], T.pf[:, 1:2], T.pf[:, 2:3]
+    fill(T.mt[:, 4 * (MO[0] + 208):4 * (MO[0] + 256)], 0.0, blocks(0))
+    ts(T.pf[:, 7:8], rr, -BIG, None, A.mult, None, ["pf"], ["pf7"])
+    ts(T.pf[:, 8:9], rr, 1.0, 4096.0, A.add, A.mult, ["pf"], ["pf8"])
     ts(T.pf[:, 3:4], par, 65536.0, rr, A.mult, A.subtract, ["pf"], ["pf3"])
     ts(T.pf[:, 4:5], par, -65536.0, rr, A.mult, A.subtract, ["pf"], ["pf4"])
+    ts(T.uoff[:], T.yy[:, 0:8], 16.0, None, A.mult, None, ["yy"], ["uoff"])
+    ts(T.diag[:], T.yy[:], rr, None, A.is_equal, None, ["yy", "pf"], ["diag"])
     ts(T.pf[:, 3:4], T.pf[:, 3:4], 15.5, None, A.add, None, ["pf3"], ["pf3"])
     ts(T.pf[:, 4:5], T.pf[:, 4:5], 15.5 + 16 * 65536.0, None, A.add, None, ["pf4"], ["pf4"])
-    ts(T.uoff[:], T.yy[:, 0:8], 16.0, None, A.mult, None, ["yy"], ["uoff"])
-    ts(T.bigm[:], T.yy[:], rr, BIG, A.not_equal, A.mult, ["yy", "pf"], ["bigm"])
-    ts(T.kres[:], T.yy[:], 0.0, 5 * BIG, A.is_equal, A.mult, ["yy"], ["kres"])
-    ts(T.diag[:], T.yy[:], rr, None, A.is_equal, None, ["yy", "pf"], ["diag"])
-    ts(T.keep[:], T.yy[:], 0.0, None, A.not_equal, None, ["yy"], ["keep"])
-    ts(T.k0[:, 0:16], T.yy[:, 0:16], 16.0, T.pf[:, 3:4], A.mult, A.add, ["yy", "pf3"], ["k0a"])
-    ts(T.k0[:, 16:32], T.yy[:, 0:16], 16.0, T.pf[:, 4:5], A.mult, A.add, ["yy", "pf4"], ["k0b"])
+    act(T.bigm[:], T.yy[:], AF.Abs, ["yy", "pf7"], ["bigm"], scale=BIG, bias=T.pf[:, 7:8])
+    act(T.kres[:], T.yy[:], AF.Relu, ["yy"], ["kres"], scale=-64 * BIG, bias=64 * BIG)
+    act(T.keep[:], T.yy[:], AF.Sign, ["yy"], ["keep"])
+    act(T.k0[:, 0:16], T.yy[:, 0:16], AF.Identity, ["yy", "pf3"], ["k0a"], scale=16.0, bias=T.pf[:, 3:4])
+    act(T.k0[:, 16:32], T.yy[:, 0:16], AF.Identity, ["yy", "pf4"], ["k0b"], scale=16.0, bias=T.pf[:, 4:5])
+    for k in range(2):
+        act(T.hold[:, C * k:C * k + C], T.yy[:], AF.Relu, ["yy", "pf8"], ["hold%d" % k], scale=-4096.0, bias=T.pf[:, 8:9])
     for t in range(4):
         ts(T.ot[:, t:512:4], T.g16[:], gp, None, A.is_equal, None, ["g16", "pf"], ["ot%d" % t])
-    quant(T.uq[:], T.us[:], T.ut[:], ["ut"], ["uq"])
     tt(T.et[:, 3:515:4], T.ot[:, 0:512:4], T.diag[:, 0:128], A.mult, ["ot0", "diag"], ["et"])
-    op("v", lambda: V.tensor_copy(T.uq2[:].bitcast(dt.uint32), T.uq[:].bitcast(dt.uint32).indirect(T.uoff[:])),
-       ["uq", "uoff"], ["uq2"])
-    act(T.us2[:], T.us[:].indirect(T.uoff[:]), AF.Copy, ["uq", "uoff"], ["us2"])
     quant(T.oq[:], T.osb[:], T.ot[:], ["ot0", "ot1", "ot2", "ot3"], ["oq"])
     for b in range(4):
         quant(T.eq[:, 128 * b:128 * b + 128], T.es[:, 128 * b:128 * b + 128], T.et[:, 3 - b:515 - b], ["et"], ["eq%d" % b])
+    quant(T.uq[:], T.us[:], T.ut[:], ["ut"], ["uq"])
+    fill(T.mt[:, 4 * (MO[1] + 144):4 * (MO[1] + 192)], 0.0, blocks(1))
+    op("v", lambda: V.tensor_copy(T.uq2[:].bitcast(dt.uint32), T.uq[:].bitcast(dt.uint32).indirect(T.uoff[:])),
+       ["uq", "uoff"], ["uq2"])
+    act(T.us2[:], T.us[:].indirect(T.uoff[:]), AF.Copy, ["uq", "uoff"], ["us2"])
 
     def later_constants():
-        ts(T.hold[:], T.yy[:], rr, 65536.0, A.is_le, A.mult, ["yy", "pf"], ["hold"])
         ts(T.m32[:, 32:64], T.g16[:, 0:32], par, None, A.is_equal, None, ["g16", "pf"], ["same"])
         ts(T.m32[:, 0:32], T.yy[:, 0:32], rr, None, A.is_gt, None, ["yy", "pf"], ["lt"])
         ts(T.pf[:, 5:6], rr, 16.0, None, A.mult, None, ["pf"], ["pf5"])
+        ts(T.pf[:, 6:7], rr, 2.0, 257.0, A.mult, A.add, ["pf"], ["pf6"])
         tt(T.m32[:, 0:32], T.m32[:, 0:32], T.m32[:, 32:64], A.mult, ["lt", "same"], ["lt"])
-        ts(T.cidx[:, 0:16], T.yy[:, 0:16], T.pf[:, 5:6], 256.0, A.add, A.add, ["yy", "pf5"], ["cidx"])
+        ts(T.cidx[:, 0:16], T.yy[:, 0:16], T.pf[:, 5:6], 512.0, A.add, A.add, ["yy", "pf5"], ["cidx"])
+        ts(T.cidx[:, 16:32], T.yy[:, 0:16], 32.0, T.pf[:, 6:7], A.mult, A.add, ["yy", "pf6"], ["cidx2"])
         fill(T.cidx[:, 32:52], -M0, ["negm"])
-        fill(T.w[:, 0:1], M0, ["w0"])
-        ts(T.cidx[:, 16:32], T.cidx[:, 0:16], 2.0, 256.0, A.mult, A.add, ["cidx"], ["cidx2"])
-        ts(T.src[:, 0:256], T.src[:, 256:512], -256.0, None, A.add, None, ["srcb"], ["srca"])
+        fill(T.cidx[:, 52:72], 0.0, ["zero"])
+        fill(T.w[:, 0:1], 0.0, ["w0"])
+        fill(T.fl[:, 0:1], 0.0, ["fl0"])
 
     quant(T.xq0[:], T.xs0[:], T.xin[:], ["x0"], ["xq0"])
+    fill(T.mt[:, 4 * (MO[2] + 80):4 * (MO[2] + 128)], 0.0, blocks(2))
+    fill(T.mt[:, 4 * (MO[3] + 16):4 * (MO[3] + 128)], 0.0, blocks(3))
 
     for rnd, h in enumerate(STEPS):
         mate = T.cores[rank ^ h]
@@ -275,6 +283,10 @@ def rank_program(g, core, T, topo):
         nq = cuts[5]
         op("g", lambda trs=trs: g.remote_dma_fused(trs, local_sem=T.sem.gone), [X], [])
         gone[0] += nq
+        if rnd == 0:
+            iota(T.src[:], [[1, 16], [16, 16]], 1, 0, ["src"])
+        if rnd == 2:
+            iota(T.idw[:, 0:C], [[1, C]], 0, 0, ["id0"])
 
         mm(0, C, T.uq2[:], T.us2[:], xq[:], xs[:], ["uq2", "us2", X])
         mm(1, C, T.uq2[:], T.us2[:], xq[:], xs[:], ["uq2", "us2", X])
@@ -282,6 +294,10 @@ def rank_program(g, core, T, topo):
             mm(3 + b, C, T.eq[:, 128 * b:128 * b + 128], T.es[:, 128 * b:128 * b + 128], xq[:], xs[:], ["eq%d" % b, X])
         tt(T.m1[:], bank(0, 0, C), T.bigm[:], A.add, ["P0", "bigm"], ["m1"])
         scan(T.tq[:], T.kres[:], T.m1[:], A.add, A.min, ["kres", "m1"], ["tq"])
+
+        def own_copy(b):
+            act(T.win[:, WN * b:WN * b + C], bank(3 + b, 0, C), AF.Copy, ["P%d" % (3 + b)], ["wt%d" % b], scale=64.0)
+
         for k, c in enumerate(BOTH):
             sg = T.sg[:, 256 * k:256 * k + 16 * c]
             act(sg, bank(1, 0, 16 * c), AF.Sign, ["P1", "tq"], ["sg%d" % k], bias=T.tq[:, 16 * c + 15:16 * c + 16], scale=-1.0)
@@ -295,31 +311,38 @@ def rank_program(g, core, T, topo):
         def rowsum(c):
             act(T.junk[:, 8 * c * (c - 1):8 * c * (c + 1)], slot(c, 16 * c), AF.Copy, ["m%d" % c], ["r%d" % c], accum_out=T.r1[:, c:c + 1])
 
+        def packed(k0, k1):
+            a, b = MO[k0], MO[k1] + MW[k1]
+            quant(T.mq[:, a:b], T.ms[:, a:b], T.mt[:, 4 * a:4 * b], sum([blocks(k) for k in range(k0, k1 + 1)], []),
+                  ["mq%d" % k for k in range(k0, k1 + 1)])
+
         def colsum(k):
             a, b = MO[k], MO[k] + MW[k]
-            quant(T.mq[:, a:b], T.ms[:, a:b], T.mt[:, 4 * a:4 * b], blocks(k), ["mq%d" % k])
             mm(2, MW[k], T.oq[:], T.osb[:], T.mq[:, a:b], T.ms[:, a:b], ["oq", "mq%d" % k], k == 0, k == 3)
 
         tt(slot(0, C), bank(0, 0, C), T.tq[:], A.is_gt, ["P0", "tq"], ["m0"])
-        for c in range(13, 8, -1):
+        for c in range(12, 8, -1):
             compare(c)
         scan(T.dsc[:], T.keep[:], slot(0, C), A.mult, A.add, ["keep", "m0"], ["dsc"])
-        colsum(0)
-        colsum(1)
+        packed(1, 1)
         for c in range(8, 0, -1):
             compare(c)
-        colsum(2)
-        colsum(3)
-        for c in range(13, 0, -1):
+        packed(0, 0)
+        packed(2, 3)
+        for k in range(4):
+            colsum(k)
+        for c in range(12, 3, -1):
             rowsum(c)
+        for c in range(3, 0, -1):
+            red(T.r1[:, c:c + 1], slot(c, 16 * c), ["m%d" % c], ["r%d" % c])
         for k in range(2):
             tt(T.u1[:, 16 * k:16 * k + 16], T.k0[:, 16 * k:16 * k + 16], T.dsc[:, 15:256:16], A.subtract,
                ["k0a", "k0b", "dsc"], ["u1%d" % k])
         tt(T.cm[:], bank(2, 0, C), T.diag[:], A.mult, ["P2", "diag"], ["cm"])
+        scan(T.csc[:], T.keep[:], T.cm[:], A.mult, A.add, ["keep", "cm"], ["csc"])
         for k in range(2):
             tt(T.u2[:, 16 * k:16 * k + 16], T.u1[:, 16 * k:16 * k + 16], T.r1[:], A.subtract,
                ["u1%d" % k] + ["r%d" % c for c in range(16)], ["u2%d" % k])
-        scan(T.csc[:], T.keep[:], T.cm[:], A.mult, A.add, ["keep", "cm"], ["csc"])
         for k in range(2):
             tt(T.i32[:, 16 * k:16 * k + 16], T.u2[:, 16 * k:16 * k + 16], T.csc[:, 15:256:16], A.add,
                ["u2%d" % k, "csc"], ["i32%d" % k])
@@ -332,124 +355,121 @@ def rank_program(g, core, T, topo):
            g.remote_dma(gl, gm, T.sem["af%d" % rnd], T.sem.gone, pid, rid, m), [G], [])
         gone[0] += len(eng)
 
+        if rnd == 0:
+            later_constants()
         tb = [7, 1, 0, 2]
         for b in range(4):
             mm(tb[b], C, T.eq[:, 128 * b:128 * b + 128], T.es[:, 128 * b:128 * b + 128], pq[:], pz[:], ["eq%d" % b],
                ext=[("aq%d" % rnd, nq)] if b == 0 else [])
         for b in range(4):
-            act(T.win[:, 384 * b:384 * b + C], bank(3 + b, 0, C), AF.Copy, ["P%d" % (3 + b)], ["wt%d" % b], scale=64.0)
-        if rnd == 0:
-            later_constants()
-        o = T.own
-        pa, pb, of = o[:, 16:32], o[:, 32:48], o[:, 128:129]
-        scan(o[:, 0:16], gm, T.cidx[:, 32:48], A.add, A.add, [G, "negm"], ["cfl"])
-        ts(pa, gm, M0, None, A.is_le, None, [G], ["pa"])
-        ts(pb, gm, M0 + 2, None, A.is_lt, None, [G], ["pb"])
-        ts(o[:, 64:96], T.m32[:, 0:32], o[:, 15:16], None, A.mult, None, ["lt", "cfl"], ["fx"])
-        tt(pa, pa, T.cidx[:, 0:16], A.mult, ["pa", "cidx"], ["pa"])
-        tr(o[:, 96:128], o[:, 64:96], ["fx"], ["fxt"])
-        tt(pb, pb, T.cidx[:, 16:32], A.mult, ["pb", "cidx2"], ["pb"])
-        red(of, o[:, 96:128], ["fxt"], ["of"])
-        tt(pa, pa, gm, A.subtract, ["pa", G], ["pa"])
-        ts(pb, pb, of, None, A.add, None, ["pb", "of"], ["pb"])
-        ts(pa, pa, of, M0, A.add, A.add, ["pa", "of"], ["pa"])
-        for b in range(2):
-            cp(T.tp[:, C * b:C * b + C], bank(tb[b], 0, C), ["P%d" % tb[b]], ["tp%d" % b])
-        for b in range(2, 4):
+            own_copy(b)
+        for b in range(4):
             act(T.tp[:, C * b:C * b + C], bank(tb[b], 0, C), AF.Copy, ["P%d" % tb[b]], ["tp%d" % b])
+        o = T.own
+        of = o[:, 128:129]
+        scan(o[:, 0:16], gm, T.cidx[:, 32:48], A.add, A.add, [G, "negm"], ["cfl"])
+        fill(T.ln[:, 0:2 * C], 0.0, ["ln"])
+        ts(o[:, 64:96], T.m32[:, 0:32], o[:, 15:16], None, A.mult, None, ["lt", "cfl"], ["fx"])
+        fill(T.le[:, 128:SH], 256.0, ["le"])
+        tr(o[:, 96:128], o[:, 64:96], ["fx"], ["fxt"])
         if rnd == 1:
             quant(T.vq[:], T.vs[:], T.vt[:], ["vt"], ["vq"])
+        red(of, o[:, 96:128], ["fxt"], ["of"])
 
         w = T.w
-        mm_, hh, nh, cs, pen = w[:, 1:17], w[:, 20:36], w[:, 36:52], w[:, 52:68], w[:, 68:84]
+        mm_, hh, cs, pen = w[:, 212:228], w[:, 20:36], w[:, 52:68], w[:, 68:84]
         oh, om, mt_, sc = w[:, 84:85], w[:, 85:86], w[:, 86:87], w[:, 87:88]
+        cml, res, crx, sb_, pr = w[:, 160:176], w[:, 1:17], w[:, 180:196], w[:, 196:212], w[:, 384:400]
         tt(mm_, gm, gl, A.min, [G], ["mm"], ext=[("af%d" % rnd, len(eng))])
         ts(hh, mm_, M0, None, A.is_gt, None, ["mm"], ["hh"])
-        ts(nh, mm_, M0, FAR, A.is_le, A.mult, ["mm"], ["nh"])
+        ts(pen, mm_, M0, FAR, A.is_le, A.mult, ["mm"], ["pen"])
         scan(cs, hh, hh, A.add, A.max, ["hh"], ["cs"])
-        tt(pen, nh, T.cidx[:, 0:16], A.min, ["nh", "cidx"], ["pen"])
+        tt(pen, pen, T.cidx[:, 0:16], A.min, ["pen", "cidx"], ["pen"])
         ts(w[:, 96:128], T.m32[:, 0:32], w[:, 67:68], None, A.mult, None, ["lt", "cs"], ["hx"])
         tt(pen, pen, cs, A.add, ["pen", "cs"], ["pen"])
         at = len(ops)
         tr(w[:, 128:160], w[:, 96:128], ["hx"], ["hxt"])
         red(oh, w[:, 128:160], ["hxt"], ["oh"])
         ts(T.offe[:], pen, oh, -1.0, A.add, A.add, ["pen", "oh"], ["offe"])
-        cp(T.le[:].indirect(T.offe[:]), T.src[:, 256:512], ["offe", "srcb"], ["le"])
-        scan(T.lek[:], T.hold[:, 0:128], T.le[:, 0:128], A.add, A.min, ["hold", "le"], ["lek"])
-        cp(T.el[:], T.lek[:, 15:128:16], ["lek"], ["el"])
+        cp(T.le[:].indirect(T.offe[:]), T.src[:], ["offe", "src"], ["le"])
+        scan(T.lek[:], T.hold[:, 0:SH], T.le[:, 0:SH], A.add, A.min, ["hold0", "le"], ["lek"])
+        ts(T.el[:], T.lek[:, 15:SH:16], -1.0, None, A.add, None, ["lek"], ["el"])
         list_e = taken(at)
 
-        cmx, cml, crl, sb_ = w[:, 160:176], w[:, 161:177], w[:, 180:196], w[:, 196:212]
-        scan(w[:, 160:177], w[:, 0:17], T.cidx[:, 32:49], A.add, A.add, ["mm", "w0", "negm"], ["cml"])
-        ts(w[:, 256:320], T.m32[:], w[:, 176:177], None, A.mult, None, ["lt", "same", "cml"], ["mx"])
+        scan(cml, mm_, T.cidx[:, 32:48], A.add, A.add, ["mm", "negm"], ["cml"])
+        ts(w[:, 256:320], T.m32[:], w[:, 175:176], None, A.mult, None, ["lt", "same", "cml"], ["mx"])
         tr(w[:, 320:384], w[:, 256:320], ["mx"], ["mxt"])
         red(om, w[:, 320:352], ["mxt"], ["om"])
         red(mt_, w[:, 352:384], ["mxt"], ["mtot"])
-        ts(sb_, mm_, M0 + 2, FAR, A.is_lt, A.mult, ["mm"], ["sb"])
+        tt(res, gm, mm_, A.subtract, [G, "mm"], ["res"])
         weave(list_e, taken(at))
         ts(sc, om, -2.0, mt_, A.mult, A.add, ["om", "mtot"], ["sc"])
-        tt(w[:, 224:240], cmx, nh, A.add, ["cml", "nh"], ["x1a"])
-        scan(crl, gm, mm_, A.add, A.subtract, [G, "mm", "sc"], ["crl"], sc)
-        tt(w[:, 240:256], cml, sb_, A.add, ["cml", "sb"], ["x1b"])
-        tt(w[:, 384:400], crl, pa, A.add, ["crl", "pa"], ["x2a"])
-        tt(w[:, 400:416], crl, pb, A.add, ["crl", "pb"], ["x2b"])
-        tt(w[:, 224:256], w[:, 224:256], w[:, 384:416], A.min, ["x1a", "x1b", "x2a", "x2b"], ["x1a", "x1b"])
-        ts(T.offn[:, 0:16], w[:, 224:240], om, None, A.add, None, ["x1a", "om"], ["offa"])
-        ts(T.offn[:, 16:32], w[:, 240:256], om, -1.0, A.add, A.add, ["x1b", "om"], ["offb"])
+        ts(pr, res, 0.0, FAR, A.is_le, A.mult, ["res"], ["pr"])
+        ts(sc, sc, of, -255.0, A.add, A.add, ["sc", "of"], ["sc"])
+        tt(pr, pr, T.cidx[:, 0:16], A.min, ["pr", "cidx"], ["pr"])
+        scan(crx, w[:, 0:16], T.cidx[:, 52:68], A.add, A.add, ["res", "w0", "zero", "sc"], ["crx"], sc)
+        ts(sb_, mm_, M0 + 2, FAR, A.is_lt, A.mult, ["mm"], ["sb"])
+        tt(pr, pr, crx, A.add, ["crx", "pr"], ["pr"])
+        tt(sb_, cml, sb_, A.add, ["cml", "sb"], ["sb"])
+        tt(pr, pr, sb_, A.min, ["pr", "sb"], ["pr"])
+        ts(T.offn[:], pr, om, 255.0, A.add, A.add, ["pr", "om"], ["offn"])
 
         for b in range(4):
-            act(T.ft[:, b:512:4], T.tp[:, C * b:C * b + C].indirect(T.el[:]), AF.Copy, ["tp%d" % b, "el"], ["ft%d" % b])
+            act(T.ft[:, b:512:4], T.tp[:, C * b:C * b + C].indirect(T.el[:, 0:8]), AF.Copy, ["tp%d" % b, "el"], ["ft%d" % b])
         for b in range(4):
-            act(T.fp[:, 128 * b:128 * b + 128], T.win[:, 384 * b:384 * b + C].indirect(T.el[:]), AF.Copy,
+            act(T.fp[:, SH * b:SH * b + SH], T.win[:, WN * b:WN * b + C].indirect(T.el[:]), AF.Copy,
                 ["wt%d" % b, "el"], ["fp%d" % b], scale=1.0 / 64)
-        act(T.f64[:], T.fp[:], AF.Copy, ["fp0", "fp1", "fp2", "fp3"], ["f64"], scale=64.0)
+        for b in range(4):
+            act(T.win[:, WN * b + C + 1:WN * b + WN:2], T.fp[:, SH * b:SH * b + SH], AF.Copy, ["fp%d" % b], ["wo%d" % b], scale=64.0)
+            act(T.win[:, WN * b + 2 * C:WN * b + WN:2], T.fp[:, SH * b + 128:SH * b + SH], AF.Copy, ["fp%d" % b], ["we%d" % b], scale=64.0)
         quant(T.fq[:], T.fs[:], T.ft[:], ["ft0", "ft1", "ft2", "ft3"], ["fq"])
         for b in range(4):
             mm(3 + b, 128, T.eq[:, 128 * b:128 * b + 128], T.es[:, 128 * b:128 * b + 128], T.fq[:], T.fs[:], ["eq%d" % b, "fq"])
-        cp(T.ln[:].indirect(T.offn[:]), T.src[:], ["offa", "offb", "srca", "srcb"], ["ln"])
+        cp(T.ln[:].indirect(T.offn[:]), T.src[:], ["offn", "src"], ["ln"])
+        ts(T.fl[:, 1:C + 1], T.ln[:, C:2 * C], 0.0, None, A.is_gt, None, ["ln"], ["fl"])
+        scan(T.ks[:, 0:C], T.ln[:, 0:C], T.ln[:, 0:C], A.max, A.max, ["ln"], ["ks0"])
 
         for b in range(4):
-            tt(T.zt[:, b:512:4], T.fp[:, 128 * b:128 * b + 128], bank(3 + b, 0, 128), A.subtract,
+            tt(T.zt[:, b:512:4], T.fp[:, SH * b:SH * b + 128], bank(3 + b, 0, 128), A.subtract,
                ["fp%d" % b, "P%d" % (3 + b)], ["zt%d" % b])
-        ts(T.isa[:], T.ln[:, 0:C], 0.0, None, A.is_lt, None, ["ln"], ["isa"])
+        scan(T.ks[:, C:2 * C], T.fl[:, 1:C + 1], T.fl[:, 0:C], A.add, A.add, ["fl", "fl0"], ["ks1"])
         quant(T.zq[:], T.zs[:], T.zt[:], ["zt0", "zt1", "zt2", "zt3"], ["zq"])
         for b in range(4):
             mm(tb[b], 128, T.wq[:, 128 * b:128 * b + 128], T.wsc[:, 128 * b:128 * b + 128], T.zq[:], T.zs[:], ["wq", "wsc", "zq"])
 
         def made(k):
-            tt(T.win[:, 384 * k + C:384 * k + 384], bank(tb[k], 0, 128), T.f64[:, 128 * k:128 * k + 128], A.add,
-               ["P%d" % tb[k], "f64"], ["wg%d" % k])
+            tt(T.win[:, WN * k + C:WN * k + 2 * C:2], bank(tb[k], 0, 128), T.win[:, WN * k + C + 1:WN * k + 2 * C:2], A.add,
+               ["P%d" % tb[k], "wo%d" % k], ["wg%d" % k])
 
-        scan(T.ks[:], T.isa[:], T.src[:, 0:C], A.add, A.max, ["isa", "srca"], ["ks"], -1.0)
-        tt(T.lm[:], T.ln[:, 0:C], T.diag[:], A.mult, ["ln", "diag"], ["lm"])
-        scan(T.kw[:], T.hold[:], T.ks[:], A.add, A.min, ["hold", "ks"], ["kw"])
-        scan(T.lw[:], T.keep[:], T.lm[:], A.mult, A.add, ["keep", "lm"], ["lw"])
-        lw, kw = T.lw[:, 15:256:16], T.kw[:, 15:256:16]
-        q2, nm, z2 = w[:, 432:448], w[:, 448:464], w[:, 464:480]
+        scan(T.kw[:], T.hold[:], T.ks[:], A.add, A.min, ["hold0", "hold1", "ks0", "ks1"], ["kw"])
+        lw, kw = T.kw[:, 15:C:16], T.kw[:, C + 15:2 * C:16]
+        q2, z2 = w[:, 432:448], w[:, 464:480]
+        ts(q2, lw, 0.0, FAR, A.is_le, A.mult, ["kw"], ["q2"])
+        tt(z2, T.cidx[:, 16:32], kw, A.subtract, ["kw", "cidx2"], ["z2"])
+        tt(q2, q2, lw, A.add, ["kw", "q2"], ["q2"])
         made(0)
-        ts(q2, lw, 0.0, 256.0, A.is_ge, A.mult, ["lw"], ["q2"])
+        tt(z2, z2, q2, A.min, ["z2", "q2"], ["z2"])
         made(1)
-        tt(z2, kw, q2, A.add, ["kw", "q2"], ["z2"])
-        tt(nm, lw, q2, A.subtract, ["lw", "q2"], ["nm"])
-        ts(z2, z2, 127.0, -1024.0, A.is_gt, A.mult, ["z2"], ["z2"])
-        tt(z2, z2, kw, A.add, ["z2", "kw"], ["z2"])
-        tt(z2, z2, nm, A.max, ["z2", "nm"], ["z2"])
-        ts(T.nlist[:], z2, 256.0, None, A.add, None, ["z2"], ["nlist"])
+        ts(T.nlist[:], z2, -1.0, None, A.add, None, ["z2"], ["nlist"])
         made(2)
         made(3)
 
+        def part(b):
+            return ["wt%d" % b, "wg%d" % b, "wo%d" % b, "we%d" % b, "nlist"]
+
         for b in (0, 1):
-            act(T.xt[:, b:1024:4], T.win[:, 384 * b:384 * b + 384].indirect(T.nlist[:]), AF.Copy,
-                ["wt%d" % b, "wg%d" % b, "nlist"], ["xt%d" % b], scale=1.0 / 64)
-        for b in (2, 3):
-            ts(T.xt[:, b:1024:4], T.win[:, 384 * b:384 * b + 384].indirect(T.nlist[:]), 1.0 / 64, None, A.mult, None,
-               ["wt%d" % b, "wg%d" % b, "nlist"], ["xt%d" % b])
-        quant(T["xq%d" % (rnd + 1)][:], T["xs%d" % (rnd + 1)][:], T.xt[:], ["xt0", "xt1", "xt2", "xt3"], ["xq%d" % (rnd + 1)])
+            act(T.xt[:, b:1024:4], T.win[:, WN * b:WN * b + WN].indirect(T.nlist[:]), AF.Copy, part(b), ["xt%d" % b], scale=1.0 / 64)
+        act(T.xt[:, 2:128:4], T.win[:, WN * 2:WN * 3].indirect(T.nlist[:, 0:2]), AF.Copy, part(2), ["xt4"], scale=1.0 / 64)
+        ts(T.xt[:, 130:1024:4], T.win[:, WN * 2:WN * 3].indirect(T.nlist[:, 2:16]), 1.0 / 64, None, A.mult, None, part(2), ["xt2"])
+        ts(T.xt[:, 3:1024:4], T.win[:, WN * 3:WN * 4].indirect(T.nlist[:]), 1.0 / 64, None, A.mult, None, part(3), ["xt3"])
+        quant(T["xq%d" % (rnd + 1)][:], T["xs%d" % (rnd + 1)][:], T.xt[:], ["xt0", "xt1", "xt2", "xt3", "xt4"], ["xq%d" % (rnd + 1)])
+        if rnd == 2:
+            for k in range(2):
+                ts(T.idw[:, C + k:WN:2], T.le[:, 0:SH], -1.0, None, A.add, None, ["le"], ["id%d" % (k + 1)])
 
     mm(3, C, T.vq[:], T.vs[:], T.xq3[:], T.xs3[:], ["vq", "xq3"])
     dma("s", T.oc[:], T.xq3[:].bitcast(dt.uint8), ["xq3"], [])
-    ts(T.isa[:], T.isa[:], 256.0, None, A.mult, None, ["isa"], ["isa"])
-    tt(T.nlo[:], T.ln[:, 0:C], T.isa[:], A.add, ["ln", "isa"], ["nlo"])
+    cp(T.nlo[:], T.idw[:].indirect(T.nlist[:]), ["id0", "id1", "id2", "nlist"], ["nlo"])
     act(T.yo[:], bank(3, 0, C), AF.Copy, ["P3"], ["yo"])
     dma("a", T.y[:], T.yo[:], ["yo"], [])
     for k in range(4):

@@ -5,15 +5,12 @@ A = AluOpType
 AF = ActivationFunctionType
 C = 256
 SH = 192
-WN = C + 2 * SH
+WN = SH + C
 STEPS = [1, 2, 4]
-M0 = 12582912.0
 BIG = 2.0 ** 88
-FAR = 8192.0
+ETA = 2.0 ** -10
 CODE = "float8_e4m3fn_x4"
-MW = [256, 192, 128, 128]
-MO = [0, 256, 448, 576]
-BOTH = (15, 14, 13)
+OPT = dict(nss=3, nred=8, vsplit=2, tpv=0)
 
 
 def sb(n, d):
@@ -27,24 +24,26 @@ SCRATCH = {
     "uq": sb(128, CODE), "us": sb(128, "uint8"), "uq2": sb(128, CODE), "us2": sb(128, "uint8"),
     "vq": sb(128, CODE), "vs": sb(128, "uint8"),
     "eq": sb(512, CODE), "es": sb(512, "uint8"), "oq": sb(128, CODE), "osb": sb(128, "uint8"),
-    "mq": sb(704, CODE), "ms": sb(704, "uint8"), "mt": sb(4 * 704, "bfloat16"),
-    "fq": sb(128, CODE), "fs": sb(128, "uint8"), "zq": sb(128, CODE), "zs": sb(128, "uint8"),
-    "ft": sb(512, "bfloat16"), "zt": sb(512, "bfloat16"), "fp": sb(4 * SH, "bfloat16"),
+    "mq": sb(768, CODE), "ms": sb(768, "uint8"), "mt": sb(4 * 768, "bfloat16"),
+    "fq": sb(256, CODE), "fs": sb(256, "uint8"), "zq": sb(128, CODE), "zs": sb(128, "uint8"),
+    "zt": sb(512, "bfloat16"), "zf": sb(1024, "bfloat16"),
     "win": sb(4 * WN, "bfloat16"), "tp": sb(1024, "bfloat16"), "idw": sb(WN, "float32"),
-    "et": sb(528, "bfloat16"), "ot": sb(512, "bfloat16"),
-    "pi": sb(4, "int32"), "pf": sb(12, "float32"),
-    "yy": sb(256, "bfloat16"), "g16": sb(128, "bfloat16"), "src": sb(256, "bfloat16"),
-    "bigm": sb(256, "float32"), "kres": sb(256, "float32"), "diag": sb(256, "bfloat16"),
-    "keep": sb(256, "bfloat16"), "hold": sb(512, "bfloat16"), "m32": sb(64, "float32"),
-    "k0": sb(32, "float32"), "cidx": sb(72, "float32"), "uoff": sb(8, "uint16"),
-    "m1": sb(256, "float32"), "tq": sb(256, "float32"), "sg": sb(768, "bfloat16"), "junk": sb(2048, "bfloat16"),
-    "r1": sb(16, "float32"), "dsc": sb(256, "bfloat16"), "cm": sb(256, "bfloat16"), "csc": sb(256, "bfloat16"),
-    "u1": sb(32, "float32"), "u2": sb(32, "float32"), "i32": sb(32, "float32"), "o32": sb(32, "float32"),
-    "rk": sb(16, "float32"), "gm": sb(48, "float32"), "gl": sb(48, "float32"),
-    "own": sb(160, "float32"), "w": sb(512, "float32"),
-    "offe": sb(16, "uint16"), "le": sb(1024, "bfloat16"), "lek": sb(SH, "bfloat16"), "el": sb(12, "uint16"),
-    "offn": sb(16, "uint16"), "ln": sb(1024, "bfloat16"), "fl": sb(272, "bfloat16"), "ks": sb(512, "bfloat16"),
-    "kw": sb(512, "bfloat16"), "nlist": sb(16, "uint16"),
+    "et": sb(528, "bfloat16"), "ot": sb(512, "bfloat16"), "one": sb(128, "bfloat16"),
+    "pi": sb(4, "int32"), "pf": sb(16, "float32"),
+    "yy": sb(256, "bfloat16"), "g16": sb(128, "bfloat16"), "up": sb(256, "bfloat16"), "down": sb(256, "bfloat16"),
+    "slot": sb(256, "bfloat16"),
+    "bigm": sb(256, "float32"), "kres": sb(256, "float32"),
+    "keep": sb(256, "bfloat16"), "hold": sb(256, "bfloat16"), "drop": sb(256, "bfloat16"),
+    "m32": sb(96, "bfloat16"), "k32": sb(128, "bfloat16"),
+    "k0": sb(16, "float32"), "cidx": sb(64, "float32"), "uoff": sb(8, "uint16"),
+    "m1": sb(256, "float32"), "tq": sb(256, "float32"), "sg": sb(1024, "bfloat16"), "junk": sb(2048, "bfloat16"),
+    "r1": sb(16, "float32"), "dsc": sb(256, "bfloat16"), "csc": sb(256, "float32"),
+    "ua": sb(48, "float32"), "i32": sb(32, "bfloat16"), "o32": sb(32, "bfloat16"),
+    "gm": sb(96, "bfloat16"), "gl": sb(96, "bfloat16"),
+    "own": sb(192, "float32"), "w": sb(256, "float32"), "mx": sb(384, "bfloat16"),
+    "offe": sb(16, "uint16"), "le": sb(768, "bfloat16"), "lek": sb(SH, "bfloat16"), "el": sb(12, "uint16"),
+    "offn": sb(16, "uint16"), "ln": sb(768, "bfloat16"), "ks": sb(5 * C, "bfloat16"), "ux": sb(C, "float32"),
+    "nlist": sb(16, "uint16"),
     "nlo": sb(256, "float32"), "yo": sb(256, "float32"),
     "ps": ("psum", [128, 4096], "float32"),
 }
@@ -55,7 +54,7 @@ for _k in range(3):
     SCRATCH["pq%d" % _k] = sb(256, CODE)
     SCRATCH["pz%d" % _k] = sb(256, "uint8")
 
-POOL = {"v": 60, "a": 30, "p": 20, "g": 6}
+POOL = {"v": 60, "a": 30, "p": 20, "g": 10}
 NDMA = 16
 SEMAPHORES = (["%s%d" % (q, k) for q in POOL for k in range(POOL[q])] + ["d%d" % k for k in range(NDMA)]
               + ["aq0", "aq1", "aq2", "af0", "af1", "af2", "gone"])
@@ -168,6 +167,9 @@ def rank_program(g, core, T, topo):
         op("p", lambda: PE.matmul_mx(T.ps[:, 512 * bank:512 * bank + n], lq, ls, rq, rs, start, stop),
            rd, ["P%d" % bank], ext)
 
+    def unpack(bank, b, rq, rs, rd, start=True, stop=True, ext=()):
+        mm(bank, C, T.eq[:, 128 * b:128 * b + 128], T.es[:, 128 * b:128 * b + 128], rq, rs, ["eq%d" % b] + rd, start, stop, ext)
+
     def bank(k, a, b):
         return T.ps[:, 512 * k + a:512 * k + b]
 
@@ -181,87 +183,108 @@ def rank_program(g, core, T, topo):
         else:
             op("g", lambda: g.iota(out, pat, base, mult), [], wr)
 
-    def slot(c, n):
-        k, t = (0, 0) if c == 0 else divmod(16 - c, 4)
-        return T.mt[:, 4 * MO[k] + t:4 * (MO[k] + n):4]
+    nss = OPT["nss"]
+    both = list(range(15, 15 - nss, -1))
+    rest = [c for c in range(15, 8, -1) if c not in both]
+    lanes = [[0] + rest[:3], [8, 7, 6, 5], [4, 3, 2, 1], both + rest[3:]]
+    MW = [256, 128, 128, 240]
+    MO = [0, 256, 384, 512]
+
+    def slot(c, n, a=0):
+        k = [c in x for x in lanes].index(True)
+        t = lanes[k].index(c)
+        return T.mt[:, 4 * (MO[k] + a) + t:4 * (MO[k] + n):4]
 
     def blocks(k):
-        return ["m%d" % c for c in range(16) if (c == 0 and k == 0) or (c > 0 and (16 - c) // 4 == k)]
+        return ["m%d" % c for c in lanes[k]]
+
+    def pad(k):
+        a = 16 * min(c if c else 16 for c in lanes[k])
+        fill(T.mt[:, 4 * (MO[k] + a):4 * (MO[k] + MW[k])], 0.0, blocks(k))
 
     def maskof(es):
         return sum(1 << e for e in es)
 
-    def weave(first, second):
-        for k in range(max(len(first), len(second))):
-            ops.extend(first[k:k + 1])
-            ops.extend(second[k:k + 1])
-
-    def taken(start):
-        got = ops[start:]
-        del ops[start:]
-        return got
-
     gone = [0]
 
-    dma("s", T.xin[:], T.x[:], [], ["x0"])
     dma("a", T.ut[:], T.u[:], [], ["ut"])
+    dma("s", T.xin[:], T.x[:], [], ["x0"])
     dma("s", T.wq[:].bitcast(dt.uint8), T.wc[:], ["x0"], ["wq"])
     dma("s", T.wsc[:], T.ws[:], [], ["wsc"])
     dma("s", T.vt[:], T.v[:], [], ["vt"])
 
     iota(T.pi[:, 0:1], [[0, 1]], 0, 1, ["pi0"], False)
     iota(T.yy[:], [[0, 16], [1, 16]], 0, 0, ["yy"])
-    iota(T.g16[:], [[16, 8], [0, 16]], 0, 0, ["g16"])
+    fill(T.one[:], 1.0, ["one"])
     fill(T.et[:], 0.0, ["et"])
+    iota(T.g16[:], [[16, 8], [0, 16]], 0, 0, ["g16"])
+    op("g", lambda: g.affine_select(T.et[:, 3:515:4], T.one[:], [[-1, 128]], A.is_equal, 0.0, 0, 1), ["one"], ["et"])
     for k, bits in enumerate([15, 112, 16]):
         ts(T.pi[:, 1 + k:2 + k], T.pi[:, 0:1], bits, None, A.bitwise_and, None, ["pi0"], ["pi%d" % (k + 1)])
     fill(T.r1[:, 0:1], 0.0, ["r0"])
     cp(T.pf[:, 0:3], T.pi[:, 1:4], ["pi1", "pi2", "pi3"], ["pf"])
     rr, gp, par = T.pf[:, 0:1], T.pf[:, 1:2], T.pf[:, 2:3]
-    fill(T.mt[:, 4 * (MO[0] + 208):4 * (MO[0] + 256)], 0.0, blocks(0))
-    ts(T.pf[:, 7:8], rr, -BIG, None, A.mult, None, ["pf"], ["pf7"])
-    ts(T.pf[:, 8:9], rr, 1.0, 4096.0, A.add, A.mult, ["pf"], ["pf8"])
-    ts(T.pf[:, 3:4], par, 65536.0, rr, A.mult, A.subtract, ["pf"], ["pf3"])
-    ts(T.pf[:, 4:5], par, -65536.0, rr, A.mult, A.subtract, ["pf"], ["pf4"])
+
+    def column(k, src, scale, bias):
+        ts(T.pf[:, k:k + 1], src, scale, bias, A.mult, A.add, ["pf"], ["pf%d" % k])
+        return T.pf[:, k:k + 1]
+
+    pad(0)
+    nbig = column(3, rr, -BIG, 0.0)
+    hbias = column(4, rr, 4096.0, 4096.0)
+    kbias = column(5, rr, -1025.0, 15375.5)
     ts(T.uoff[:], T.yy[:, 0:8], 16.0, None, A.mult, None, ["yy"], ["uoff"])
-    ts(T.diag[:], T.yy[:], rr, None, A.is_equal, None, ["yy", "pf"], ["diag"])
-    ts(T.pf[:, 3:4], T.pf[:, 3:4], 15.5, None, A.add, None, ["pf3"], ["pf3"])
-    ts(T.pf[:, 4:5], T.pf[:, 4:5], 15.5 + 16 * 65536.0, None, A.add, None, ["pf4"], ["pf4"])
-    act(T.bigm[:], T.yy[:], AF.Abs, ["yy", "pf7"], ["bigm"], scale=BIG, bias=T.pf[:, 7:8])
+    act(T.bigm[:], T.yy[:], AF.Abs, ["yy", "pf3"], ["bigm"], scale=BIG, bias=nbig)
     act(T.kres[:], T.yy[:], AF.Relu, ["yy"], ["kres"], scale=-64 * BIG, bias=64 * BIG)
-    act(T.keep[:], T.yy[:], AF.Sign, ["yy"], ["keep"])
-    act(T.k0[:, 0:16], T.yy[:, 0:16], AF.Identity, ["yy", "pf3"], ["k0a"], scale=16.0, bias=T.pf[:, 3:4])
-    act(T.k0[:, 16:32], T.yy[:, 0:16], AF.Identity, ["yy", "pf4"], ["k0b"], scale=16.0, bias=T.pf[:, 4:5])
-    for k in range(2):
-        act(T.hold[:, C * k:C * k + C], T.yy[:], AF.Relu, ["yy", "pf8"], ["hold%d" % k], scale=-4096.0, bias=T.pf[:, 8:9])
-    for t in range(4):
-        ts(T.ot[:, t:512:4], T.g16[:], gp, None, A.is_equal, None, ["g16", "pf"], ["ot%d" % t])
-    tt(T.et[:, 3:515:4], T.ot[:, 0:512:4], T.diag[:, 0:128], A.mult, ["ot0", "diag"], ["et"])
-    quant(T.oq[:], T.osb[:], T.ot[:], ["ot0", "ot1", "ot2", "ot3"], ["oq"])
-    for b in range(4):
-        quant(T.eq[:, 128 * b:128 * b + 128], T.es[:, 128 * b:128 * b + 128], T.et[:, 3 - b:515 - b], ["et"], ["eq%d" % b])
     quant(T.uq[:], T.us[:], T.ut[:], ["ut"], ["uq"])
-    fill(T.mt[:, 4 * (MO[1] + 144):4 * (MO[1] + 192)], 0.0, blocks(1))
+    pad(1)
     op("v", lambda: V.tensor_copy(T.uq2[:].bitcast(dt.uint32), T.uq[:].bitcast(dt.uint32).indirect(T.uoff[:])),
        ["uq", "uoff"], ["uq2"])
     act(T.us2[:], T.us[:].indirect(T.uoff[:]), AF.Copy, ["uq", "uoff"], ["us2"])
+    act(T.keep[:], T.yy[:], AF.Sign, ["yy"], ["keep"])
+    act(T.k0[:], T.yy[:, 0:16], AF.Identity, ["yy", "pf5"], ["k0"], scale=16.0, bias=kbias)
+    act(T.hold[:], T.yy[:], AF.Relu, ["yy", "pf4"], ["hold"], scale=-4096.0, bias=hbias)
+    act(T.drop[:], T.hold[:], AF.Identity, ["hold"], ["drop"], scale=16.0, bias=-1024.0)
+    for t in range(4):
+        ts(T.ot[:, t:512:4], T.g16[:], gp, None, A.is_equal, None, ["g16", "pf"], ["ot%d" % t])
+    for b in range(4):
+        quant(T.eq[:, 128 * b:128 * b + 128], T.es[:, 128 * b:128 * b + 128], T.et[:, 3 - b:515 - b], ["et"], ["eq%d" % b])
+    quant(T.xq0[:], T.xs0[:], T.xin[:], ["x0"], ["xq0"])
+    quant(T.oq[:], T.osb[:], T.ot[:], ["ot0", "ot1", "ot2", "ot3"], ["oq"])
+    pad(3)
+    pad(2)
+    scale = [T.pf[:, 6:7], T.pf[:, 7:8]]
+    shift = [T.pf[:, 8:9], T.pf[:, 9:10]]
+
+    def middle_constants():
+        column(6, par, -2.0 ** -21, 2.0 ** -17)
+        column(7, par, 2.0 ** -21, 0.0)
+        column(8, par, -1.0 / 64, 0.125)
+        column(9, par, 1.0 / 64, -0.125)
+        fill(T.gm[:], 0.0, ["gm0", "gm1", "gm2"])
+
+    lt, step, negk, ieta = T.m32[:, 0:32], T.cidx[:, 0:17], T.cidx[:, 32:48], T.cidx[:, 48:64]
+    first, ubias = T.pf[:, 10:11], T.pf[:, 11:12]
 
     def later_constants():
-        ts(T.m32[:, 32:64], T.g16[:, 0:32], par, None, A.is_equal, None, ["g16", "pf"], ["same"])
-        ts(T.m32[:, 0:32], T.yy[:, 0:32], rr, None, A.is_gt, None, ["yy", "pf"], ["lt"])
-        ts(T.pf[:, 5:6], rr, 16.0, None, A.mult, None, ["pf"], ["pf5"])
-        ts(T.pf[:, 6:7], rr, 2.0, 257.0, A.mult, A.add, ["pf"], ["pf6"])
-        tt(T.m32[:, 0:32], T.m32[:, 0:32], T.m32[:, 32:64], A.mult, ["lt", "same"], ["lt"])
-        ts(T.cidx[:, 0:16], T.yy[:, 0:16], T.pf[:, 5:6], 512.0, A.add, A.add, ["yy", "pf5"], ["cidx"])
-        ts(T.cidx[:, 16:32], T.yy[:, 0:16], 32.0, T.pf[:, 6:7], A.mult, A.add, ["yy", "pf6"], ["cidx2"])
-        fill(T.cidx[:, 32:52], -M0, ["negm"])
-        fill(T.cidx[:, 52:72], 0.0, ["zero"])
-        fill(T.w[:, 0:1], 0.0, ["w0"])
-        fill(T.fl[:, 0:1], 0.0, ["fl0"])
+        ts(T.m32[:, 64:96], T.g16[:, 0:32], par, None, A.is_equal, None, ["g16", "pf"], ["same"])
+        ts(lt, T.yy[:, 0:32], rr, None, A.is_gt, None, ["yy", "pf"], ["lt"])
+        column(10, rr, 16.0, 255.0)
+        tt(lt, lt, T.m32[:, 64:96], A.mult, ["lt", "same"], ["lt"])
+        column(11, rr, 1024.0, WN + 1 - 15360.0)
+        fill(T.own[:, 0:18], 0.0, ["kb"])
+        ts(T.m32[:, 32:64], lt, -2.0, None, A.mult, None, ["lt"], ["sl"])
+        ts(negk, T.yy[:, 0:16], first, -1.0, A.add, A.mult, ["yy", "pf10"], ["negk"])
+        tt(T.m32[:, 32:64], T.m32[:, 32:64], T.m32[:, 64:96], A.add, ["sl", "same"], ["sl"])
+        ts(ieta, negk, 255.0, -ETA, A.add, A.mult, ["negk"], ["ieta"])
+        ts(T.m32[:, 64:96], T.m32[:, 64:96], 4096.0 / ETA, None, A.mult, None, ["same"], ["same"])
 
-    quant(T.xq0[:], T.xs0[:], T.xin[:], ["x0"], ["xq0"])
-    fill(T.mt[:, 4 * (MO[2] + 80):4 * (MO[2] + 128)], 0.0, blocks(2))
-    fill(T.mt[:, 4 * (MO[3] + 16):4 * (MO[3] + 128)], 0.0, blocks(3))
+    def last_constants():
+        fill(T.cidx[:, 0:16], 1.0, ["step"])
+        ts(T.cidx[:, 16:17], rr, -16.0, -271.0, A.mult, A.add, ["pf"], ["step2"])
+        fill(T.k32[:], 1.0, ["k32"])
+        fill(T.w[:, 0:64], 0.0, ["mm", "hh"])
+        fill(T.k32[:, 0:128:32], 0.0, ["k32"])
 
     for rnd, h in enumerate(STEPS):
         mate = T.cores[rank ^ h]
@@ -270,206 +293,190 @@ def rank_program(g, core, T, topo):
         xq, xs, pq, pz = T["xq%d" % rnd], T["xs%d" % rnd], T["pq%d" % rnd], T["pz%d" % rnd]
         X = "xq%d" % rnd
 
-        quarter, eighth = len(eng) // 4, len(eng) // 8
-        cuts = [0, quarter, 2 * quarter, 3 * quarter, 3 * quarter + eighth, 4 * quarter]
-        trs = []
-        for k in range(5):
-            if k < 4:
-                s_, d_ = xq[:, 64 * k:64 * k + 64].bitcast(dt.uint8), pq[:, 64 * k:64 * k + 64].bitcast(dt.uint8)
-            else:
-                s_, d_ = xs[:], pz[:]
-            trs.append(RemoteDMATransfer(dst_ids=[DstId(rid=rid, pnc=pid)], dma_engine_mask=maskof(eng[cuts[k]:cuts[k + 1]]),
-                                         remote_sem=T.sem["aq%d" % rnd], src=s_, dst=d_))
-        nq = cuts[5]
-        op("g", lambda trs=trs: g.remote_dma_fused(trs, local_sem=T.sem.gone), [X], [])
-        gone[0] += nq
+        def send(out, a, sem, rd, pid=pid, rid=rid, eng=eng):
+            op("g", lambda: g.remote_dma(out, a, T.sem[sem], T.sem.gone, pid, rid, maskof(eng)), rd, [])
+            gone[0] += len(eng)
+
+        send(pq[:].bitcast(dt.uint8), xq[:].bitcast(dt.uint8), "aq%d" % rnd, [X])
+        send(pz[:], xs[:], "aq%d" % rnd, [X])
         if rnd == 0:
-            iota(T.src[:], [[1, 16], [16, 16]], 1, 0, ["src"])
+            iota(T.up[:], [[1, 16], [16, 16]], 1, 0, ["up"])
+            iota(T.down[:], [[-1, 16], [-16, 16]], C, 0, ["down"])
+            iota(T.slot[:], [[1, C]], -1, 0, ["slot"])
         if rnd == 2:
-            iota(T.idw[:, 0:C], [[1, C]], 0, 0, ["id0"])
+            iota(T.idw[:, SH:WN], [[1, C]], 0, 0, ["id0"])
 
         mm(0, C, T.uq2[:], T.us2[:], xq[:], xs[:], ["uq2", "us2", X])
         mm(1, C, T.uq2[:], T.us2[:], xq[:], xs[:], ["uq2", "us2", X])
         for b in range(4):
-            mm(3 + b, C, T.eq[:, 128 * b:128 * b + 128], T.es[:, 128 * b:128 * b + 128], xq[:], xs[:], ["eq%d" % b, X])
-        tt(T.m1[:], bank(0, 0, C), T.bigm[:], A.add, ["P0", "bigm"], ["m1"])
-        scan(T.tq[:], T.kres[:], T.m1[:], A.add, A.min, ["kres", "m1"], ["tq"])
+            unpack(3 + b, b, xq[:], xs[:], [X])
+        for a in (128, 0):
+            tt(T.m1[:, a:a + 128], bank(0, a, a + 128), T.bigm[:, a:a + 128], A.add, ["P0", "bigm"], ["m1%d" % a])
+        for a in (128, 0):
+            scan(T.tq[:, a:a + 128], T.kres[:, a:a + 128], T.m1[:, a:a + 128], A.add, A.min, ["kres", "m1%d" % a], ["tq%d" % a])
 
-        def own_copy(b):
-            act(T.win[:, WN * b:WN * b + C], bank(3 + b, 0, C), AF.Copy, ["P%d" % (3 + b)], ["wt%d" % b], scale=64.0)
-
-        for k, c in enumerate(BOTH):
-            sg = T.sg[:, 256 * k:256 * k + 16 * c]
-            act(sg, bank(1, 0, 16 * c), AF.Sign, ["P1", "tq"], ["sg%d" % k], bias=T.tq[:, 16 * c + 15:16 * c + 16], scale=-1.0)
-        for k, c in enumerate(BOTH):
-            sg = T.sg[:, 256 * k:256 * k + 16 * c]
-            act(slot(c, 16 * c), sg, AF.Sign, ["sg%d" % k], ["m%d" % c, "r%d" % c], bias=1.0, scale=-1.0, accum_out=T.r1[:, c:c + 1])
+        def pivot(c):
+            return T.tq[:, 16 * c + 15:16 * c + 16], "tq%d" % (c // 8 * 128)
 
         def compare(c):
-            ts(slot(c, 16 * c), bank(0, 0, 16 * c), T.tq[:, 16 * c + 15:16 * c + 16], None, A.is_ge, None, ["P0", "tq"], ["m%d" % c])
+            ts(slot(c, 16 * c), bank(0, 0, 16 * c), pivot(c)[0], None, A.is_ge, None, ["P0", pivot(c)[1]], ["m%d" % c])
 
         def rowsum(c):
-            act(T.junk[:, 8 * c * (c - 1):8 * c * (c + 1)], slot(c, 16 * c), AF.Copy, ["m%d" % c], ["r%d" % c], accum_out=T.r1[:, c:c + 1])
+            if c > OPT["nred"]:
+                act(T.junk[:, 8 * c * (c - 1):8 * c * (c + 1)], slot(c, 16 * c), AF.Copy, ["m%d" % c], ["r%d" % c], accum_out=T.r1[:, c:c + 1])
+            else:
+                red(T.r1[:, c:c + 1], slot(c, 16 * c), ["m%d" % c], ["r%d" % c])
 
         def packed(k0, k1):
             a, b = MO[k0], MO[k1] + MW[k1]
             quant(T.mq[:, a:b], T.ms[:, a:b], T.mt[:, 4 * a:4 * b], sum([blocks(k) for k in range(k0, k1 + 1)], []),
                   ["mq%d" % k for k in range(k0, k1 + 1)])
+            for k in range(k0, k1 + 1):
+                a, b = MO[k], MO[k] + MW[k]
+                mm(2, MW[k], T.oq[:], T.osb[:], T.mq[:, a:b], T.ms[:, a:b], ["oq", "mq%d" % k], k == 0, k == 3)
 
-        def colsum(k):
-            a, b = MO[k], MO[k] + MW[k]
-            mm(2, MW[k], T.oq[:], T.osb[:], T.mq[:, a:b], T.ms[:, a:b], ["oq", "mq%d" % k], k == 0, k == 3)
-
-        tt(slot(0, C), bank(0, 0, C), T.tq[:], A.is_gt, ["P0", "tq"], ["m0"])
-        for c in range(12, 8, -1):
-            compare(c)
-        scan(T.dsc[:], T.keep[:], slot(0, C), A.mult, A.add, ["keep", "m0"], ["dsc"])
-        packed(1, 1)
-        for c in range(8, 0, -1):
+        for k, c in enumerate(both):
+            sg = T.sg[:, 256 * k:256 * k + 16 * c]
+            act(sg, bank(1, 0, 16 * c), AF.Sign, ["P1", pivot(c)[1]], ["sg%d" % k], bias=pivot(c)[0], scale=-1.0)
+        for k, c in enumerate(both):
+            sg = T.sg[:, 256 * k:256 * k + 16 * c]
+            act(slot(c, 16 * c), sg, AF.Sign, ["sg%d" % k], ["m%d" % c, "r%d" % c], bias=1.0, scale=-1.0, accum_out=T.r1[:, c:c + 1])
+        compare(rest[0])
+        tt(slot(0, C), bank(0, 0, C), T.tq[:], A.is_gt, ["P0", "tq0", "tq128"], ["m0"])
+        for c in rest[1:]:
             compare(c)
         packed(0, 0)
-        packed(2, 3)
-        for k in range(4):
-            colsum(k)
-        for c in range(12, 3, -1):
+        for c in range(8, 0, -1):
+            compare(c)
+        scan(T.dsc[:], T.keep[:], slot(0, C), A.mult, A.add, ["keep", "m0"], ["dsc"])
+        packed(1, 2)
+        packed(3, 3)
+        for c in rest + list(range(8, 0, -1)):
             rowsum(c)
-        for c in range(3, 0, -1):
-            red(T.r1[:, c:c + 1], slot(c, 16 * c), ["m%d" % c], ["r%d" % c])
-        for k in range(2):
-            tt(T.u1[:, 16 * k:16 * k + 16], T.k0[:, 16 * k:16 * k + 16], T.dsc[:, 15:256:16], A.subtract,
-               ["k0a", "k0b", "dsc"], ["u1%d" % k])
-        tt(T.cm[:], bank(2, 0, C), T.diag[:], A.mult, ["P2", "diag"], ["cm"])
-        scan(T.csc[:], T.keep[:], T.cm[:], A.mult, A.add, ["keep", "cm"], ["csc"])
-        for k in range(2):
-            tt(T.u2[:, 16 * k:16 * k + 16], T.u1[:, 16 * k:16 * k + 16], T.r1[:], A.subtract,
-               ["u1%d" % k] + ["r%d" % c for c in range(16)], ["u2%d" % k])
-        for k in range(2):
-            tt(T.i32[:, 16 * k:16 * k + 16], T.u2[:, 16 * k:16 * k + 16], T.csc[:, 15:256:16], A.add,
-               ["u2%d" % k, "csc"], ["i32%d" % k])
-        tr(T.o32[:], T.i32[:], ["i320", "i321"], ["o32"])
-        tt(T.rk[:], T.o32[:, 0:16], T.o32[:, 16:32], A.min, ["o32"], ["rk"])
-        gm, gl = T.gm[:, 16 * rnd:16 * rnd + 16], T.gl[:, 16 * rnd:16 * rnd + 16]
-        G = "gm%d" % rnd
-        ts(gm, T.rk[:], 1.0 / 128, M0, A.mult, A.add, ["rk"], [G])
-        op("g", lambda gm=gm, gl=gl, rnd=rnd, pid=pid, rid=rid, m=maskof(eng):
-           g.remote_dma(gl, gm, T.sem["af%d" % rnd], T.sem.gone, pid, rid, m), [G], [])
-        gone[0] += len(eng)
-
         if rnd == 0:
-            later_constants()
+            middle_constants()
+        ua, ub, rk = T.ua[:, 0:16], T.ua[:, 16:32], T.ua[:, 32:48]
+        tt(ua, T.dsc[:, 15:C:16], T.k0[:], A.subtract, ["dsc", "k0"], ["ua"])
+        scan(T.csc[:], T.drop[:], bank(2, 0, C), A.add, A.min, ["drop", "P2"], ["csc"])
+        tt(ub, ua, T.r1[:], A.add, ["ua"] + ["r%d" % c for c in range(16)], ["ub"])
+        tt(rk, T.csc[:, 15:C:16], ub, A.subtract, ["csc", "ub"], ["rk"])
+        for k in range(2):
+            ts(T.i32[:, 16 * k:16 * k + 16], rk, scale[k], shift[k], A.mult, A.add, ["rk", "pf6", "pf7", "pf8", "pf9"], ["i32%d" % k])
+        tr(T.o32[:], T.i32[:], ["i320", "i321"], ["o32"])
+        gm, gb, gl = T.gm[:, 32 * rnd + 8:32 * rnd + 24], T.gm[:, 32 * rnd + 7:32 * rnd + 23], T.gl[:, 32 * rnd:32 * rnd + 16]
+        G = "gm%d" % rnd
+        tt(gm, T.o32[:, 0:16], T.o32[:, 16:32], A.add, ["o32"], [G])
+        send(gl, gm, "af%d" % rnd, [G])
+
         tb = [7, 1, 0, 2]
         for b in range(4):
-            mm(tb[b], C, T.eq[:, 128 * b:128 * b + 128], T.es[:, 128 * b:128 * b + 128], pq[:], pz[:], ["eq%d" % b],
-               ext=[("aq%d" % rnd, nq)] if b == 0 else [])
+            unpack(tb[b], b, pq[:], pz[:], [], ext=[("aq%d" % rnd, 2 * len(eng))] if b == 0 else [])
         for b in range(4):
-            own_copy(b)
+            if b < 4 - OPT["tpv"]:
+                act(T.tp[:, b:1024:4], bank(tb[b], 0, C), AF.Copy, ["P%d" % tb[b]], ["tp%d" % b], scale=-1.0)
+            else:
+                ts(T.tp[:, b:1024:4], bank(tb[b], 0, C), -1.0, None, A.mult, None, ["P%d" % tb[b]], ["tp%d" % b])
         for b in range(4):
-            act(T.tp[:, C * b:C * b + C], bank(tb[b], 0, C), AF.Copy, ["P%d" % tb[b]], ["tp%d" % b])
+            unpack(tb[b], b, xq[:], xs[:], [X], True, False)
+        for b in range(4):
+            act(T.win[:, WN * b + SH:WN * b + WN], bank(3 + b, 0, C), AF.Copy, ["P%d" % (3 + b)], ["wt%d" % b], scale=64.0)
+        if rnd == 0:
+            later_constants()
         o = T.own
-        of = o[:, 128:129]
-        scan(o[:, 0:16], gm, T.cidx[:, 32:48], A.add, A.add, [G, "negm"], ["cfl"])
-        fill(T.ln[:, 0:2 * C], 0.0, ["ln"])
-        ts(o[:, 64:96], T.m32[:, 0:32], o[:, 15:16], None, A.mult, None, ["lt", "cfl"], ["fx"])
+        kb, dk, thr, tot, of = o[:, 1:17], o[:, 32:49], o[:, 64:80], o[:, 80:81], o[:, 81:82]
+        red(tot, gm, [G], ["tot"])
+        ts(kb, gm, 1.5 * ETA, 511 * ETA, A.is_gt, A.mult, [G], ["kb"])
+        ts(o[:, 96:128], lt, tot, None, A.mult, None, ["lt", "tot"], ["fx"])
+        tt(kb, kb, ieta, A.max, ["kb", "ieta"], ["kb"])
+        tr(o[:, 128:160], o[:, 96:128], ["fx"], ["fxt"])
+        tt(dk, o[:, 1:18], o[:, 0:17], A.subtract, ["kb"], ["dk"])
+        red(of, o[:, 128:160], ["fxt"], ["of"])
+        ts(thr, gm, 0.5 * ETA, 0.5 * ETA, A.is_lt, A.max, [G], ["thr"])
+        fill(T.ln[:, 2 * C:3 * C], 512.0, ["ln"])
         fill(T.le[:, 128:SH], 256.0, ["le"])
-        tr(o[:, 96:128], o[:, 64:96], ["fx"], ["fxt"])
+        if rnd == 0:
+            last_constants()
         if rnd == 1:
             quant(T.vq[:], T.vs[:], T.vt[:], ["vt"], ["vq"])
-        red(of, o[:, 96:128], ["fxt"], ["of"])
+        quant(T.fq[:], T.fs[:], T.tp[:], ["tp0", "tp1", "tp2", "tp3"], ["fq"])
+        for b in range(4):
+            unpack(tb[b], b, T.fq[:], T.fs[:], ["fq"], False, True)
+        for b in range(4):
+            act(T.zf[:, C * b:C * b + C], bank(tb[b], 0, C), AF.Copy, ["P%d" % tb[b]], ["zf%d" % b])
 
-        w = T.w
-        mm_, hh, cs, pen = w[:, 212:228], w[:, 20:36], w[:, 52:68], w[:, 68:84]
-        oh, om, mt_, sc = w[:, 84:85], w[:, 85:86], w[:, 86:87], w[:, 87:88]
-        cml, res, crx, sb_, pr = w[:, 160:176], w[:, 1:17], w[:, 180:196], w[:, 196:212], w[:, 384:400]
+        w, mx = T.w, T.mx
+        mm_, hh = w[:, 1:17], w[:, 32:48]
+        p1, ck, t1, nq, p2 = w[:, 64:81], w[:, 96:113], w[:, 128:144], w[:, 144:160], w[:, 160:176]
+        oh, om, sc, mtot = mx[:, 287:288], mx[:, 319:320], mx[:, 351:352], mx[:, 383:384]
         tt(mm_, gm, gl, A.min, [G], ["mm"], ext=[("af%d" % rnd, len(eng))])
-        ts(hh, mm_, M0, None, A.is_gt, None, ["mm"], ["hh"])
-        ts(pen, mm_, M0, FAR, A.is_le, A.mult, ["mm"], ["pen"])
-        scan(cs, hh, hh, A.add, A.max, ["hh"], ["cs"])
-        tt(pen, pen, T.cidx[:, 0:16], A.min, ["pen", "cidx"], ["pen"])
-        ts(w[:, 96:128], T.m32[:, 0:32], w[:, 67:68], None, A.mult, None, ["lt", "cs"], ["hx"])
-        tt(pen, pen, cs, A.add, ["pen", "cs"], ["pen"])
-        at = len(ops)
-        tr(w[:, 128:160], w[:, 96:128], ["hx"], ["hxt"])
-        red(oh, w[:, 128:160], ["hxt"], ["oh"])
-        ts(T.offe[:], pen, oh, -1.0, A.add, A.add, ["pen", "oh"], ["offe"])
-        cp(T.le[:].indirect(T.offe[:]), T.src[:], ["offe", "src"], ["le"])
-        scan(T.lek[:], T.hold[:, 0:SH], T.le[:, 0:SH], A.add, A.min, ["hold0", "le"], ["lek"])
+        tt(hh, gl, thr, A.is_gt, ["thr"], ["hh"])
+        scan(p1, dk, w[:, 1:18], A.add, A.add, ["dk", "mm"], ["p1"])
+        scan(ck, step, w[:, 32:49], A.add, A.add, ["step", "step2", "hh", "pf10"], ["ck"], first)
+        ts(mx[:, 32:128], T.m32[:], w[:, 80:81], None, A.mult, None, ["lt", "sl", "same", "p1"], ["mx1"])
+        ts(mx[:, 0:32], lt, w[:, 112:113], None, A.mult, None, ["lt", "ck"], ["mx0"])
+        tt(t1, hh, negk, A.mult, ["hh", "negk"], ["t1"])
+        tr(mx[:, 128:256], mx[:, 0:128], ["mx0", "mx1"], ["mxt"])
+        tt(t1, t1, w[:, 96:112], A.add, ["t1", "ck"], ["t1"])
+        scan(mx[:, 256:384], T.k32[:], mx[:, 128:256], A.mult, A.add, ["k32", "mxt"], ["sums"])
+        scan(p2, gb, w[:, 0:16], A.add, A.subtract, [G, "mm", "of"], ["p2"], of)
+        ts(T.offe[:], t1, oh, -2.0, A.add, A.add, ["t1", "sums"], ["offe"])
+        tt(nq, gl, gm, A.is_ge, [G], ["nq"])
+        cp(T.le[:].indirect(T.offe[:]), T.up[:], ["offe", "up"], ["le"])
+        act(T.ks[:, 0:C], T.slot[:], AF.Relu, ["slot", "sums"], ["anew"], scale=-4096.0, bias=mtot)
+        tt(p2, p2, nq, A.subtract, ["p2", "nq"], ["p2"])
+        scan(T.lek[:], T.hold[:, 0:SH], T.le[:, 0:SH], A.add, A.min, ["hold", "le"], ["lek"])
+        ts(p2, p2, sc, 512 * ETA, A.add, A.add, ["p2", "sums"], ["p2"])
         ts(T.el[:], T.lek[:, 15:SH:16], -1.0, None, A.add, None, ["lek"], ["el"])
-        list_e = taken(at)
-
-        scan(cml, mm_, T.cidx[:, 32:48], A.add, A.add, ["mm", "negm"], ["cml"])
-        ts(w[:, 256:320], T.m32[:], w[:, 175:176], None, A.mult, None, ["lt", "same", "cml"], ["mx"])
-        tr(w[:, 320:384], w[:, 256:320], ["mx"], ["mxt"])
-        red(om, w[:, 320:352], ["mxt"], ["om"])
-        red(mt_, w[:, 352:384], ["mxt"], ["mtot"])
-        tt(res, gm, mm_, A.subtract, [G, "mm"], ["res"])
-        weave(list_e, taken(at))
-        ts(sc, om, -2.0, mt_, A.mult, A.add, ["om", "mtot"], ["sc"])
-        ts(pr, res, 0.0, FAR, A.is_le, A.mult, ["res"], ["pr"])
-        ts(sc, sc, of, -255.0, A.add, A.add, ["sc", "of"], ["sc"])
-        tt(pr, pr, T.cidx[:, 0:16], A.min, ["pr", "cidx"], ["pr"])
-        scan(crx, w[:, 0:16], T.cidx[:, 52:68], A.add, A.add, ["res", "w0", "zero", "sc"], ["crx"], sc)
-        ts(sb_, mm_, M0 + 2, FAR, A.is_lt, A.mult, ["mm"], ["sb"])
-        tt(pr, pr, crx, A.add, ["crx", "pr"], ["pr"])
-        tt(sb_, cml, sb_, A.add, ["cml", "sb"], ["sb"])
-        tt(pr, pr, sb_, A.min, ["pr", "sb"], ["pr"])
-        ts(T.offn[:], pr, om, 255.0, A.add, A.add, ["pr", "om"], ["offn"])
+        tt(p2, p2, w[:, 64:80], A.max, ["p2", "p1"], ["p2"])
+        ts(T.offn[:], p2, om, 1.0 / ETA, A.add, A.mult, ["p2", "sums"], ["offn"])
 
         for b in range(4):
-            act(T.ft[:, b:512:4], T.tp[:, C * b:C * b + C].indirect(T.el[:, 0:8]), AF.Copy, ["tp%d" % b, "el"], ["ft%d" % b])
+            act(T.zt[:, b:512:4], T.zf[:, C * b:C * b + C].indirect(T.el[:, 0:8]), AF.Copy, ["zf%d" % b, "el"], ["zt%d" % b])
         for b in range(4):
-            act(T.fp[:, SH * b:SH * b + SH], T.win[:, WN * b:WN * b + C].indirect(T.el[:]), AF.Copy,
-                ["wt%d" % b, "el"], ["fp%d" % b], scale=1.0 / 64)
-        for b in range(4):
-            act(T.win[:, WN * b + C + 1:WN * b + WN:2], T.fp[:, SH * b:SH * b + SH], AF.Copy, ["fp%d" % b], ["wo%d" % b], scale=64.0)
-            act(T.win[:, WN * b + 2 * C:WN * b + WN:2], T.fp[:, SH * b + 128:SH * b + SH], AF.Copy, ["fp%d" % b], ["we%d" % b], scale=64.0)
-        quant(T.fq[:], T.fs[:], T.ft[:], ["ft0", "ft1", "ft2", "ft3"], ["fq"])
-        for b in range(4):
-            mm(3 + b, 128, T.eq[:, 128 * b:128 * b + 128], T.es[:, 128 * b:128 * b + 128], T.fq[:], T.fs[:], ["eq%d" % b, "fq"])
-        cp(T.ln[:].indirect(T.offn[:]), T.src[:], ["offn", "src"], ["ln"])
-        ts(T.fl[:, 1:C + 1], T.ln[:, C:2 * C], 0.0, None, A.is_gt, None, ["ln"], ["fl"])
-        scan(T.ks[:, 0:C], T.ln[:, 0:C], T.ln[:, 0:C], A.max, A.max, ["ln"], ["ks0"])
-
-        for b in range(4):
-            tt(T.zt[:, b:512:4], T.fp[:, SH * b:SH * b + 128], bank(3 + b, 0, 128), A.subtract,
-               ["fp%d" % b, "P%d" % (3 + b)], ["zt%d" % b])
-        scan(T.ks[:, C:2 * C], T.fl[:, 1:C + 1], T.fl[:, 0:C], A.add, A.add, ["fl", "fl0"], ["ks1"])
+            act(T.win[:, WN * b:WN * b + SH], T.win[:, WN * b + SH:WN * b + WN].indirect(T.el[:]), AF.Copy,
+                ["wt%d" % b, "el"], ["wf%d" % b])
+        cp(T.ln[:].indirect(T.offn[:]), T.down[:], ["offn", "down"], ["ln"])
         quant(T.zq[:], T.zs[:], T.zt[:], ["zt0", "zt1", "zt2", "zt3"], ["zq"])
         for b in range(4):
-            mm(tb[b], 128, T.wq[:, 128 * b:128 * b + 128], T.wsc[:, 128 * b:128 * b + 128], T.zq[:], T.zs[:], ["wq", "wsc", "zq"])
+            mm(3 + b, 128, T.wq[:, 128 * b:128 * b + 128], T.wsc[:, 128 * b:128 * b + 128], T.zq[:], T.zs[:], ["wq", "wsc", "zq"])
 
-        def made(k):
-            tt(T.win[:, WN * k + C:WN * k + 2 * C:2], bank(tb[k], 0, 128), T.win[:, WN * k + C + 1:WN * k + 2 * C:2], A.add,
-               ["P%d" % tb[k], "wo%d" % k], ["wg%d" % k])
+        got, free, held, cnt, cx = T.ln[:, 2 * C:3 * C], T.ks[:, C:2 * C], T.ks[:, 2 * C:3 * C], T.ks[:, 3 * C:4 * C], T.ks[:, 4 * C:5 * C]
+        z = w[:, 192:208]
 
-        scan(T.kw[:], T.hold[:], T.ks[:], A.add, A.min, ["hold0", "hold1", "ks0", "ks1"], ["kw"])
-        lw, kw = T.kw[:, 15:C:16], T.kw[:, C + 15:2 * C:16]
-        q2, z2 = w[:, 432:448], w[:, 464:480]
-        ts(q2, lw, 0.0, FAR, A.is_le, A.mult, ["kw"], ["q2"])
-        tt(z2, T.cidx[:, 16:32], kw, A.subtract, ["kw", "cidx2"], ["z2"])
-        tt(q2, q2, lw, A.add, ["kw", "q2"], ["q2"])
+        def made(b):
+            tt(T.win[:, WN * b:WN * b + 128], bank(3 + b, 0, 128), T.win[:, WN * b:WN * b + 128], A.add,
+               ["P%d" % (3 + b), "wf%d" % b], ["wf%d" % b])
+
+        ts(free, got, 300.0, None, A.is_gt, None, ["ln"], ["free"])
+        scan(held, T.ks[:, 0:C], got, A.add, A.min, ["anew", "ln"], ["held"])
+        scan(cnt, free, free, A.add, A.max, ["free"], ["cnt"])
+        scan(T.ux[:], T.drop[:], held, A.add, A.min, ["drop", "held"], ["ux"])
+        scan(cx, T.hold[:], cnt, A.add, A.min, ["hold", "cnt"], ["cx"])
+        ts(z, T.ux[:, 15:C:16], -1.0, ubias, A.mult, A.add, ["ux", "pf11"], ["z"])
         made(0)
-        tt(z2, z2, q2, A.min, ["z2", "q2"], ["z2"])
+        tt(z, z, T.ks[:, 4 * C + 15:5 * C:16], A.max, ["z", "cx"], ["z"])
         made(1)
-        ts(T.nlist[:], z2, -1.0, None, A.add, None, ["z2"], ["nlist"])
+        ts(T.nlist[:], z, -1.0, None, A.add, None, ["z"], ["nlist"])
         made(2)
         made(3)
 
         def part(b):
-            return ["wt%d" % b, "wg%d" % b, "wo%d" % b, "we%d" % b, "nlist"]
+            return ["wt%d" % b, "wf%d" % b, "nlist"]
 
+        vs = OPT["vsplit"]
         for b in (0, 1):
             act(T.xt[:, b:1024:4], T.win[:, WN * b:WN * b + WN].indirect(T.nlist[:]), AF.Copy, part(b), ["xt%d" % b], scale=1.0 / 64)
-        act(T.xt[:, 2:128:4], T.win[:, WN * 2:WN * 3].indirect(T.nlist[:, 0:2]), AF.Copy, part(2), ["xt4"], scale=1.0 / 64)
-        ts(T.xt[:, 130:1024:4], T.win[:, WN * 2:WN * 3].indirect(T.nlist[:, 2:16]), 1.0 / 64, None, A.mult, None, part(2), ["xt2"])
+        if vs:
+            act(T.xt[:, 2:64 * vs:4], T.win[:, WN * 2:WN * 3].indirect(T.nlist[:, 0:vs]), AF.Copy, part(2), ["xt4"], scale=1.0 / 64)
+        ts(T.xt[:, 64 * vs + 2:1024:4], T.win[:, WN * 2:WN * 3].indirect(T.nlist[:, vs:16]), 1.0 / 64, None, A.mult, None, part(2), ["xt2"])
         ts(T.xt[:, 3:1024:4], T.win[:, WN * 3:WN * 4].indirect(T.nlist[:]), 1.0 / 64, None, A.mult, None, part(3), ["xt3"])
         quant(T["xq%d" % (rnd + 1)][:], T["xs%d" % (rnd + 1)][:], T.xt[:], ["xt0", "xt1", "xt2", "xt3", "xt4"], ["xq%d" % (rnd + 1)])
         if rnd == 2:
-            for k in range(2):
-                ts(T.idw[:, C + k:WN:2], T.le[:, 0:SH], -1.0, None, A.add, None, ["le"], ["id%d" % (k + 1)])
+            ts(T.idw[:, 0:SH], T.le[:, 0:SH], -1.0, None, A.add, None, ["le"], ["id1"])
 
     mm(3, C, T.vq[:], T.vs[:], T.xq3[:], T.xs3[:], ["vq", "xq3"])
     dma("s", T.oc[:], T.xq3[:].bitcast(dt.uint8), ["xq3"], [])
-    cp(T.nlo[:], T.idw[:].indirect(T.nlist[:]), ["id0", "id1", "id2", "nlist"], ["nlo"])
+    cp(T.nlo[:], T.idw[:].indirect(T.nlist[:]), ["id0", "id1", "nlist"], ["nlo"])
     act(T.yo[:], bank(3, 0, C), AF.Copy, ["P3"], ["yo"])
     dma("a", T.y[:], T.yo[:], ["yo"], [])
     for k in range(4):

@@ -1,16 +1,16 @@
-from concourse.bass import DstId, RemoteDMATransfer
 from concourse.mybir import dt, AluOpType, AxisListType, ActivationFunctionType
 
 A = AluOpType
 AF = ActivationFunctionType
 C = 256
 SH = 192
-WN = SH + C
+ZO, TO, WN = 384, 640, 896
 STEPS = [1, 2, 4]
 BIG = 2.0 ** 88
-ETA = 2.0 ** -10
+ETA = 2.0 ** -16
+GAP = 191
 CODE = "float8_e4m3fn_x4"
-OPT = dict(nss=3, nred=8, vsplit=2, tpv=0)
+OPT = dict(lastq=2, order="c12 c11 m c10 c9 c8 q00 c7 c6 c5 c4 c3 c2 c1 s q33 q12 d r11 r10 r9 l0 l1 l2 l3", nss=3, c0=9, vsplit=2, tfirst=1, thr="v", k1="v", tot="v", fx="v", of="v", cut=192, tail=1, padv=(0, 2), small=2)
 
 
 def sb(n, d):
@@ -26,23 +26,21 @@ SCRATCH = {
     "eq": sb(512, CODE), "es": sb(512, "uint8"), "oq": sb(128, CODE), "osb": sb(128, "uint8"),
     "mq": sb(768, CODE), "ms": sb(768, "uint8"), "mt": sb(4 * 768, "bfloat16"),
     "fq": sb(256, CODE), "fs": sb(256, "uint8"), "zq": sb(128, CODE), "zs": sb(128, "uint8"),
-    "zt": sb(512, "bfloat16"), "zf": sb(1024, "bfloat16"),
-    "win": sb(4 * WN, "bfloat16"), "tp": sb(1024, "bfloat16"), "idw": sb(WN, "float32"),
+    "zt": sb(512, "bfloat16"), "win": sb(4 * WN, "bfloat16"), "tp": sb(1024, "bfloat16"), "idw": sb(WN, "float32"),
     "et": sb(528, "bfloat16"), "ot": sb(512, "bfloat16"), "one": sb(128, "bfloat16"),
     "pi": sb(4, "int32"), "pf": sb(16, "float32"),
-    "yy": sb(256, "bfloat16"), "g16": sb(128, "bfloat16"), "up": sb(256, "bfloat16"), "down": sb(256, "bfloat16"),
-    "slot": sb(256, "bfloat16"),
-    "bigm": sb(256, "float32"), "kres": sb(256, "float32"),
-    "keep": sb(256, "bfloat16"), "hold": sb(256, "bfloat16"), "drop": sb(256, "bfloat16"),
-    "m32": sb(96, "bfloat16"), "k32": sb(128, "bfloat16"),
-    "k0": sb(16, "float32"), "cidx": sb(64, "float32"), "uoff": sb(8, "uint16"),
-    "m1": sb(256, "float32"), "tq": sb(256, "float32"), "sg": sb(1024, "bfloat16"), "junk": sb(2048, "bfloat16"),
-    "r1": sb(16, "float32"), "dsc": sb(256, "bfloat16"), "csc": sb(256, "float32"),
-    "ua": sb(48, "float32"), "i32": sb(32, "bfloat16"), "o32": sb(32, "bfloat16"),
+    "yy": sb(256, "bfloat16"), "g16": sb(128, "bfloat16"), "up": sb(256, "bfloat16"),
+    "bigm": sb(256, "float32"), "hold": sb(256, "bfloat16"), "drop": sb(256, "bfloat16"),
+    "kd": sb(256, "bfloat16"), "k2": sb(256, "bfloat16"),
+    "m32": sb(96, "bfloat16"), "k32": sb(96, "bfloat16"),
+    "cidx": sb(96, "float32"), "uoff": sb(8, "uint16"),
+    "m1": sb(256, "float32"), "tq": sb(256, "float32"), "sg": sb(1280, "bfloat16"), "junk": sb(1024, "bfloat16"),
+    "r1": sb(16, "float32"), "rs": sb(2944, "bfloat16"), "dsc": sb(256, "bfloat16"), "csc": sb(256, "float32"),
+    "ua": sb(32, "float32"), "i32": sb(32, "bfloat16"), "o32": sb(32, "bfloat16"),
     "gm": sb(96, "bfloat16"), "gl": sb(96, "bfloat16"),
-    "own": sb(192, "float32"), "w": sb(256, "float32"), "mx": sb(384, "bfloat16"),
+    "own": sb(192, "float32"), "w": sb(192, "float32"), "mx": sb(288, "bfloat16"),
     "offe": sb(16, "uint16"), "le": sb(768, "bfloat16"), "lek": sb(SH, "bfloat16"), "el": sb(12, "uint16"),
-    "offn": sb(16, "uint16"), "ln": sb(768, "bfloat16"), "ks": sb(5 * C, "bfloat16"), "ux": sb(C, "float32"),
+    "offn": sb(16, "uint16"), "ln": sb(1024, "bfloat16"), "un": sb(272, "bfloat16"), "ks": sb(3 * C, "float16"),
     "nlist": sb(16, "uint16"),
     "nlo": sb(256, "float32"), "yo": sb(256, "float32"),
     "ps": ("psum", [128, 4096], "float32"),
@@ -94,7 +92,7 @@ def emit(g, T, ops):
                 known[q] |= closure[k]
                 needed.add(k)
         waits.append(mine)
-        if op[5] or q == "g":
+        if op[5] == "dma" or op[5] == "far":
             closure.append(known[q] | 1 << n)
         else:
             issued[q] |= 1 << n
@@ -107,7 +105,7 @@ def emit(g, T, ops):
         for s, val in ext:
             queue[q].wait_ge(T.sem[s], val)
         ins = fn()
-        if dma:
+        if dma == "dma":
             mark[n] = (T.sem["d%d" % ndma], 16)
             ndma += 1
             ins.then_inc(*mark[n])
@@ -130,7 +128,7 @@ def rank_program(g, core, T, topo):
     V, S, PE = g.vector, g.scalar, g.tensor
     ops = []
 
-    def op(q, fn, rd, wr, ext=(), dma=False):
+    def op(q, fn, rd, wr, ext=(), dma=""):
         ops.append((q, fn, list(rd), list(wr), list(ext), dma))
 
     def ts(out, in0, s1, s2, o0, o1, rd, wr, ext=()):
@@ -151,9 +149,6 @@ def rank_program(g, core, T, topo):
     def tr(out, a, rd, wr):
         op("v", lambda: V.transpose(out, a), rd, wr)
 
-    def red(out, a, rd, wr):
-        op("v", lambda: V.tensor_reduce(out, a, AxisListType.X, A.add), rd, wr)
-
     def fill(ap, val, wr):
         op("v", lambda: V.memset(ap, val), [], wr)
 
@@ -162,6 +157,18 @@ def rank_program(g, core, T, topo):
 
     def act(out, a, fn, rd, wr, **kw):
         op("a", lambda: S.activation(out, a, fn, **kw), rd, wr)
+
+    def lin(q, out, a, scale, bias, rd, wr):
+        if q == "a":
+            act(out, a, AF.Identity, rd, wr, scale=scale, bias=bias)
+        else:
+            ts(out, a, scale, bias, A.mult, A.add, rd, wr)
+
+    def total(q, out, a, spare, rd, wr):
+        if q == "a":
+            act(spare, a, AF.Copy, rd, wr + ["spare"], accum_out=out)
+        else:
+            op("v", lambda: V.tensor_reduce(out, a, AxisListType.X, A.add), rd, wr)
 
     def mm(bank, n, lq, ls, rq, rs, rd, start=True, stop=True, ext=()):
         op("p", lambda: PE.matmul_mx(T.ps[:, 512 * bank:512 * bank + n], lq, ls, rq, rs, start, stop),
@@ -175,7 +182,7 @@ def rank_program(g, core, T, topo):
 
     def dma(q, out, a, rd, wr):
         eng = {"s": g.sync, "a": g.scalar, "g": g}[q]
-        op(q, lambda: eng.dma_start(out, a), rd, wr, (), True)
+        op(q, lambda: eng.dma_start(out, a), rd, wr, (), "dma")
 
     def iota(out, pat, base, mult, wr, small=True):
         if small:
@@ -183,24 +190,34 @@ def rank_program(g, core, T, topo):
         else:
             op("g", lambda: g.iota(out, pat, base, mult), [], wr)
 
-    nss = OPT["nss"]
+    def win(b, a, e, step=1):
+        return T.win[:, WN * b + a:WN * b + e:step]
+
+    nss, c0, cut = OPT["nss"], OPT["c0"], OPT["cut"]
     both = list(range(15, 15 - nss, -1))
-    rest = [c for c in range(15, 8, -1) if c not in both]
-    lanes = [[0] + rest[:3], [8, 7, 6, 5], [4, 3, 2, 1], both + rest[3:]]
+    rest = [c for c in (12, 11, 10, 9) if c not in both]
+    lanes = [[0, 11, 10, 9], [1, 2, 3, 4], [5, 6, 7, 8], [15, 14, 13, 12]]
     MW = [256, 128, 128, 240]
     MO = [0, 256, 384, 512]
 
-    def slot(c, n, a=0):
+    def slot(c, n):
         k = [c in x for x in lanes].index(True)
         t = lanes[k].index(c)
-        return T.mt[:, 4 * (MO[k] + a) + t:4 * (MO[k] + n):4]
+        return T.mt[:, 4 * MO[k] + t:4 * (MO[k] + n):4]
 
     def blocks(k):
         return ["m%d" % c for c in lanes[k]]
 
     def pad(k):
         a = 16 * min(c if c else 16 for c in lanes[k])
-        fill(T.mt[:, 4 * (MO[k] + a):4 * (MO[k] + MW[k])], 0.0, blocks(k))
+        out = T.mt[:, 4 * (MO[k] + a):4 * (MO[k] + MW[k])]
+        if k in OPT["padv"]:
+            fill(out, 0.0, blocks(k))
+        else:
+            act(out, T.et[:, 0:4 * (MW[k] - a)], AF.Copy, ["et"], blocks(k), scale=0.0)
+
+    def summed(c):
+        return C + GAP * (c - 1)
 
     def maskof(es):
         return sum(1 << e for e in es)
@@ -217,74 +234,70 @@ def rank_program(g, core, T, topo):
     iota(T.yy[:], [[0, 16], [1, 16]], 0, 0, ["yy"])
     fill(T.one[:], 1.0, ["one"])
     fill(T.et[:], 0.0, ["et"])
-    iota(T.g16[:], [[16, 8], [0, 16]], 0, 0, ["g16"])
     op("g", lambda: g.affine_select(T.et[:, 3:515:4], T.one[:], [[-1, 128]], A.is_equal, 0.0, 0, 1), ["one"], ["et"])
+    iota(T.g16[:], [[16, 8], [0, 16]], 0, 0, ["g16"])
+    iota(T.kd[:], [[-16, 16], [4096, 16]], 0, 0, ["kd"])
     for k, bits in enumerate([15, 112, 16]):
         ts(T.pi[:, 1 + k:2 + k], T.pi[:, 0:1], bits, None, A.bitwise_and, None, ["pi0"], ["pi%d" % (k + 1)])
-    fill(T.r1[:, 0:1], 0.0, ["r0"])
+    fill(T.rs[:, summed(0):summed(0) + 1], 0.0, ["r0"])
     cp(T.pf[:, 0:3], T.pi[:, 1:4], ["pi1", "pi2", "pi3"], ["pf"])
     rr, gp, par = T.pf[:, 0:1], T.pf[:, 1:2], T.pf[:, 2:3]
 
-    def column(k, src, scale, bias):
-        ts(T.pf[:, k:k + 1], src, scale, bias, A.mult, A.add, ["pf"], ["pf%d" % k])
+    def column(q, k, src, scale, bias, rd=()):
+        lin(q, T.pf[:, k:k + 1], src, scale, bias, ["pf"] + list(rd), ["pf%d" % k])
         return T.pf[:, k:k + 1]
 
-    pad(0)
-    nbig = column(3, rr, -BIG, 0.0)
-    hbias = column(4, rr, 4096.0, 4096.0)
-    kbias = column(5, rr, -1025.0, 15375.5)
+    fill(T.gm[:], 0.0, ["gm0", "gm1", "gm2"])
+    nbig = column("v", 3, rr, -BIG, 0.0)
+    hbias = column("v", 4, rr, 64 * BIG, 64 * BIG)
     ts(T.uoff[:], T.yy[:, 0:8], 16.0, None, A.mult, None, ["yy"], ["uoff"])
     act(T.bigm[:], T.yy[:], AF.Abs, ["yy", "pf3"], ["bigm"], scale=BIG, bias=nbig)
-    act(T.kres[:], T.yy[:], AF.Relu, ["yy"], ["kres"], scale=-64 * BIG, bias=64 * BIG)
+    act(T.hold[:], T.yy[:], AF.Relu, ["yy", "pf4"], ["hold"], scale=-64 * BIG, bias=hbias)
+    pad(0)
+    pad(2)
+
+    def packed_unit(b):
+        quant(T.eq[:, 128 * b:128 * b + 128], T.es[:, 128 * b:128 * b + 128], T.et[:, 3 - b:515 - b], ["et"], ["eq%d" % b])
+
+    packed_unit(0)
     quant(T.uq[:], T.us[:], T.ut[:], ["ut"], ["uq"])
-    pad(1)
+    packed_unit(1)
     op("v", lambda: V.tensor_copy(T.uq2[:].bitcast(dt.uint32), T.uq[:].bitcast(dt.uint32).indirect(T.uoff[:])),
        ["uq", "uoff"], ["uq2"])
+    packed_unit(2)
+    packed_unit(3)
     act(T.us2[:], T.us[:].indirect(T.uoff[:]), AF.Copy, ["uq", "uoff"], ["us2"])
-    act(T.keep[:], T.yy[:], AF.Sign, ["yy"], ["keep"])
-    act(T.k0[:], T.yy[:, 0:16], AF.Identity, ["yy", "pf5"], ["k0"], scale=16.0, bias=kbias)
-    act(T.hold[:], T.yy[:], AF.Relu, ["yy", "pf4"], ["hold"], scale=-4096.0, bias=hbias)
-    act(T.drop[:], T.hold[:], AF.Identity, ["hold"], ["drop"], scale=16.0, bias=-1024.0)
+    pad(1)
+    pad(3)
+    act(T.drop[:], T.hold[:], AF.Identity, ["hold"], ["drop"], scale=2.0 ** -76, bias=-1024.0)
+    unit = ETA / 128
+    scale = [column("a", 6, par, -unit / 16, unit), column("a", 7, par, unit / 16, 0.0)]
+    column("a", 5, rr, -1025.0, 15375.5 + 32768)
+    shift = [column("a", 8 + k, T.pf[:, 5:6], scale[k], -128 * ETA, ["pf5", "pf%d" % (6 + k)]) for k in range(2)]
+    quant(T.xq0[:], T.xs0[:], T.xin[:], ["x0"], ["xq0"])
     for t in range(4):
         ts(T.ot[:, t:512:4], T.g16[:], gp, None, A.is_equal, None, ["g16", "pf"], ["ot%d" % t])
-    for b in range(4):
-        quant(T.eq[:, 128 * b:128 * b + 128], T.es[:, 128 * b:128 * b + 128], T.et[:, 3 - b:515 - b], ["et"], ["eq%d" % b])
-    quant(T.xq0[:], T.xs0[:], T.xin[:], ["x0"], ["xq0"])
     quant(T.oq[:], T.osb[:], T.ot[:], ["ot0", "ot1", "ot2", "ot3"], ["oq"])
-    pad(3)
-    pad(2)
-    scale = [T.pf[:, 6:7], T.pf[:, 7:8]]
-    shift = [T.pf[:, 8:9], T.pf[:, 9:10]]
 
-    def middle_constants():
-        column(6, par, -2.0 ** -21, 2.0 ** -17)
-        column(7, par, 2.0 ** -21, 0.0)
-        column(8, par, -1.0 / 64, 0.125)
-        column(9, par, 1.0 / 64, -0.125)
-        fill(T.gm[:], 0.0, ["gm0", "gm1", "gm2"])
-
-    lt, step, negk, ieta = T.m32[:, 0:32], T.cidx[:, 0:17], T.cidx[:, 32:48], T.cidx[:, 48:64]
-    first, ubias = T.pf[:, 10:11], T.pf[:, 11:12]
+    lt, same, negk, ieta = T.m32[:, 0:32], T.m32[:, 64:96], T.cidx[:, 48:64], T.cidx[:, 64:80]
 
     def later_constants():
-        ts(T.m32[:, 64:96], T.g16[:, 0:32], par, None, A.is_equal, None, ["g16", "pf"], ["same"])
-        ts(lt, T.yy[:, 0:32], rr, None, A.is_gt, None, ["yy", "pf"], ["lt"])
-        column(10, rr, 16.0, 255.0)
-        tt(lt, lt, T.m32[:, 64:96], A.mult, ["lt", "same"], ["lt"])
-        column(11, rr, 1024.0, WN + 1 - 15360.0)
-        fill(T.own[:, 0:18], 0.0, ["kb"])
-        ts(T.m32[:, 32:64], lt, -2.0, None, A.mult, None, ["lt"], ["sl"])
-        ts(negk, T.yy[:, 0:16], first, -1.0, A.add, A.mult, ["yy", "pf10"], ["negk"])
-        tt(T.m32[:, 32:64], T.m32[:, 32:64], T.m32[:, 64:96], A.add, ["sl", "same"], ["sl"])
-        ts(ieta, negk, 255.0, -ETA, A.add, A.mult, ["negk"], ["ieta"])
-        ts(T.m32[:, 64:96], T.m32[:, 64:96], 4096.0 / ETA, None, A.mult, None, ["same"], ["same"])
+        first = column("a", 10, rr, -16.0, -255.0)
+        lin("a", negk, T.yy[:, 0:16], -1.0, first, ["yy", "pf10"], ["negk"])
+        lin("a", ieta, negk, -ETA, -255 * ETA, ["negk"], ["ieta"])
+        lin("a", T.cidx[:, 17:18], rr, 16.0, 256.0, ["pf", "step"], ["step1"])
+        lin("a", T.cidx[:, 33:34], rr, -16.0, -271.0, ["pf", "step"], ["step2"])
+        act(T.k32[:], T.k32[:], AF.Sign, ["k32"], ["k32"])
 
-    def last_constants():
-        fill(T.cidx[:, 0:16], 1.0, ["step"])
-        ts(T.cidx[:, 16:17], rr, -16.0, -271.0, A.mult, A.add, ["pf"], ["step2"])
-        fill(T.k32[:], 1.0, ["k32"])
-        fill(T.w[:, 0:64], 0.0, ["mm", "hh"])
-        fill(T.k32[:, 0:128:32], 0.0, ["k32"])
+    masks = [lambda: ts(same, T.g16[:, 0:32], par, None, A.is_equal, None, ["g16", "pf"], ["same"]),
+             lambda: ts(lt, T.yy[:, 0:32], rr, None, A.is_gt, None, ["yy", "pf"], ["lt"]),
+             lambda: tt(lt, lt, same, A.mult, ["lt", "same"], ["lt"]),
+             lambda: lin("v", T.m32[:, 32:64], lt, -2.0, 0.0, ["lt"], ["sl"]),
+             lambda: tt(T.m32[:, 32:64], T.m32[:, 32:64], same, A.add, ["sl", "same"], ["sl"])]
+
+    def beside():
+        if masks:
+            masks.pop(0)()
 
     for rnd, h in enumerate(STEPS):
         mate = T.cores[rank ^ h]
@@ -292,40 +305,53 @@ def rank_program(g, core, T, topo):
         eng = topo.engines(core, mate)
         xq, xs, pq, pz = T["xq%d" % rnd], T["xs%d" % rnd], T["pq%d" % rnd], T["pz%d" % rnd]
         X = "xq%d" % rnd
+        last = rnd == len(STEPS) - 1
 
         def send(out, a, sem, rd, pid=pid, rid=rid, eng=eng):
-            op("g", lambda: g.remote_dma(out, a, T.sem[sem], T.sem.gone, pid, rid, maskof(eng)), rd, [])
+            op("g", lambda: g.remote_dma(out, a, T.sem[sem], T.sem.gone, pid, rid, maskof(eng)), rd, [], (), "far")
             gone[0] += len(eng)
 
         send(pq[:].bitcast(dt.uint8), xq[:].bitcast(dt.uint8), "aq%d" % rnd, [X])
         send(pz[:], xs[:], "aq%d" % rnd, [X])
         if rnd == 0:
-            iota(T.up[:], [[1, 16], [16, 16]], 1, 0, ["up"])
-            iota(T.down[:], [[-1, 16], [-16, 16]], C, 0, ["down"])
-            iota(T.slot[:], [[1, C]], -1, 0, ["slot"])
-        if rnd == 2:
-            iota(T.idw[:, SH:WN], [[1, C]], 0, 0, ["id0"])
+            iota(T.k2[:, 0:128], [[-4096, 128]], 127 * 4096, 0, ["k2a"])
+            iota(T.k2[:, 128:256], [[0, 128]], 4096, 0, ["k2b"])
+            iota(T.cidx[:, 17:34], [[0, 17]], 1, 0, ["step"])
+            iota(T.k32[:], [[0, 3], [1, 32]], 0, 0, ["k32"])
+            iota(T.own[:, 0:18], [[0, 18]], 0, 0, ["kb"])
+            iota(T.w[:, 0:36], [[0, 36]], 0, 0, ["mm", "hh"])
+            iota(T.un[:, 0:1], [[0, 1]], 1, 0, ["un0"])
+        iota(T.le[:, 128:SH], [[0, SH - 128]], C, 0, ["le"])
+        if rnd > 0:
+            iota(T.ln[:, 2 * C:4 * C], [[0, 2 * C]], -1024, 0, ["ln"])
+        if last:
+            iota(T.idw[:, ZO:WN], [[1, WN - ZO]], ZO - TO, 0, ["id0"])
 
         mm(0, C, T.uq2[:], T.us2[:], xq[:], xs[:], ["uq2", "us2", X])
         mm(1, C, T.uq2[:], T.us2[:], xq[:], xs[:], ["uq2", "us2", X])
         for b in range(4):
             unpack(3 + b, b, xq[:], xs[:], [X])
-        for a in (128, 0):
-            tt(T.m1[:, a:a + 128], bank(0, a, a + 128), T.bigm[:, a:a + 128], A.add, ["P0", "bigm"], ["m1%d" % a])
-        for a in (128, 0):
-            scan(T.tq[:, a:a + 128], T.kres[:, a:a + 128], T.m1[:, a:a + 128], A.add, A.min, ["kres", "m1%d" % a], ["tq%d" % a])
+        halves = [(cut, C), (0, cut)]
+        for a, e in halves:
+            tt(T.m1[:, a:e], bank(0, a, e), T.bigm[:, a:e], A.add, ["P0", "bigm"], ["m1%d" % a])
+        for a, e in halves:
+            scan(T.tq[:, a:e], T.hold[:, a:e], T.m1[:, a:e], A.add, A.min, ["hold", "m1%d" % a], ["tq%d" % a])
 
         def pivot(c):
-            return T.tq[:, 16 * c + 15:16 * c + 16], "tq%d" % (c // 8 * 128)
+            return T.tq[:, 16 * c + 15:16 * c + 16], "tq%d" % (cut if 16 * c >= cut else 0)
 
         def compare(c):
             ts(slot(c, 16 * c), bank(0, 0, 16 * c), pivot(c)[0], None, A.is_ge, None, ["P0", pivot(c)[1]], ["m%d" % c])
 
         def rowsum(c):
-            if c > OPT["nred"]:
-                act(T.junk[:, 8 * c * (c - 1):8 * c * (c + 1)], slot(c, 16 * c), AF.Copy, ["m%d" % c], ["r%d" % c], accum_out=T.r1[:, c:c + 1])
+            if c >= c0:
+                act(T.junk[:, C * (c - 9):C * (c - 9) + 16 * c], slot(c, 16 * c), AF.Copy, ["m%d" % c], ["q%d" % c], accum_out=T.r1[:, c:c + 1])
             else:
-                red(T.r1[:, c:c + 1], slot(c, 16 * c), ["m%d" % c], ["r%d" % c])
+                scan(T.rs[:, summed(c) + 1 - 16 * c:summed(c) + 1], slot(c, 16 * c), slot(c, 16 * c), A.add, A.max, ["m%d" % c], ["r%d" % c])
+
+        def rowsums(t):
+            scan(T.rs[:, GAP * t:GAP * t + 4 * C - 3:4], T.mt[:, 4 * MO[1] + t:4 * MO[3]:4], T.k2[:], A.add, A.min,
+                 ["m%d" % (1 + t), "m%d" % (5 + t), "k2a", "k2b"], ["r%d" % (1 + t), "r%d" % (5 + t)])
 
         def packed(k0, k1):
             a, b = MO[k0], MO[k1] + MW[k1]
@@ -333,154 +359,213 @@ def rank_program(g, core, T, topo):
                   ["mq%d" % k for k in range(k0, k1 + 1)])
             for k in range(k0, k1 + 1):
                 a, b = MO[k], MO[k] + MW[k]
-                mm(2, MW[k], T.oq[:], T.osb[:], T.mq[:, a:b], T.ms[:, a:b], ["oq", "mq%d" % k], k == 0, k == 3)
+                mm(2, MW[k], T.oq[:], T.osb[:], T.mq[:, a:b], T.ms[:, a:b], ["oq", "mq%d" % k], k == 0, k == OPT["lastq"])
 
-        for k, c in enumerate(both):
-            sg = T.sg[:, 256 * k:256 * k + 16 * c]
-            act(sg, bank(1, 0, 16 * c), AF.Sign, ["P1", pivot(c)[1]], ["sg%d" % k], bias=pivot(c)[0], scale=-1.0)
-        for k, c in enumerate(both):
-            sg = T.sg[:, 256 * k:256 * k + 16 * c]
-            act(slot(c, 16 * c), sg, AF.Sign, ["sg%d" % k], ["m%d" % c, "r%d" % c], bias=1.0, scale=-1.0, accum_out=T.r1[:, c:c + 1])
-        compare(rest[0])
-        tt(slot(0, C), bank(0, 0, C), T.tq[:], A.is_gt, ["P0", "tq0", "tq128"], ["m0"])
-        for c in rest[1:]:
-            compare(c)
-        packed(0, 0)
-        for c in range(8, 0, -1):
-            compare(c)
-        scan(T.dsc[:], T.keep[:], slot(0, C), A.mult, A.add, ["keep", "m0"], ["dsc"])
-        packed(1, 2)
-        packed(3, 3)
-        for c in rest + list(range(8, 0, -1)):
-            rowsum(c)
-        if rnd == 0:
-            middle_constants()
-        ua, ub, rk = T.ua[:, 0:16], T.ua[:, 16:32], T.ua[:, 32:48]
-        tt(ua, T.dsc[:, 15:C:16], T.k0[:], A.subtract, ["dsc", "k0"], ["ua"])
+        def own_copy(b):
+            act(win(b, TO, WN), bank(3 + b, 0, C), AF.Copy, ["P%d" % (3 + b)], ["wt%d" % b], scale=64.0)
+
+        def signs(c):
+            act(T.sg[:, C * (15 - c):C * (15 - c) + 16 * c], bank(1, 0, 16 * c), AF.Sign, ["P1", pivot(c)[1]], ["sg%d" % c], bias=pivot(c)[0], scale=-1.0)
+
+        def beaten(c):
+            act(slot(c, 16 * c), T.sg[:, C * (15 - c):C * (15 - c) + 16 * c], AF.Sign, ["sg%d" % c], ["m%d" % c, "q%d" % c],
+                bias=1.0, scale=-1.0, accum_out=T.r1[:, c:c + 1])
+
+        if nss == 5:
+            signs(15), signs(11), signs(14), beaten(11), signs(13), signs(12)
+            for c in both[:4]:
+                beaten(c)
+        else:
+            for c in both:
+                signs(c)
+            for c in both:
+                beaten(c)
+        def inside():
+            tt(slot(0, C), bank(0, 0, C), T.tq[:], A.is_gt, ["P0", "tq0", "tq%d" % cut], ["m0"])
+
+        def inside_sums():
+            scan(T.dsc[:], slot(0, C), T.kd[:], A.add, A.min, ["kd", "m0"], ["dsc"])
+
+        def by_scalar():
+            for c in rest:
+                if c >= c0:
+                    rowsum(c)
+            act(T.rs[:, summed(c0):summed(15) + 1:GAP], T.r1[:, c0:16], AF.Copy, ["q%d" % c for c in range(c0, 16)], ["r%d" % c for c in range(c0, 16)])
+
+        for x in OPT["order"].split():
+            k = int(x[1:] or 0)
+            if x[0] == "c":
+                if k in rest or k < 9:
+                    compare(k)
+            elif x[0] == "r":
+                if k < c0:
+                    rowsum(k)
+            elif x[0] == "q":
+                packed(k // 10, k % 10)
+            else:
+                {"m": inside, "d": inside_sums, "s": by_scalar, "l": lambda: rowsums(k)}[x[0]]()
+        ub, rk = T.ua[:, 0:16], T.ua[:, 16:32]
+        tt(ub, T.dsc[:, 15:C:16], T.rs[:, summed(0):summed(15) + 1:GAP], A.add, ["dsc"] + ["r%d" % c for c in range(16)], ["ub"])
         scan(T.csc[:], T.drop[:], bank(2, 0, C), A.add, A.min, ["drop", "P2"], ["csc"])
-        tt(ub, ua, T.r1[:], A.add, ["ua"] + ["r%d" % c for c in range(16)], ["ub"])
+        for b in range(OPT["tfirst"]):
+            own_copy(b)
+        if rnd == 0:
+            later_constants()
+        beside()
         tt(rk, T.csc[:, 15:C:16], ub, A.subtract, ["csc", "ub"], ["rk"])
+        beside()
         for k in range(2):
             ts(T.i32[:, 16 * k:16 * k + 16], rk, scale[k], shift[k], A.mult, A.add, ["rk", "pf6", "pf7", "pf8", "pf9"], ["i32%d" % k])
+        beside()
         tr(T.o32[:], T.i32[:], ["i320", "i321"], ["o32"])
+        beside()
         gm, gb, gl = T.gm[:, 32 * rnd + 8:32 * rnd + 24], T.gm[:, 32 * rnd + 7:32 * rnd + 23], T.gl[:, 32 * rnd:32 * rnd + 16]
         G = "gm%d" % rnd
         tt(gm, T.o32[:, 0:16], T.o32[:, 16:32], A.add, ["o32"], [G])
+        beside()
         send(gl, gm, "af%d" % rnd, [G])
+        if rnd == 0:
+            iota(T.up[:], [[1, 16], [16, 16]], 1, 0, ["up"])
+            iota(T.ln[:, 2 * C:4 * C], [[0, 2 * C]], -1024, 0, ["ln"])
 
         tb = [7, 1, 0, 2]
+        o = T.own
+        kb, dk, thr, tot, of = o[:, 1:17], T.cidx[:, 0:17], o[:, 64:80], o[:, 80:81], o[:, 81:82]
+
+        def own_sums():
+            if OPT["k1"] == "a":
+                act(kb, gm, AF.Relu, [G], ["kb"], scale=511.0, bias=-511 * ETA)
+            else:
+                ts(kb, gm, 1.5 * ETA, 511 * ETA, A.is_gt, A.mult, [G], ["kb"])
+            total(OPT["tot"], tot, gm, o[:, 160:176], [G], ["tot"])
+            if OPT["thr"] == "a":
+                act(thr, gm, AF.Relu, [G], ["thr"], scale=-1 / ETA, bias=1.0)
+            else:
+                ts(thr, gm, 0.5 * ETA, None, A.is_lt, None, [G], ["thr"])
+            lin(OPT["fx"], o[:, 96:128], lt, tot, 0.0, ["lt", "tot"], ["fx"])
+            tt(kb, kb, ieta, A.max, ["kb", "ieta"], ["kb"])
+            tr(o[:, 128:160], o[:, 96:128], ["fx"], ["fxt"])
+            tt(dk, o[:, 1:18], o[:, 0:17], A.subtract, ["kb"], ["dk"])
+
         for b in range(4):
             unpack(tb[b], b, pq[:], pz[:], [], ext=[("aq%d" % rnd, 2 * len(eng))] if b == 0 else [])
         for b in range(4):
-            if b < 4 - OPT["tpv"]:
-                act(T.tp[:, b:1024:4], bank(tb[b], 0, C), AF.Copy, ["P%d" % tb[b]], ["tp%d" % b], scale=-1.0)
-            else:
-                ts(T.tp[:, b:1024:4], bank(tb[b], 0, C), -1.0, None, A.mult, None, ["P%d" % tb[b]], ["tp%d" % b])
+            if b == OPT["small"]:
+                own_sums()
+            act(T.tp[:, b:1024:4], bank(tb[b], 0, C), AF.Copy, ["P%d" % tb[b]], ["tp%d" % b], scale=-1.0)
+        if OPT["small"] == 4:
+            own_sums()
+        total(OPT["of"], of, o[:, 128:160], o[:, 160:192], ["fxt"], ["of"])
         for b in range(4):
             unpack(tb[b], b, xq[:], xs[:], [X], True, False)
-        for b in range(4):
-            act(T.win[:, WN * b + SH:WN * b + WN], bank(3 + b, 0, C), AF.Copy, ["P%d" % (3 + b)], ["wt%d" % b], scale=64.0)
-        if rnd == 0:
-            later_constants()
-        o = T.own
-        kb, dk, thr, tot, of = o[:, 1:17], o[:, 32:49], o[:, 64:80], o[:, 80:81], o[:, 81:82]
-        red(tot, gm, [G], ["tot"])
-        ts(kb, gm, 1.5 * ETA, 511 * ETA, A.is_gt, A.mult, [G], ["kb"])
-        ts(o[:, 96:128], lt, tot, None, A.mult, None, ["lt", "tot"], ["fx"])
-        tt(kb, kb, ieta, A.max, ["kb", "ieta"], ["kb"])
-        tr(o[:, 128:160], o[:, 96:128], ["fx"], ["fxt"])
-        tt(dk, o[:, 1:18], o[:, 0:17], A.subtract, ["kb"], ["dk"])
-        red(of, o[:, 128:160], ["fxt"], ["of"])
-        ts(thr, gm, 0.5 * ETA, 0.5 * ETA, A.is_lt, A.max, [G], ["thr"])
-        fill(T.ln[:, 2 * C:3 * C], 512.0, ["ln"])
-        fill(T.le[:, 128:SH], 256.0, ["le"])
-        if rnd == 0:
-            last_constants()
+        for b in range(OPT["tfirst"], 4):
+            own_copy(b)
         if rnd == 1:
             quant(T.vq[:], T.vs[:], T.vt[:], ["vt"], ["vq"])
         quant(T.fq[:], T.fs[:], T.tp[:], ["tp0", "tp1", "tp2", "tp3"], ["fq"])
         for b in range(4):
             unpack(tb[b], b, T.fq[:], T.fs[:], ["fq"], False, True)
         for b in range(4):
-            act(T.zf[:, C * b:C * b + C], bank(tb[b], 0, C), AF.Copy, ["P%d" % tb[b]], ["zf%d" % b])
+            act(win(b, ZO, TO), bank(tb[b], 0, C), AF.Copy, ["P%d" % tb[b]], ["zf%d" % b])
 
         w, mx = T.w, T.mx
-        mm_, hh = w[:, 1:17], w[:, 32:48]
-        p1, ck, t1, nq, p2 = w[:, 64:81], w[:, 96:113], w[:, 128:144], w[:, 144:160], w[:, 160:176]
-        oh, om, sc, mtot = mx[:, 287:288], mx[:, 319:320], mx[:, 351:352], mx[:, 383:384]
+        mm_, hh = w[:, 1:17], w[:, 18:34]
+        t1, nq, p2 = w[:, 128:144], w[:, 144:160], w[:, 160:176]
+        oh, om, sc = mx[:, 223:224], mx[:, 255:256], mx[:, 287:288]
         tt(mm_, gm, gl, A.min, [G], ["mm"], ext=[("af%d" % rnd, len(eng))])
         tt(hh, gl, thr, A.is_gt, ["thr"], ["hh"])
-        scan(p1, dk, w[:, 1:18], A.add, A.add, ["dk", "mm"], ["p1"])
-        scan(ck, step, w[:, 32:49], A.add, A.add, ["step", "step2", "hh", "pf10"], ["ck"], first)
-        ts(mx[:, 32:128], T.m32[:], w[:, 80:81], None, A.mult, None, ["lt", "sl", "same", "p1"], ["mx1"])
-        ts(mx[:, 0:32], lt, w[:, 112:113], None, A.mult, None, ["lt", "ck"], ["mx0"])
-        tt(t1, hh, negk, A.mult, ["hh", "negk"], ["t1"])
-        tr(mx[:, 128:256], mx[:, 0:128], ["mx0", "mx1"], ["mxt"])
-        tt(t1, t1, w[:, 96:112], A.add, ["t1", "ck"], ["t1"])
-        scan(mx[:, 256:384], T.k32[:], mx[:, 128:256], A.mult, A.add, ["k32", "mxt"], ["sums"])
-        scan(p2, gb, w[:, 0:16], A.add, A.subtract, [G, "mm", "of"], ["p2"], of)
-        ts(T.offe[:], t1, oh, -2.0, A.add, A.add, ["t1", "sums"], ["offe"])
         tt(nq, gl, gm, A.is_ge, [G], ["nq"])
-        cp(T.le[:].indirect(T.offe[:]), T.up[:], ["offe", "up"], ["le"])
-        act(T.ks[:, 0:C], T.slot[:], AF.Relu, ["slot", "sums"], ["anew"], scale=-4096.0, bias=mtot)
+        scan(w[:, 64:98], T.cidx[:, 0:34], w[:, 1:35], A.add, A.add, ["dk", "step1", "step2", "mm", "hh"], ["pk"])
+        tt(t1, hh, negk, A.mult, ["hh", "negk"], ["t1"])
+        ts(mx[:, 32:96], T.m32[:, 0:64], w[:, 80:81], None, A.mult, None, ["lt", "sl", "pk"], ["mx1"])
+        ts(mx[:, 0:32], lt, w[:, 97:98], None, A.mult, None, ["lt", "pk"], ["mx0"])
+        tt(t1, t1, w[:, 81:97], A.add, ["t1", "pk"], ["t1"])
+        tr(mx[:, 96:192], mx[:, 0:96], ["mx0", "mx1"], ["mxt"])
+        scan(p2, gb, w[:, 0:16], A.add, A.subtract, [G, "mm", "of"], ["p2"], of)
+        scan(mx[:, 192:288], T.k32[:], mx[:, 96:192], A.mult, A.add, ["k32", "mxt"], ["sums"])
         tt(p2, p2, nq, A.subtract, ["p2", "nq"], ["p2"])
+        ts(T.offe[:], t1, oh, -2.0, A.add, A.add, ["t1", "sums"], ["offe"])
+        ts(p2, p2, sc, 768 * ETA, A.add, A.add, ["p2", "sums"], ["p2"])
+        cp(T.le[:].indirect(T.offe[:]), T.up[:], ["offe", "up"], ["le"])
+        tt(p2, p2, w[:, 64:80], A.max, ["p2", "pk"], ["p2"])
         scan(T.lek[:], T.hold[:, 0:SH], T.le[:, 0:SH], A.add, A.min, ["hold", "le"], ["lek"])
-        ts(p2, p2, sc, 512 * ETA, A.add, A.add, ["p2", "sums"], ["p2"])
-        ts(T.el[:], T.lek[:, 15:SH:16], -1.0, None, A.add, None, ["lek"], ["el"])
-        tt(p2, p2, w[:, 64:80], A.max, ["p2", "p1"], ["p2"])
         ts(T.offn[:], p2, om, 1.0 / ETA, A.add, A.mult, ["p2", "sums"], ["offn"])
+        ts(T.el[:], T.lek[:, 15:SH:16], -1.0, None, A.add, None, ["lek"], ["el"])
+        if last:
+            for k in range(2):
+                lin("a", T.idw[:, k:ZO:2], T.le[:, 0:SH], 1.0, -1.0, ["le"], ["id%d" % (k + 1)])
 
         for b in range(4):
-            act(T.zt[:, b:512:4], T.zf[:, C * b:C * b + C].indirect(T.el[:, 0:8]), AF.Copy, ["zf%d" % b, "el"], ["zt%d" % b])
+            act(T.zt[:, b:512:4], win(b, ZO, TO).indirect(T.el[:, 0:8]), AF.Copy, ["zf%d" % b, "el"], ["zt%d" % b])
         for b in range(4):
-            act(T.win[:, WN * b:WN * b + SH], T.win[:, WN * b + SH:WN * b + WN].indirect(T.el[:]), AF.Copy,
-                ["wt%d" % b, "el"], ["wf%d" % b])
-        cp(T.ln[:].indirect(T.offn[:]), T.down[:], ["offn", "down"], ["ln"])
+            act(win(b, 1, ZO, 2), win(b, TO, WN).indirect(T.el[:]), AF.Copy, ["wt%d" % b, "el"], ["wf%d" % b])
+            op("g", lambda b=b: g.affine_select(win(b, C, ZO, 2), win(b, C + 1, ZO, 2), [[0, SH - 128]], A.is_ge, 0.0, 0, 0),
+               ["wf%d" % b], ["we%d" % b])
+        cp(T.ln[:].indirect(T.offn[:]), T.up[:], ["offn", "up"], ["ln"])
+        ts(T.un[:, 1:C + 1], T.ln[:, 2 * C:3 * C], 0.0, None, A.is_lt, None, ["ln"], ["un"])
         quant(T.zq[:], T.zs[:], T.zt[:], ["zt0", "zt1", "zt2", "zt3"], ["zq"])
         for b in range(4):
             mm(3 + b, 128, T.wq[:, 128 * b:128 * b + 128], T.wsc[:, 128 * b:128 * b + 128], T.zq[:], T.zs[:], ["wq", "wsc", "zq"])
 
-        got, free, held, cnt, cx = T.ln[:, 2 * C:3 * C], T.ks[:, C:2 * C], T.ks[:, 2 * C:3 * C], T.ks[:, 3 * C:4 * C], T.ks[:, 4 * C:5 * C]
-        z = w[:, 192:208]
-
         def made(b):
-            tt(T.win[:, WN * b:WN * b + 128], bank(3 + b, 0, 128), T.win[:, WN * b:WN * b + 128], A.add,
-               ["P%d" % (3 + b), "wf%d" % b], ["wf%d" % b])
+            tt(win(b, 0, C, 2), bank(3 + b, 0, 128), win(b, 1, C, 2), A.add, ["P%d" % (3 + b), "wf%d" % b], ["wm%d" % b])
 
-        ts(free, got, 300.0, None, A.is_gt, None, ["ln"], ["free"])
-        scan(held, T.ks[:, 0:C], got, A.add, A.min, ["anew", "ln"], ["held"])
-        scan(cnt, free, free, A.add, A.max, ["free"], ["cnt"])
-        scan(T.ux[:], T.drop[:], held, A.add, A.min, ["drop", "held"], ["ux"])
-        scan(cx, T.hold[:], cnt, A.add, A.min, ["hold", "cnt"], ["cx"])
-        ts(z, T.ux[:, 15:C:16], -1.0, ubias, A.mult, A.add, ["ux", "pf11"], ["z"])
+        pair, best, kept = T.ks[:, 0:C], T.ks[:, C:2 * C], T.ks[:, 2 * C:3 * C]
+        scan(pair, T.un[:, 1:C + 1], T.un[:, 0:C], A.add, A.add, ["un", "un0"], ["pair"], -1.0 - TO)
+        scan(best, pair, T.ln[:, 3 * C:4 * C], A.max, A.max, ["pair", "ln"], ["best"], -1024.0)
+        scan(kept, T.hold[:], best, A.add, A.min, ["hold", "best"], ["kept"])
         made(0)
-        tt(z, z, T.ks[:, 4 * C + 15:5 * C:16], A.max, ["z", "cx"], ["z"])
+        ts(T.nlist[:], T.ks[:, 2 * C + 15:3 * C:16], TO - 1.0, None, A.add, None, ["kept"], ["nlist"])
         made(1)
-        ts(T.nlist[:], z, -1.0, None, A.add, None, ["z"], ["nlist"])
         made(2)
         made(3)
 
-        def part(b):
-            return ["wt%d" % b, "wf%d" % b, "nlist"]
+        def take(q, b, a, e):
+            rd = ["wt%d" % b, "wf%d" % b, "we%d" % b, "wm%d" % b, "zf%d" % b, "nlist"]
+            out, src = T.xt[:, 64 * a + b:64 * e:4], win(b, 0, WN).indirect(T.nlist[:, a:e])
+            wr = ["xt%d_%d" % (b, k) for k in range(a // 2, e // 2)]
+            if q == "a":
+                act(out, src, AF.Copy, rd, wr, scale=1.0 / 64)
+            else:
+                ts(out, src, 1.0 / 64, None, A.mult, None, rd, wr)
+
+        def state(a, e):
+            n = rnd + 1
+            quant(T["xq%d" % n][:, 16 * a:16 * e], T["xs%d" % n][:, 16 * a:16 * e], T.xt[:, 64 * a:64 * e],
+                  ["xt%d_%d" % (b, k) for b in range(4) for k in range(a // 2, e // 2)], ["xq%d" % n if e == 16 else "xh"])
 
         vs = OPT["vsplit"]
-        for b in (0, 1):
-            act(T.xt[:, b:1024:4], T.win[:, WN * b:WN * b + WN].indirect(T.nlist[:]), AF.Copy, part(b), ["xt%d" % b], scale=1.0 / 64)
-        if vs:
-            act(T.xt[:, 2:64 * vs:4], T.win[:, WN * 2:WN * 3].indirect(T.nlist[:, 0:vs]), AF.Copy, part(2), ["xt4"], scale=1.0 / 64)
-        ts(T.xt[:, 64 * vs + 2:1024:4], T.win[:, WN * 2:WN * 3].indirect(T.nlist[:, vs:16]), 1.0 / 64, None, A.mult, None, part(2), ["xt2"])
-        ts(T.xt[:, 3:1024:4], T.win[:, WN * 3:WN * 4].indirect(T.nlist[:]), 1.0 / 64, None, A.mult, None, part(3), ["xt3"])
-        quant(T["xq%d" % (rnd + 1)][:], T["xs%d" % (rnd + 1)][:], T.xt[:], ["xt0", "xt1", "xt2", "xt3", "xt4"], ["xq%d" % (rnd + 1)])
-        if rnd == 2:
-            ts(T.idw[:, 0:SH], T.le[:, 0:SH], -1.0, None, A.add, None, ["le"], ["id1"])
+        if last and OPT["tail"]:
+            for a in (0, 8):
+                for b in range(4):
+                    take("a" if b < 2 else "v", b, a, a + 8)
+                state(a, a + 8)
+        else:
+            take("a", 0, 0, 16)
+            take("a", 1, 0, 16)
+            if vs:
+                take("a", 2, 0, vs)
+            take("v", 2, vs, 16)
+            take("v", 3, 0, 16)
+            state(0, 16)
 
-    mm(3, C, T.vq[:], T.vs[:], T.xq3[:], T.xs3[:], ["vq", "xq3"])
-    dma("s", T.oc[:], T.xq3[:].bitcast(dt.uint8), ["xq3"], [])
-    cp(T.nlo[:], T.idw[:].indirect(T.nlist[:]), ["id0", "id1", "nlist"], ["nlo"])
-    act(T.yo[:], bank(3, 0, C), AF.Copy, ["P3"], ["yo"])
-    dma("a", T.y[:], T.yo[:], ["yo"], [])
+    whole = ["xq3", "xh"]
+    if OPT["tail"]:
+        for k, tag in enumerate(["xh", "xq3"]):
+            mm(3 + k, 128, T.vq[:], T.vs[:], T.xq3[:, 128 * k:128 * k + 128], T.xs3[:, 128 * k:128 * k + 128], ["vq", tag])
+        dma("s", T.oc[:], T.xq3[:].bitcast(dt.uint8), whole, [])
+        act(T.yo[:, 0:128], bank(3, 0, 128), AF.Copy, ["P3"], ["yo0"])
+        dma("a", T.y[:, 0:128], T.yo[:, 0:128], ["yo0"], [])
+        act(T.yo[:, 128:C], bank(4, 0, 128), AF.Copy, ["P4"], ["yo1"])
+        dma("a", T.y[:, 128:C], T.yo[:, 128:C], ["yo1"], [])
+    else:
+        mm(3, C, T.vq[:], T.vs[:], T.xq3[:], T.xs3[:], ["vq", "xq3"])
+        dma("s", T.oc[:], T.xq3[:].bitcast(dt.uint8), ["xq3"], [])
+        act(T.yo[:], bank(3, 0, C), AF.Copy, ["P3"], ["yo"])
+        dma("a", T.y[:], T.yo[:], ["yo"], [])
+    cp(T.nlo[:], T.idw[:].indirect(T.nlist[:]), ["id0", "id1", "id2", "nlist"], ["nlo"])
     for k in range(4):
-        dma("s" if k < 3 else "a", T.osc[4 * k:4 * k + 4, :], T.xs3[32 * k:32 * k + 4, :], ["xq3"], [])
+        dma("s", T.osc[4 * k:4 * k + 4, :], T.xs3[32 * k:32 * k + 4, :], whole, [])
     dma("s", T.nl[:], T.nlo[0:128:16, :], ["nlo"], [])
     emit(g, T, ops)
     g.wait_ge(T.sem.gone, gone[0])

@@ -1,3 +1,4 @@
+from concourse.bass import DstId, RemoteDMATransfer
 from concourse.mybir import dt, AluOpType, AxisListType, ActivationFunctionType
 
 A = AluOpType
@@ -10,7 +11,9 @@ BIG = 2.0 ** 88
 ETA = 2.0 ** -16
 GAP = 191
 CODE = "float8_e4m3fn_x4"
-OPT = dict(lastq=2, order="c12 c11 m c10 c9 c8 q00 c7 c6 c5 c4 c3 c2 c1 s q33 q12 d r11 r10 r9 l0 l1 l2 l3", nss=3, c0=9, vsplit=2, tfirst=1, thr="v", k1="v", tot="v", fx="v", of="v", cut=192, tail=1, padv=(0, 2), small=2)
+OPT = dict(window="bsktrmodvq", forder=(0, 1, 2, 3), slots="szuqpbk0n123", ftail=(("a", 0), ("v", 1), ("a", 2), ("v", 3)),
+           final=(("a", 0, 0, 16), ("v", 1, 0, 16), ("a", 2, 0, 16), ("v", 3, 0, 14), ("a", 3, 14, 16)),
+           fold=1, scfirst=1, lastq=1, order="c13 c12 c11 m c10 c9 c8 c7 q00 c6 c5 c4 c3 c2 q22 c1 s q33 q11 d r11 r10 r9 l0 l1 l2 l3", nss=3, c0=9, vsplit=2, tfirst=1, thr="v", k1="v", tot="v", fx="v", of="v", cut=176, tail=1, padv=(0, 2), small=2)
 
 
 def sb(n, d):
@@ -34,11 +37,11 @@ SCRATCH = {
     "kd": sb(256, "bfloat16"), "k2": sb(256, "bfloat16"),
     "m32": sb(96, "bfloat16"), "k32": sb(96, "bfloat16"),
     "cidx": sb(96, "float32"), "uoff": sb(8, "uint16"),
-    "m1": sb(256, "float32"), "tq": sb(256, "float32"), "sg": sb(1280, "bfloat16"), "junk": sb(1024, "bfloat16"),
+    "m1": sb(256, "float32"), "tq": sb(256, "float32"), "sg": sb(1280, "bfloat16"), "junk": sb(1280, "bfloat16"),
     "r1": sb(16, "float32"), "rs": sb(2944, "bfloat16"), "dsc": sb(256, "bfloat16"), "csc": sb(256, "float32"),
-    "ua": sb(32, "float32"), "i32": sb(32, "bfloat16"), "o32": sb(32, "bfloat16"),
-    "gm": sb(96, "bfloat16"), "gl": sb(96, "bfloat16"),
-    "own": sb(192, "float32"), "w": sb(192, "float32"), "mx": sb(288, "bfloat16"),
+    "ua": sb(32, "float32"), "i32": sb(32, "bfloat16"), "o32": sb(96, "bfloat16"),
+    "gm": sb(192, "bfloat16"), "fx": sb(128, "bfloat16"), "gl": sb(96, "bfloat16"),
+    "own": sb(192, "float32"), "w": sb(192, "float32"), "mx": sb(192, "bfloat16"), "ex": sb(128, "bfloat16"), "stay": sb(48, "bfloat16"),
     "offe": sb(16, "uint16"), "le": sb(768, "bfloat16"), "lek": sb(SH, "bfloat16"), "el": sb(12, "uint16"),
     "offn": sb(16, "uint16"), "ln": sb(1024, "bfloat16"), "un": sb(272, "bfloat16"), "ks": sb(3 * C, "float16"),
     "nlist": sb(16, "uint16"),
@@ -195,7 +198,7 @@ def rank_program(g, core, T, topo):
 
     nss, c0, cut = OPT["nss"], OPT["c0"], OPT["cut"]
     both = list(range(15, 15 - nss, -1))
-    rest = [c for c in (12, 11, 10, 9) if c not in both]
+    rest = [c for c in (13, 12, 11, 10, 9) if c not in both]
     lanes = [[0, 11, 10, 9], [1, 2, 3, 4], [5, 6, 7, 8], [15, 14, 13, 12]]
     MW = [256, 128, 128, 240]
     MO = [0, 256, 384, 512]
@@ -279,21 +282,23 @@ def rank_program(g, core, T, topo):
         ts(T.ot[:, t:512:4], T.g16[:], gp, None, A.is_equal, None, ["g16", "pf"], ["ot%d" % t])
     quant(T.oq[:], T.osb[:], T.ot[:], ["ot0", "ot1", "ot2", "ot3"], ["oq"])
 
-    lt, same, negk, ieta = T.m32[:, 0:32], T.m32[:, 64:96], T.cidx[:, 48:64], T.cidx[:, 64:80]
+    lt, same, far, ieta = T.m32[:, 0:32], T.m32[:, 64:96], T.cidx[:, 48:64], T.cidx[:, 64:80]
 
     def later_constants():
-        first = column("a", 10, rr, -16.0, -255.0)
-        lin("a", negk, T.yy[:, 0:16], -1.0, first, ["yy", "pf10"], ["negk"])
-        lin("a", ieta, negk, -ETA, -255 * ETA, ["negk"], ["ieta"])
-        lin("a", T.cidx[:, 17:18], rr, 16.0, 256.0, ["pf", "step"], ["step1"])
-        lin("a", T.cidx[:, 33:34], rr, -16.0, -271.0, ["pf", "step"], ["step2"])
+        first = column("a", 10, rr, 16.0, 256.0)
+        column("a", 11, rr, -1.0, 47.0)
         act(T.k32[:], T.k32[:], AF.Sign, ["k32"], ["k32"])
+        lin("a", far, T.yy[:, 0:16], 1.0, first, ["yy", "pf10"], ["far"])
+        lin("a", T.pf[:, 12:13], par, -1.0, T.pf[:, 11:12], ["pf", "pf11"], ["pf12"])
+        lin("a", T.k32[:, 80:81], par, -1.0 / 16, 1.0, ["pf", "k32"], ["k16"])
+        lin("a", ieta, far, ETA, -256 * ETA, ["far"], ["ieta"])
 
     masks = [lambda: ts(same, T.g16[:, 0:32], par, None, A.is_equal, None, ["g16", "pf"], ["same"]),
              lambda: ts(lt, T.yy[:, 0:32], rr, None, A.is_gt, None, ["yy", "pf"], ["lt"]),
              lambda: tt(lt, lt, same, A.mult, ["lt", "same"], ["lt"]),
              lambda: lin("v", T.m32[:, 32:64], lt, -2.0, 0.0, ["lt"], ["sl"]),
-             lambda: tt(T.m32[:, 32:64], T.m32[:, 32:64], same, A.add, ["sl", "same"], ["sl"])]
+             lambda: tt(T.m32[:, 32:64], T.m32[:, 32:64], same, A.add, ["sl", "same"], ["sl"]),
+             lambda: ts(T.stay[:], T.stay[:], T.pf[:, 12:13], None, A.is_lt, None, ["stay", "pf12"], ["stay"])]
 
     def beside():
         if masks:
@@ -316,10 +321,10 @@ def rank_program(g, core, T, topo):
         if rnd == 0:
             iota(T.k2[:, 0:128], [[-4096, 128]], 127 * 4096, 0, ["k2a"])
             iota(T.k2[:, 128:256], [[0, 128]], 4096, 0, ["k2b"])
-            iota(T.cidx[:, 17:34], [[0, 17]], 1, 0, ["step"])
+            iota(T.stay[:], [[1, 48]], 0, 0, ["stay"])
             iota(T.k32[:], [[0, 3], [1, 32]], 0, 0, ["k32"])
             iota(T.own[:, 0:18], [[0, 18]], 0, 0, ["kb"])
-            iota(T.w[:, 0:36], [[0, 36]], 0, 0, ["mm", "hh"])
+            iota(T.w[:, 0:80], [[0, 80]], 0, 0, ["mm", "hh"])
             iota(T.un[:, 0:1], [[0, 1]], 1, 0, ["un0"])
         iota(T.le[:, 128:SH], [[0, SH - 128]], C, 0, ["le"])
         if rnd > 0:
@@ -417,77 +422,82 @@ def rank_program(g, core, T, topo):
         for k in range(2):
             ts(T.i32[:, 16 * k:16 * k + 16], rk, scale[k], shift[k], A.mult, A.add, ["rk", "pf6", "pf7", "pf8", "pf9"], ["i32%d" % k])
         beside()
-        tr(T.o32[:], T.i32[:], ["i320", "i321"], ["o32"])
+        tr(T.o32[:, 32 * rnd:32 * rnd + 32], T.i32[:], ["i320", "i321"], ["o%d" % rnd])
         beside()
-        gm, gb, gl = T.gm[:, 32 * rnd + 8:32 * rnd + 24], T.gm[:, 32 * rnd + 7:32 * rnd + 23], T.gl[:, 32 * rnd:32 * rnd + 16]
+        gm, gb, gl = T.gm[:, 64 * rnd + 8:64 * rnd + 24], T.gm[:, 64 * rnd + 7:64 * rnd + 23], T.gl[:, 32 * rnd:32 * rnd + 16]
         G = "gm%d" % rnd
-        tt(gm, T.o32[:, 0:16], T.o32[:, 16:32], A.add, ["o32"], [G])
+        lo, hi = T.o32[:, 32 * rnd:32 * rnd + 16], T.o32[:, 32 * rnd + 16:32 * rnd + 32]
+        tt(gm, lo, hi, A.add, ["o%d" % rnd], [G])
         beside()
-        send(gl, gm, "af%d" % rnd, [G])
+        if OPT["fold"]:
+            fold = RemoteDMATransfer(dst_ids=[DstId(rid=rid, pnc=pid)], dma_engine_mask=maskof(eng), remote_sem=T.sem["af%d" % rnd],
+                                     srcs=[lo, hi], dsts=[gl], alu_op=1)
+            op("g", lambda fold=fold: g.remote_dma_fused([fold], local_sem=T.sem.gone), ["o%d" % rnd], [], (), "far")
+            gone[0] += len(eng)
+        else:
+            send(gl, gm, "af%d" % rnd, [G])
         if rnd == 0:
             iota(T.up[:], [[1, 16], [16, 16]], 1, 0, ["up"])
             iota(T.ln[:, 2 * C:4 * C], [[0, 2 * C]], -1024, 0, ["ln"])
 
         tb = [7, 1, 0, 2]
-        o = T.own
-        kb, dk, thr, tot, of = o[:, 1:17], T.cidx[:, 0:17], o[:, 64:80], o[:, 80:81], o[:, 81:82]
-
-        def own_sums():
-            if OPT["k1"] == "a":
-                act(kb, gm, AF.Relu, [G], ["kb"], scale=511.0, bias=-511 * ETA)
-            else:
-                ts(kb, gm, 1.5 * ETA, 511 * ETA, A.is_gt, A.mult, [G], ["kb"])
-            total(OPT["tot"], tot, gm, o[:, 160:176], [G], ["tot"])
-            if OPT["thr"] == "a":
-                act(thr, gm, AF.Relu, [G], ["thr"], scale=-1 / ETA, bias=1.0)
-            else:
-                ts(thr, gm, 0.5 * ETA, None, A.is_lt, None, [G], ["thr"])
-            lin(OPT["fx"], o[:, 96:128], lt, tot, 0.0, ["lt", "tot"], ["fx"])
-            tt(kb, kb, ieta, A.max, ["kb", "ieta"], ["kb"])
-            tr(o[:, 128:160], o[:, 96:128], ["fx"], ["fxt"])
-            tt(dk, o[:, 1:18], o[:, 0:17], A.subtract, ["kb"], ["dk"])
-
+        o, fx = T.own, T.fx
+        kb, dk, thr, of = o[:, 1:17], T.cidx[:, 0:17], o[:, 64:80], fx[:, 127:128]
         for b in range(4):
             unpack(tb[b], b, pq[:], pz[:], [], ext=[("aq%d" % rnd, 2 * len(eng))] if b == 0 else [])
         for b in range(4):
-            if b == OPT["small"]:
-                own_sums()
             act(T.tp[:, b:1024:4], bank(tb[b], 0, C), AF.Copy, ["P%d" % tb[b]], ["tp%d" % b], scale=-1.0)
-        if OPT["small"] == 4:
-            own_sums()
-        total(OPT["of"], of, o[:, 128:160], o[:, 160:192], ["fxt"], ["of"])
         for b in range(4):
             unpack(tb[b], b, xq[:], xs[:], [X], True, False)
         for b in range(OPT["tfirst"], 4):
             own_copy(b)
-        if rnd == 1:
-            quant(T.vq[:], T.vs[:], T.vt[:], ["vt"], ["vq"])
-        quant(T.fq[:], T.fs[:], T.tp[:], ["tp0", "tp1", "tp2", "tp3"], ["fq"])
-        for b in range(4):
-            unpack(tb[b], b, T.fq[:], T.fs[:], ["fq"], False, True)
-        for b in range(4):
-            act(win(b, ZO, TO), bank(tb[b], 0, C), AF.Copy, ["P%d" % tb[b]], ["zf%d" % b])
 
-        w, mx = T.w, T.mx
-        mm_, hh = w[:, 1:17], w[:, 18:34]
-        t1, nq, p2 = w[:, 128:144], w[:, 144:160], w[:, 160:176]
-        oh, om, sc = mx[:, 223:224], mx[:, 255:256], mx[:, 287:288]
-        tt(mm_, gm, gl, A.min, [G], ["mm"], ext=[("af%d" % rnd, len(eng))])
-        tt(hh, gl, thr, A.is_gt, ["thr"], ["hh"])
+        def difference():
+            quant(T.fq[:], T.fs[:], T.tp[:], ["tp0", "tp1", "tp2", "tp3"], ["fq"])
+            for b in range(4):
+                unpack(tb[b], b, T.fq[:], T.fs[:], ["fq"], False, True)
+            for b in range(4):
+                act(win(b, ZO, TO), bank(tb[b], 0, C), AF.Copy, ["P%d" % tb[b]], ["zf%d" % b])
+
+        steps = {
+            "k": lambda: ts(kb, gm, 1.5 * ETA, 511 * ETA, A.is_gt, A.mult, [G], ["kb"]),
+            "t": lambda: ts(thr, gm, 0.5 * ETA, None, A.is_lt, None, [G], ["thr"]),
+            "s": lambda: scan(fx[:, 47::-1], T.stay[:], T.gm[:, 64 * rnd + 8:64 * rnd + 56], A.mult, A.add, ["stay", G], ["fx"]),
+            "m": lambda: tt(kb, kb, ieta, A.max, ["kb", "ieta"], ["kb"]),
+            "r": lambda: tr(fx[:, 64:96], fx[:, 0:32], ["fx"], ["fxt"]),
+            "d": lambda: tt(dk, o[:, 1:18], o[:, 0:17], A.subtract, ["kb"], ["dk"]),
+            "o": lambda: scan(fx[:, 96:128], T.k32[:, 64:96], fx[:, 64:96], A.mult, A.add, ["k32", "k16", "fxt"], ["of"]),
+            "v": lambda: rnd == 1 and quant(T.vq[:], T.vs[:], T.vt[:], ["vt"], ["vq"]),
+            "b": beside, "q": difference}
+        for x in OPT["window"]:
+            steps[x]()
+
+        w, mx, ex = T.w, T.mx, T.ex
+        mm_, hh = w[:, 1:17], w[:, 32:48]
+        t1, nq, p2, p1 = w[:, 128:144], w[:, 144:160], w[:, 160:176], w[:, 96:113]
+        oh, om, sc = ex[:, 127:128], mx[:, 159:160], mx[:, 191:192]
+        tt(hh, gl, thr, A.is_gt, ["thr"], ["hh"], ext=[("af%d" % rnd, len(eng))])
+        tt(mm_, gm, gl, A.min, [G], ["mm"])
+        tt(t1, gl, thr, A.is_le, ["thr"], ["t1"])
         tt(nq, gl, gm, A.is_ge, [G], ["nq"])
-        scan(w[:, 64:98], T.cidx[:, 0:34], w[:, 1:35], A.add, A.add, ["dk", "step1", "step2", "mm", "hh"], ["pk"])
-        tt(t1, hh, negk, A.mult, ["hh", "negk"], ["t1"])
-        ts(mx[:, 32:96], T.m32[:, 0:64], w[:, 80:81], None, A.mult, None, ["lt", "sl", "pk"], ["mx1"])
-        ts(mx[:, 0:32], lt, w[:, 97:98], None, A.mult, None, ["lt", "pk"], ["mx0"])
-        tt(t1, t1, w[:, 81:97], A.add, ["t1", "pk"], ["t1"])
-        tr(mx[:, 96:192], mx[:, 0:96], ["mx0", "mx1"], ["mxt"])
+        scan(ex[:, 47::-1], T.stay[:], w[:, 32:80], A.mult, A.add, ["stay", "hh"], ["ex"])
+        scan(p1, dk, w[:, 1:18], A.add, A.add, ["dk", "mm"], ["p1"])
+        tt(t1, t1, far, A.mult, ["t1", "far"], ["t1"])
         scan(p2, gb, w[:, 0:16], A.add, A.subtract, [G, "mm", "of"], ["p2"], of)
-        scan(mx[:, 192:288], T.k32[:], mx[:, 96:192], A.mult, A.add, ["k32", "mxt"], ["sums"])
+        tr(ex[:, 64:96], ex[:, 0:32], ["ex"], ["ext"])
+        ts(mx[:, 0:64], T.m32[:, 0:64], w[:, 112:113], None, A.mult, None, ["lt", "sl", "p1"], ["mx"])
+        tt(t1, t1, ex[:, 47:31:-1], A.add, ["t1", "ex"], ["t1"])
         tt(p2, p2, nq, A.subtract, ["p2", "nq"], ["p2"])
-        ts(T.offe[:], t1, oh, -2.0, A.add, A.add, ["t1", "sums"], ["offe"])
-        ts(p2, p2, sc, 768 * ETA, A.add, A.add, ["p2", "sums"], ["p2"])
+        scan(ex[:, 96:128], T.k32[:, 64:96], ex[:, 64:96], A.mult, A.add, ["k32", "k16", "ext"], ["oh"])
+        tr(mx[:, 64:128], mx[:, 0:64], ["mx"], ["mxt"])
+        ts(T.offe[:], t1, oh, -1.0, A.add, A.add, ["t1", "oh"], ["offe"])
+        scan(mx[:, 128:192], T.k32[:, 0:64], mx[:, 64:128], A.mult, A.add, ["k32", "mxt"], ["sums"])
+        if OPT["scfirst"]:
+            ts(p2, p2, sc, 768 * ETA, A.add, A.add, ["p2", "sums"], ["p2"])
         cp(T.le[:].indirect(T.offe[:]), T.up[:], ["offe", "up"], ["le"])
-        tt(p2, p2, w[:, 64:80], A.max, ["p2", "pk"], ["p2"])
+        if not OPT["scfirst"]:
+            ts(p2, p2, sc, 768 * ETA, A.add, A.add, ["p2", "sums"], ["p2"])
+        tt(p2, p2, w[:, 96:112], A.max, ["p2", "p1"], ["p2"])
         scan(T.lek[:], T.hold[:, 0:SH], T.le[:, 0:SH], A.add, A.min, ["hold", "le"], ["lek"])
         ts(T.offn[:], p2, om, 1.0 / ETA, A.add, A.mult, ["p2", "sums"], ["offn"])
         ts(T.el[:], T.lek[:, 15:SH:16], -1.0, None, A.add, None, ["lek"], ["el"])
@@ -495,30 +505,42 @@ def rank_program(g, core, T, topo):
             for k in range(2):
                 lin("a", T.idw[:, k:ZO:2], T.le[:, 0:SH], 1.0, -1.0, ["le"], ["id%d" % (k + 1)])
 
-        for b in range(4):
+        zv = OPT["slots"].count("z")
+        for b in range(zv, 4):
             act(T.zt[:, b:512:4], win(b, ZO, TO).indirect(T.el[:, 0:8]), AF.Copy, ["zf%d" % b, "el"], ["zt%d" % b])
-        for b in range(4):
+        mine = list(range(zv))
+
+        def chosen():
+            b = mine.pop()
+            cp(T.zt[:, b:512:4], win(b, ZO, TO).indirect(T.el[:, 0:8]), ["zf%d" % b, "el"], ["zt%d" % b])
+
+        for b in OPT["forder"]:
             act(win(b, 1, ZO, 2), win(b, TO, WN).indirect(T.el[:]), AF.Copy, ["wt%d" % b, "el"], ["wf%d" % b])
             op("g", lambda b=b: g.affine_select(win(b, C, ZO, 2), win(b, C + 1, ZO, 2), [[0, SH - 128]], A.is_ge, 0.0, 0, 0),
                ["wf%d" % b], ["we%d" % b])
-        cp(T.ln[:].indirect(T.offn[:]), T.up[:], ["offn", "up"], ["ln"])
-        ts(T.un[:, 1:C + 1], T.ln[:, 2 * C:3 * C], 0.0, None, A.is_lt, None, ["ln"], ["un"])
-        quant(T.zq[:], T.zs[:], T.zt[:], ["zt0", "zt1", "zt2", "zt3"], ["zq"])
-        for b in range(4):
-            mm(3 + b, 128, T.wq[:, 128 * b:128 * b + 128], T.wsc[:, 128 * b:128 * b + 128], T.zq[:], T.zs[:], ["wq", "wsc", "zq"])
+
+        def layer():
+            quant(T.zq[:], T.zs[:], T.zt[:], ["zt0", "zt1", "zt2", "zt3"], ["zq"])
+            for b in OPT["forder"]:
+                mm(3 + b, 128, T.wq[:, 128 * b:128 * b + 128], T.wsc[:, 128 * b:128 * b + 128], T.zq[:], T.zs[:], ["wq", "wsc", "zq"])
 
         def made(b):
             tt(win(b, 0, C, 2), bank(3 + b, 0, 128), win(b, 1, C, 2), A.add, ["P%d" % (3 + b), "wf%d" % b], ["wm%d" % b])
 
         pair, best, kept = T.ks[:, 0:C], T.ks[:, C:2 * C], T.ks[:, 2 * C:3 * C]
-        scan(pair, T.un[:, 1:C + 1], T.un[:, 0:C], A.add, A.add, ["un", "un0"], ["pair"], -1.0 - TO)
-        scan(best, pair, T.ln[:, 3 * C:4 * C], A.max, A.max, ["pair", "ln"], ["best"], -1024.0)
-        scan(kept, T.hold[:], best, A.add, A.min, ["hold", "best"], ["kept"])
-        made(0)
-        ts(T.nlist[:], T.ks[:, 2 * C + 15:3 * C:16], TO - 1.0, None, A.add, None, ["kept"], ["nlist"])
-        made(1)
-        made(2)
-        made(3)
+        steps = {
+            "s": lambda: cp(T.ln[:].indirect(T.offn[:]), T.up[:], ["offn", "up"], ["ln"]),
+            "u": lambda: ts(T.un[:, 1:C + 1], T.ln[:, 2 * C:3 * C], 0.0, None, A.is_lt, None, ["ln"], ["un"]),
+            "p": lambda: scan(pair, T.un[:, 1:C + 1], T.un[:, 0:C], A.add, A.add, ["un", "un0"], ["pair"], -1.0 - TO),
+            "b": lambda: scan(best, pair, T.ln[:, 3 * C:4 * C], A.max, A.max, ["pair", "ln"], ["best"], -1024.0),
+            "k": lambda: scan(kept, T.hold[:], best, A.add, A.min, ["hold", "best"], ["kept"]),
+            "n": lambda: ts(T.nlist[:], T.ks[:, 2 * C + 15:3 * C:16], TO - 1.0, None, A.add, None, ["kept"], ["nlist"]),
+            "q": layer, "z": chosen}
+        for x in OPT["slots"]:
+            if x in "0123":
+                made(OPT["forder"][int(x)])
+            else:
+                steps[x]()
 
         def take(q, b, a, e):
             rd = ["wt%d" % b, "wf%d" % b, "we%d" % b, "wm%d" % b, "zf%d" % b, "nlist"]
@@ -534,19 +556,14 @@ def rank_program(g, core, T, topo):
             quant(T["xq%d" % n][:, 16 * a:16 * e], T["xs%d" % n][:, 16 * a:16 * e], T.xt[:, 64 * a:64 * e],
                   ["xt%d_%d" % (b, k) for b in range(4) for k in range(a // 2, e // 2)], ["xq%d" % n if e == 16 else "xh"])
 
-        vs = OPT["vsplit"]
         if last and OPT["tail"]:
             for a in (0, 8):
-                for b in range(4):
-                    take("a" if b < 2 else "v", b, a, a + 8)
+                for q, b in OPT["ftail"]:
+                    take(q, b, a, a + 8)
                 state(a, a + 8)
         else:
-            take("a", 0, 0, 16)
-            take("a", 1, 0, 16)
-            if vs:
-                take("a", 2, 0, vs)
-            take("v", 2, vs, 16)
-            take("v", 3, 0, 16)
+            for q, b, a, e in OPT["final"]:
+                take(q, b, a, e)
             state(0, 16)
 
     whole = ["xq3", "xh"]

@@ -1,9 +1,10 @@
 from concourse.bass import DstId, RemoteDMATransfer
-from concourse.mybir import dt, AluOpType, AxisListType, ActivationFunctionType
+from concourse.mybir import dt, AluOpType, ActivationFunctionType
 
 A = AluOpType
 AF = ActivationFunctionType
 C = 256
+H = 128
 SH = 192
 ZO, TO, WN = 384, 640, 896
 STEPS = [1, 2, 4]
@@ -11,9 +12,9 @@ BIG = 2.0 ** 88
 ETA = 2.0 ** -16
 GAP = 191
 CODE = "float8_e4m3fn_x4"
-OPT = dict(window="bsktrmodvq", forder=(0, 1, 2, 3), slots="szuqpbk0n123", ftail=(("a", 0), ("v", 1), ("a", 2), ("v", 3)),
-           final=(("a", 0, 0, 16), ("v", 1, 0, 16), ("a", 2, 0, 16), ("v", 3, 0, 14), ("a", 3, 14, 16)),
-           fold=1, scfirst=1, lastq=1, order="c13 c12 c11 m c10 c9 c8 c7 q00 c6 c5 c4 c3 c2 q22 c1 s q33 q11 d r11 r10 r9 l0 l1 l2 l3", nss=3, c0=9, vsplit=2, tfirst=1, thr="v", k1="v", tot="v", fx="v", of="v", cut=176, tail=1, padv=(0, 2), small=2)
+OPT = dict(lists="VTBKSMRQDbacOfegdjikhnmlpoqrstuv", slots="szuqpbk01n23", tfirst=1, padv=(0, 2), c0=9, su=(15, 14, 13), sx=(15, 14, 13), eq=4,
+           end="aU0 vU1 aU2 vU3 aL0 aL2 vL1 QU vL3 QL", head="",
+           order="aU0 vU1 aU2 vU3 aL0 aL2 vL1 QU vL3 QL o nU pU nL SU x10 u10 u9 x12 iU pL u12 x11 x9 iL u11 c5 c7 x8 q0l c6 q0u c4 c2 q2 c1 c3 q3u q3l q1 SR l1 l3 l0 r9 l2 d eU eL b")
 
 
 def sb(n, d):
@@ -37,11 +38,11 @@ SCRATCH = {
     "kd": sb(256, "bfloat16"), "k2": sb(256, "bfloat16"),
     "m32": sb(96, "bfloat16"), "k32": sb(96, "bfloat16"),
     "cidx": sb(96, "float32"), "uoff": sb(8, "uint16"),
-    "m1": sb(256, "float32"), "tq": sb(256, "float32"), "sg": sb(1280, "bfloat16"), "junk": sb(1280, "bfloat16"),
-    "r1": sb(16, "float32"), "rs": sb(2944, "bfloat16"), "dsc": sb(256, "bfloat16"), "csc": sb(256, "float32"),
+    "m1": sb(256, "float32"), "tq": sb(256, "float32"), "sg": sb(2048, "bfloat16"), "junk": sb(2048, "bfloat16"),
+    "r1": sb(32, "float32"), "rs": sb(2944, "bfloat16"), "dsc": sb(256, "bfloat16"), "csc": sb(256, "float32"),
     "ua": sb(32, "float32"), "i32": sb(32, "bfloat16"), "o32": sb(96, "bfloat16"),
     "gm": sb(192, "bfloat16"), "fx": sb(128, "bfloat16"), "gl": sb(96, "bfloat16"),
-    "own": sb(192, "float32"), "w": sb(192, "float32"), "mx": sb(192, "bfloat16"), "ex": sb(128, "bfloat16"), "stay": sb(48, "bfloat16"),
+    "own": sb(96, "float32"), "w": sb(192, "float32"), "mx": sb(192, "bfloat16"), "ex": sb(128, "bfloat16"), "stay": sb(48, "bfloat16"),
     "offe": sb(16, "uint16"), "le": sb(768, "bfloat16"), "lek": sb(SH, "bfloat16"), "el": sb(12, "uint16"),
     "offn": sb(16, "uint16"), "ln": sb(1024, "bfloat16"), "un": sb(272, "bfloat16"), "ks": sb(3 * C, "float16"),
     "nlist": sb(16, "uint16"),
@@ -167,12 +168,6 @@ def rank_program(g, core, T, topo):
         else:
             ts(out, a, scale, bias, A.mult, A.add, rd, wr)
 
-    def total(q, out, a, spare, rd, wr):
-        if q == "a":
-            act(spare, a, AF.Copy, rd, wr + ["spare"], accum_out=out)
-        else:
-            op("v", lambda: V.tensor_reduce(out, a, AxisListType.X, A.add), rd, wr)
-
     def mm(bank, n, lq, ls, rq, rs, rd, start=True, stop=True, ext=()):
         op("p", lambda: PE.matmul_mx(T.ps[:, 512 * bank:512 * bank + n], lq, ls, rq, rs, start, stop),
            rd, ["P%d" % bank], ext)
@@ -184,7 +179,7 @@ def rank_program(g, core, T, topo):
         return T.ps[:, 512 * k + a:512 * k + b]
 
     def dma(q, out, a, rd, wr):
-        eng = {"s": g.sync, "a": g.scalar, "g": g}[q]
+        eng = {"s": g.sync, "a": g.scalar}[q]
         op(q, lambda: eng.dma_start(out, a), rd, wr, (), "dma")
 
     def iota(out, pat, base, mult, wr, small=True):
@@ -196,28 +191,25 @@ def rank_program(g, core, T, topo):
     def win(b, a, e, step=1):
         return T.win[:, WN * b + a:WN * b + e:step]
 
-    nss, c0, cut = OPT["nss"], OPT["c0"], OPT["cut"]
-    both = list(range(15, 15 - nss, -1))
-    rest = [c for c in (13, 12, 11, 10, 9) if c not in both]
+    c0, su, sx = OPT["c0"], OPT["su"], OPT["sx"]
     lanes = [[0, 11, 10, 9], [1, 2, 3, 4], [5, 6, 7, 8], [15, 14, 13, 12]]
-    MW = [256, 128, 128, 240]
+    MW = [256, 128, 128, 256]
     MO = [0, 256, 384, 512]
+    half = {"U": (H, C), "L": (0, H)}
 
-    def slot(c, n):
+    def slot(c, a, e):
         k = [c in x for x in lanes].index(True)
         t = lanes[k].index(c)
-        return T.mt[:, 4 * MO[k] + t:4 * (MO[k] + n):4]
-
-    def blocks(k):
-        return ["m%d" % c for c in lanes[k]]
+        return T.mt[:, 4 * (MO[k] + a) + t:4 * (MO[k] + e):4]
 
     def pad(k):
         a = 16 * min(c if c else 16 for c in lanes[k])
         out = T.mt[:, 4 * (MO[k] + a):4 * (MO[k] + MW[k])]
+        wr = ["m%s%d" % ("U" if MW[k] == C else "L", c) for c in lanes[k]]
         if k in OPT["padv"]:
-            fill(out, 0.0, blocks(k))
+            fill(out, 0.0, wr)
         else:
-            act(out, T.et[:, 0:4 * (MW[k] - a)], AF.Copy, ["et"], blocks(k), scale=0.0)
+            act(out, T.et[:, 0:4 * (MW[k] - a)], AF.Copy, ["et"], wr, scale=0.0)
 
     def summed(c):
         return C + GAP * (c - 1)
@@ -227,9 +219,10 @@ def rank_program(g, core, T, topo):
 
     gone = [0]
 
-    dma("a", T.ut[:], T.u[:], [], ["ut"])
-    dma("s", T.xin[:], T.x[:], [], ["x0"])
-    dma("s", T.wq[:].bitcast(dt.uint8), T.wc[:], ["x0"], ["wq"])
+    dma("s", T.ut[:], T.u[:], [], ["ut"])
+    dma("s", T.xin[:, 4 * H:4 * C], T.x[:, 4 * H:4 * C], [], ["xU"])
+    dma("s", T.xin[:, 0:4 * H], T.x[:, 0:4 * H], [], ["xL"])
+    dma("s", T.wq[:].bitcast(dt.uint8), T.wc[:], ["xU", "xL"], ["wq"])
     dma("s", T.wsc[:], T.ws[:], [], ["wsc"])
     dma("s", T.vt[:], T.v[:], [], ["vt"])
 
@@ -243,6 +236,7 @@ def rank_program(g, core, T, topo):
     for k, bits in enumerate([15, 112, 16]):
         ts(T.pi[:, 1 + k:2 + k], T.pi[:, 0:1], bits, None, A.bitwise_and, None, ["pi0"], ["pi%d" % (k + 1)])
     fill(T.rs[:, summed(0):summed(0) + 1], 0.0, ["r0"])
+    fill(T.gm[:], 0.0, ["gm0", "gm1", "gm2"])
     cp(T.pf[:, 0:3], T.pi[:, 1:4], ["pi1", "pi2", "pi3"], ["pf"])
     rr, gp, par = T.pf[:, 0:1], T.pf[:, 1:2], T.pf[:, 2:3]
 
@@ -250,37 +244,44 @@ def rank_program(g, core, T, topo):
         lin(q, T.pf[:, k:k + 1], src, scale, bias, ["pf"] + list(rd), ["pf%d" % k])
         return T.pf[:, k:k + 1]
 
-    fill(T.gm[:], 0.0, ["gm0", "gm1", "gm2"])
+    pad(0)
     nbig = column("v", 3, rr, -BIG, 0.0)
     hbias = column("v", 4, rr, 64 * BIG, 64 * BIG)
     ts(T.uoff[:], T.yy[:, 0:8], 16.0, None, A.mult, None, ["yy"], ["uoff"])
+    unit = ETA / 128
+    scale = [column("a", 6, par, -unit / 16, unit), column("a", 7, par, unit / 16, 0.0)]
+    column("a", 5, rr, -1025.0, 15375.5 + 32768)
     act(T.bigm[:], T.yy[:], AF.Abs, ["yy", "pf3"], ["bigm"], scale=BIG, bias=nbig)
+    shift = [column("a", 8 + k, T.pf[:, 5:6], scale[k], -128 * ETA, ["pf5", "pf%d" % (6 + k)]) for k in range(2)]
     act(T.hold[:], T.yy[:], AF.Relu, ["yy", "pf4"], ["hold"], scale=-64 * BIG, bias=hbias)
-    pad(0)
     pad(2)
+    pad(3)
 
     def packed_unit(b):
         quant(T.eq[:, 128 * b:128 * b + 128], T.es[:, 128 * b:128 * b + 128], T.et[:, 3 - b:515 - b], ["et"], ["eq%d" % b])
 
-    packed_unit(0)
+    def state(n, s):
+        a, e = half[s]
+        src, rd = (T.xin, ["x" + s]) if n == 0 else (T.xt, ["xt%s%d" % (s, b) for b in range(4)])
+        quant(T["xq%d" % n][:, a:e], T["xs%d" % n][:, a:e], src[:, 4 * a:4 * e], rd, ["xq%d%s" % (n, s)])
+
+    for b in range(OPT["eq"]):
+        packed_unit(b)
     quant(T.uq[:], T.us[:], T.ut[:], ["ut"], ["uq"])
-    packed_unit(1)
+    state(0, "U")
     op("v", lambda: V.tensor_copy(T.uq2[:].bitcast(dt.uint32), T.uq[:].bitcast(dt.uint32).indirect(T.uoff[:])),
        ["uq", "uoff"], ["uq2"])
-    packed_unit(2)
-    packed_unit(3)
+    state(0, "L")
+    for b in range(OPT["eq"], 4):
+        packed_unit(b)
     act(T.us2[:], T.us[:].indirect(T.uoff[:]), AF.Copy, ["uq", "uoff"], ["us2"])
     pad(1)
-    pad(3)
     act(T.drop[:], T.hold[:], AF.Identity, ["hold"], ["drop"], scale=2.0 ** -76, bias=-1024.0)
-    unit = ETA / 128
-    scale = [column("a", 6, par, -unit / 16, unit), column("a", 7, par, unit / 16, 0.0)]
-    column("a", 5, rr, -1025.0, 15375.5 + 32768)
-    shift = [column("a", 8 + k, T.pf[:, 5:6], scale[k], -128 * ETA, ["pf5", "pf%d" % (6 + k)]) for k in range(2)]
-    quant(T.xq0[:], T.xs0[:], T.xin[:], ["x0"], ["xq0"])
-    for t in range(4):
-        ts(T.ot[:, t:512:4], T.g16[:], gp, None, A.is_equal, None, ["g16", "pf"], ["ot%d" % t])
-    quant(T.oq[:], T.osb[:], T.ot[:], ["ot0", "ot1", "ot2", "ot3"], ["oq"])
+
+    def ones():
+        for t in range(4):
+            ts(T.ot[:, t:512:4], T.g16[:], gp, None, A.is_equal, None, ["g16", "pf"], ["ot%d" % t])
+        quant(T.oq[:], T.osb[:], T.ot[:], ["ot0", "ot1", "ot2", "ot3"], ["oq"])
 
     lt, same, far, ieta = T.m32[:, 0:32], T.m32[:, 64:96], T.cidx[:, 48:64], T.cidx[:, 64:80]
 
@@ -296,128 +297,180 @@ def rank_program(g, core, T, topo):
     masks = [lambda: ts(same, T.g16[:, 0:32], par, None, A.is_equal, None, ["g16", "pf"], ["same"]),
              lambda: ts(lt, T.yy[:, 0:32], rr, None, A.is_gt, None, ["yy", "pf"], ["lt"]),
              lambda: tt(lt, lt, same, A.mult, ["lt", "same"], ["lt"]),
+             lambda: ts(T.stay[:], T.stay[:], T.pf[:, 12:13], None, A.is_lt, None, ["stay", "pf12"], ["stay"]),
              lambda: lin("v", T.m32[:, 32:64], lt, -2.0, 0.0, ["lt"], ["sl"]),
-             lambda: tt(T.m32[:, 32:64], T.m32[:, 32:64], same, A.add, ["sl", "same"], ["sl"]),
-             lambda: ts(T.stay[:], T.stay[:], T.pf[:, 12:13], None, A.is_lt, None, ["stay", "pf12"], ["stay"])]
+             lambda: tt(T.m32[:, 32:64], T.m32[:, 32:64], same, A.add, ["sl", "same"], ["sl"])]
 
     def beside():
         if masks:
             masks.pop(0)()
+
+    def take(q, b, s):
+        a, e = half[s]
+        rd = ["wt%d" % b, "wf%d" % b, "we%d" % b, "wm%d" % b, "zf%d" % b, "nlist"]
+        out, src = T.xt[:, 4 * a + b:4 * e:4], win(b, 0, WN).indirect(T.nlist[:, a // 16:e // 16])
+        if q == "a":
+            act(out, src, AF.Copy, rd, ["xt%s%d" % (s, b)], scale=1.0 / 64)
+        else:
+            ts(out, src, 1.0 / 64, None, A.mult, None, rd, ["xt%s%d" % (s, b)])
+
+    mine, theirs, sums = {"U": 2, "L": 0}, {"U": 1, "L": 7}, {"U": 2, "L": 1}
+    tb = [7, 2, 0, 1]
 
     for rnd, h in enumerate(STEPS):
         mate = T.cores[rank ^ h]
         rid, pid, _ = topo.addr(mate)
         eng = topo.engines(core, mate)
         xq, xs, pq, pz = T["xq%d" % rnd], T["xs%d" % rnd], T["pq%d" % rnd], T["pz%d" % rnd]
-        X = "xq%d" % rnd
+        X = ["xq%dU" % rnd, "xq%dL" % rnd]
         last = rnd == len(STEPS) - 1
 
         def send(out, a, sem, rd, pid=pid, rid=rid, eng=eng):
             op("g", lambda: g.remote_dma(out, a, T.sem[sem], T.sem.gone, pid, rid, maskof(eng)), rd, [], (), "far")
             gone[0] += len(eng)
 
-        send(pq[:].bitcast(dt.uint8), xq[:].bitcast(dt.uint8), "aq%d" % rnd, [X])
-        send(pz[:], xs[:], "aq%d" % rnd, [X])
-        if rnd == 0:
-            iota(T.k2[:, 0:128], [[-4096, 128]], 127 * 4096, 0, ["k2a"])
-            iota(T.k2[:, 128:256], [[0, 128]], 4096, 0, ["k2b"])
-            iota(T.stay[:], [[1, 48]], 0, 0, ["stay"])
-            iota(T.k32[:], [[0, 3], [1, 32]], 0, 0, ["k32"])
-            iota(T.own[:, 0:18], [[0, 18]], 0, 0, ["kb"])
-            iota(T.w[:, 0:80], [[0, 80]], 0, 0, ["mm", "hh"])
-            iota(T.un[:, 0:1], [[0, 1]], 1, 0, ["un0"])
-        iota(T.le[:, 128:SH], [[0, SH - 128]], C, 0, ["le"])
-        if rnd > 0:
-            iota(T.ln[:, 2 * C:4 * C], [[0, 2 * C]], -1024, 0, ["ln"])
-        if last:
-            iota(T.idw[:, ZO:WN], [[1, WN - ZO]], ZO - TO, 0, ["id0"])
+        def scores(s):
+            a, e = half[s]
+            if rnd > 0:
+                state(rnd, s)
+            for k in (mine[s], theirs[s]):
+                if k == mine[s] or s == "U" or sx:
+                    mm(k, H, T.uq2[:], T.us2[:], xq[:, a:e], xs[:, a:e], ["uq2", "us2", "xq%d%s" % (rnd, s)])
+            if s == "U":
+                return
+            for b in range(4):
+                unpack(3 + b, b, xq[:], xs[:], X)
+            send(pq[:].bitcast(dt.uint8), xq[:].bitcast(dt.uint8), "aq%d" % rnd, X)
+            send(pz[:], xs[:], "aq%d" % rnd, X)
+            if rnd == 0:
+                iota(T.k2[:, 0:128], [[-4096, 128]], 127 * 4096, 0, ["k2a"])
+                iota(T.k2[:, 128:256], [[0, 128]], 4096, 0, ["k2b"])
+                iota(T.stay[:], [[1, 48]], 0, 0, ["stay"])
+                iota(T.k32[:], [[0, 3], [1, 32]], 0, 0, ["k32"])
+                iota(T.own[:, 0:18], [[0, 18]], 0, 0, ["kb"])
+                iota(T.w[:, 0:80], [[0, 80]], 0, 0, ["mm", "hh"])
+                iota(T.un[:, 0:1], [[0, 1]], 1, 0, ["un0"])
+            iota(T.le[:, 128:SH], [[0, SH - 128]], C, 0, ["le"])
+            if rnd > 0:
+                iota(T.ln[:, 2 * C:4 * C], [[0, 2 * C]], -1024, 0, ["ln"])
+            if last:
+                iota(T.idw[:, ZO:WN], [[1, WN - ZO]], ZO - TO, 0, ["id0"])
 
-        mm(0, C, T.uq2[:], T.us2[:], xq[:], xs[:], ["uq2", "us2", X])
-        mm(1, C, T.uq2[:], T.us2[:], xq[:], xs[:], ["uq2", "us2", X])
-        for b in range(4):
-            unpack(3 + b, b, xq[:], xs[:], [X])
-        halves = [(cut, C), (0, cut)]
-        for a, e in halves:
-            tt(T.m1[:, a:e], bank(0, a, e), T.bigm[:, a:e], A.add, ["P0", "bigm"], ["m1%d" % a])
-        for a, e in halves:
-            scan(T.tq[:, a:e], T.hold[:, a:e], T.m1[:, a:e], A.add, A.min, ["hold", "m1%d" % a], ["tq%d" % a])
+        def masked(s):
+            a, e = half[s]
+            tt(T.m1[:, a:e], bank(mine[s], 0, H), T.bigm[:, a:e], A.add, ["P%d" % mine[s], "bigm"], ["m1" + s])
+
+        def pivots(s):
+            a, e = half[s]
+            scan(T.tq[:, a:e], T.hold[:, a:e], T.m1[:, a:e], A.add, A.min, ["hold", "m1" + s], ["tq" + s])
+
+        def inside(s):
+            a, e = half[s]
+            tt(slot(0, a, e), bank(mine[s], 0, H), T.tq[:, a:e], A.is_gt, ["P%d" % mine[s], "tq" + s], ["m%s0" % s])
 
         def pivot(c):
-            return T.tq[:, 16 * c + 15:16 * c + 16], "tq%d" % (cut if 16 * c >= cut else 0)
+            return T.tq[:, 16 * c + 15:16 * c + 16], "tqU" if c >= 8 else "tqL"
 
-        def compare(c):
-            ts(slot(c, 16 * c), bank(0, 0, 16 * c), pivot(c)[0], None, A.is_ge, None, ["P0", pivot(c)[1]], ["m%d" % c])
+        def rows(c, s):
+            return half[s][0], min(half[s][1], 16 * c)
+
+        def compare(c, s):
+            a, e = rows(c, s)
+            ts(slot(c, a, e), bank(mine[s], 0, e - a), pivot(c)[0], None, A.is_ge, None, ["P%d" % mine[s], pivot(c)[1]], ["m%s%d" % (s, c)])
+
+        def signs(c, s):
+            a, e = rows(c, s)
+            act(T.sg[:, C * (15 - c) + a:C * (15 - c) + e], bank(theirs[s], 0, e - a), AF.Sign, ["P%d" % theirs[s], pivot(c)[1]],
+                ["sg%s%d" % (s, c)], bias=pivot(c)[0], scale=-1.0)
+
+        def beaten(c):
+            a, e, ss = (0, 16 * c, "UL") if c in sx else (H, 16 * c, "U")
+            more = dict(accum_out=T.r1[:, c:c + 1]) if c in sx else {}
+            act(slot(c, a, e), T.sg[:, C * (15 - c) + a:C * (15 - c) + e], AF.Sign, ["sg%s%d" % (s, c) for s in ss],
+                ["m%s%d" % (s, c) for s in ss] + ["q%d" % c], bias=1.0, scale=-1.0, **more)
+
+        def by_scalar():
+            for c in su:
+                signs(c, "U")
+            for c in su:
+                if c not in sx:
+                    beaten(c)
+            for c in sx:
+                signs(c, "L")
+            for c in sx:
+                beaten(c)
+
+        def scalar_sums():
+            for c in range(15, c0 - 1, -1):
+                if c not in sx:
+                    act(T.junk[:, 8 * c * (c - 1):8 * c * (c + 1)], slot(c, 0, 16 * c), AF.Copy, ["mL%d" % c, "mU%d" % c], ["q%d" % c],
+                        accum_out=T.r1[:, c:c + 1])
+            act(T.rs[:, summed(c0):summed(15) + 1:GAP], T.r1[:, c0:16], AF.Copy, ["q%d" % c for c in range(c0, 16)],
+                ["r%d" % c for c in range(c0, 16)])
 
         def rowsum(c):
-            if c >= c0:
-                act(T.junk[:, C * (c - 9):C * (c - 9) + 16 * c], slot(c, 16 * c), AF.Copy, ["m%d" % c], ["q%d" % c], accum_out=T.r1[:, c:c + 1])
-            else:
-                scan(T.rs[:, summed(c) + 1 - 16 * c:summed(c) + 1], slot(c, 16 * c), slot(c, 16 * c), A.add, A.max, ["m%d" % c], ["r%d" % c])
+            if c < c0:
+                scan(T.rs[:, summed(c) + 1 - 16 * c:summed(c) + 1], slot(c, 0, 16 * c), slot(c, 0, 16 * c), A.add, A.max,
+                     ["mL%d" % c, "mU%d" % c], ["r%d" % c])
 
         def rowsums(t):
+            if 5 + t >= c0:
+                return rowsum(1 + t)
             scan(T.rs[:, GAP * t:GAP * t + 4 * C - 3:4], T.mt[:, 4 * MO[1] + t:4 * MO[3]:4], T.k2[:], A.add, A.min,
-                 ["m%d" % (1 + t), "m%d" % (5 + t), "k2a", "k2b"], ["r%d" % (1 + t), "r%d" % (5 + t)])
+                 ["mL%d" % (1 + t), "mL%d" % (5 + t), "k2a", "k2b"], ["r%d" % (1 + t), "r%d" % (5 + t)])
 
-        def packed(k0, k1):
-            a, b = MO[k0], MO[k1] + MW[k1]
-            quant(T.mq[:, a:b], T.ms[:, a:b], T.mt[:, 4 * a:4 * b], sum([blocks(k) for k in range(k0, k1 + 1)], []),
-                  ["mq%d" % k for k in range(k0, k1 + 1)])
-            for k in range(k0, k1 + 1):
-                a, b = MO[k], MO[k] + MW[k]
-                mm(2, MW[k], T.oq[:], T.osb[:], T.mq[:, a:b], T.ms[:, a:b], ["oq", "mq%d" % k], k == 0, k == OPT["lastq"])
+        done = {"U": 0, "L": 0}
+
+        def packed(k, s):
+            a = MO[k] + half[s][0]
+            quant(T.mq[:, a:a + H], T.ms[:, a:a + H], T.mt[:, 4 * a:4 * (a + H)], ["m%s%d" % (s, c) for c in lanes[k]], ["mq%d%s" % (k, s)])
+            done[s] += 1
+            mm(sums[s], H, T.oq[:], T.osb[:], T.mq[:, a:a + H], T.ms[:, a:a + H], ["oq", "mq%d%s" % (k, s)],
+               done[s] == 1, done[s] == (2 if s == "U" else 4))
 
         def own_copy(b):
             act(win(b, TO, WN), bank(3 + b, 0, C), AF.Copy, ["P%d" % (3 + b)], ["wt%d" % b], scale=64.0)
 
-        def signs(c):
-            act(T.sg[:, C * (15 - c):C * (15 - c) + 16 * c], bank(1, 0, 16 * c), AF.Sign, ["P1", pivot(c)[1]], ["sg%d" % c], bias=pivot(c)[0], scale=-1.0)
+        def column_sums(s):
+            a, e = half[s]
+            scan(T.csc[:, a:e], T.drop[:, a:e], bank(sums[s], 0, H), A.add, A.min, ["drop", "P%d" % sums[s]], ["csc" + s])
 
-        def beaten(c):
-            act(slot(c, 16 * c), T.sg[:, C * (15 - c):C * (15 - c) + 16 * c], AF.Sign, ["sg%d" % c], ["m%d" % c, "q%d" % c],
-                bias=1.0, scale=-1.0, accum_out=T.r1[:, c:c + 1])
-
-        if nss == 5:
-            signs(15), signs(11), signs(14), beaten(11), signs(13), signs(12)
-            for c in both[:4]:
-                beaten(c)
-        else:
-            for c in both:
-                signs(c)
-            for c in both:
-                beaten(c)
-        def inside():
-            tt(slot(0, C), bank(0, 0, C), T.tq[:], A.is_gt, ["P0", "tq0", "tq%d" % cut], ["m0"])
-
-        def inside_sums():
-            scan(T.dsc[:], slot(0, C), T.kd[:], A.add, A.min, ["kd", "m0"], ["dsc"])
-
-        def by_scalar():
-            for c in rest:
-                if c >= c0:
-                    rowsum(c)
-            act(T.rs[:, summed(c0):summed(15) + 1:GAP], T.r1[:, c0:16], AF.Copy, ["q%d" % c for c in range(c0, 16)], ["r%d" % c for c in range(c0, 16)])
-
-        for x in OPT["order"].split():
-            k = int(x[1:] or 0)
-            if x[0] == "c":
-                if k in rest or k < 9:
-                    compare(k)
-            elif x[0] == "r":
-                if k < c0:
-                    rowsum(k)
-            elif x[0] == "q":
-                packed(k // 10, k % 10)
-            else:
-                {"m": inside, "d": inside_sums, "s": by_scalar, "l": lambda: rowsums(k)}[x[0]]()
         ub, rk = T.ua[:, 0:16], T.ua[:, 16:32]
-        tt(ub, T.dsc[:, 15:C:16], T.rs[:, summed(0):summed(15) + 1:GAP], A.add, ["dsc"] + ["r%d" % c for c in range(16)], ["ub"])
-        scan(T.csc[:], T.drop[:], bank(2, 0, C), A.add, A.min, ["drop", "P2"], ["csc"])
+        for x in OPT["head"].split() + OPT["order"].split():
+            if x[0] in "av":
+                if rnd > 0:
+                    take(x[0], int(x[2]), x[1])
+            elif x[0] in "Qnpie":
+                {"Q": scores, "n": masked, "p": pivots, "i": inside, "e": column_sums}[x[0]](x[1])
+            elif x[0] in "xc":
+                if int(x[1:]) not in sx:
+                    compare(int(x[1:]), "L")
+            elif x[0] == "u":
+                if int(x[1:]) not in su:
+                    compare(int(x[1:]), "U")
+            elif x[0] == "q":
+                packed(int(x[1]), x[2:].upper() or "L")
+            elif x[0] == "r":
+                rowsum(int(x[1:]))
+            elif x[0] == "l":
+                rowsums(int(x[1:]))
+            elif x == "d":
+                scan(T.dsc[:], slot(0, 0, C), T.kd[:], A.add, A.min, ["kd", "mU0", "mL0"], ["dsc"])
+            elif x == "b":
+                tt(ub, T.dsc[:, 15:C:16], T.rs[:, summed(0):summed(15) + 1:GAP], A.add, ["dsc"] + ["r%d" % c for c in range(16)], ["ub"])
+            elif x == "o":
+                if rnd == 0:
+                    ones()
+            elif x == "SU":
+                by_scalar()
+            elif x == "SR":
+                scalar_sums()
         for b in range(OPT["tfirst"]):
             own_copy(b)
         if rnd == 0:
             later_constants()
         beside()
-        tt(rk, T.csc[:, 15:C:16], ub, A.subtract, ["csc", "ub"], ["rk"])
+        tt(rk, T.csc[:, 15:C:16], ub, A.subtract, ["cscU", "cscL", "ub"], ["rk"])
         beside()
         for k in range(2):
             ts(T.i32[:, 16 * k:16 * k + 16], rk, scale[k], shift[k], A.mult, A.add, ["rk", "pf6", "pf7", "pf8", "pf9"], ["i32%d" % k])
@@ -429,18 +482,14 @@ def rank_program(g, core, T, topo):
         lo, hi = T.o32[:, 32 * rnd:32 * rnd + 16], T.o32[:, 32 * rnd + 16:32 * rnd + 32]
         tt(gm, lo, hi, A.add, ["o%d" % rnd], [G])
         beside()
-        if OPT["fold"]:
-            fold = RemoteDMATransfer(dst_ids=[DstId(rid=rid, pnc=pid)], dma_engine_mask=maskof(eng), remote_sem=T.sem["af%d" % rnd],
-                                     srcs=[lo, hi], dsts=[gl], alu_op=1)
-            op("g", lambda fold=fold: g.remote_dma_fused([fold], local_sem=T.sem.gone), ["o%d" % rnd], [], (), "far")
-            gone[0] += len(eng)
-        else:
-            send(gl, gm, "af%d" % rnd, [G])
+        fold = RemoteDMATransfer(dst_ids=[DstId(rid=rid, pnc=pid)], dma_engine_mask=maskof(eng), remote_sem=T.sem["af%d" % rnd],
+                                 srcs=[lo, hi], dsts=[gl], alu_op=1)
+        op("g", lambda fold=fold: g.remote_dma_fused([fold], local_sem=T.sem.gone), ["o%d" % rnd], [], (), "far")
+        gone[0] += len(eng)
         if rnd == 0:
             iota(T.up[:], [[1, 16], [16, 16]], 1, 0, ["up"])
             iota(T.ln[:, 2 * C:4 * C], [[0, 2 * C]], -1024, 0, ["ln"])
 
-        tb = [7, 1, 0, 2]
         o, fx = T.own, T.fx
         kb, dk, thr, of = o[:, 1:17], T.cidx[:, 0:17], o[:, 64:80], fx[:, 127:128]
         for b in range(4):
@@ -448,7 +497,7 @@ def rank_program(g, core, T, topo):
         for b in range(4):
             act(T.tp[:, b:1024:4], bank(tb[b], 0, C), AF.Copy, ["P%d" % tb[b]], ["tp%d" % b], scale=-1.0)
         for b in range(4):
-            unpack(tb[b], b, xq[:], xs[:], [X], True, False)
+            unpack(tb[b], b, xq[:], xs[:], X, True, False)
         for b in range(OPT["tfirst"], 4):
             own_copy(b)
 
@@ -469,38 +518,42 @@ def rank_program(g, core, T, topo):
             "o": lambda: scan(fx[:, 96:128], T.k32[:, 64:96], fx[:, 64:96], A.mult, A.add, ["k32", "k16", "fxt"], ["of"]),
             "v": lambda: rnd == 1 and quant(T.vq[:], T.vs[:], T.vt[:], ["vt"], ["vq"]),
             "b": beside, "q": difference}
-        for x in OPT["window"]:
-            steps[x]()
+        waiting = steps
 
         w, mx, ex = T.w, T.mx, T.ex
         mm_, hh = w[:, 1:17], w[:, 32:48]
         t1, nq, p2, p1 = w[:, 128:144], w[:, 144:160], w[:, 160:176], w[:, 96:113]
         oh, om, sc = ex[:, 127:128], mx[:, 159:160], mx[:, 191:192]
-        tt(hh, gl, thr, A.is_gt, ["thr"], ["hh"], ext=[("af%d" % rnd, len(eng))])
-        tt(mm_, gm, gl, A.min, [G], ["mm"])
-        tt(t1, gl, thr, A.is_le, ["thr"], ["t1"])
-        tt(nq, gl, gm, A.is_ge, [G], ["nq"])
-        scan(ex[:, 47::-1], T.stay[:], w[:, 32:80], A.mult, A.add, ["stay", "hh"], ["ex"])
-        scan(p1, dk, w[:, 1:18], A.add, A.add, ["dk", "mm"], ["p1"])
-        tt(t1, t1, far, A.mult, ["t1", "far"], ["t1"])
-        scan(p2, gb, w[:, 0:16], A.add, A.subtract, [G, "mm", "of"], ["p2"], of)
-        tr(ex[:, 64:96], ex[:, 0:32], ["ex"], ["ext"])
-        ts(mx[:, 0:64], T.m32[:, 0:64], w[:, 112:113], None, A.mult, None, ["lt", "sl", "p1"], ["mx"])
-        tt(t1, t1, ex[:, 47:31:-1], A.add, ["t1", "ex"], ["t1"])
-        tt(p2, p2, nq, A.subtract, ["p2", "nq"], ["p2"])
-        scan(ex[:, 96:128], T.k32[:, 64:96], ex[:, 64:96], A.mult, A.add, ["k32", "k16", "ext"], ["oh"])
-        tr(mx[:, 64:128], mx[:, 0:64], ["mx"], ["mxt"])
-        ts(T.offe[:], t1, oh, -1.0, A.add, A.add, ["t1", "oh"], ["offe"])
-        scan(mx[:, 128:192], T.k32[:, 0:64], mx[:, 64:128], A.mult, A.add, ["k32", "mxt"], ["sums"])
-        if OPT["scfirst"]:
-            ts(p2, p2, sc, 768 * ETA, A.add, A.add, ["p2", "sums"], ["p2"])
-        cp(T.le[:].indirect(T.offe[:]), T.up[:], ["offe", "up"], ["le"])
-        if not OPT["scfirst"]:
-            ts(p2, p2, sc, 768 * ETA, A.add, A.add, ["p2", "sums"], ["p2"])
-        tt(p2, p2, w[:, 96:112], A.max, ["p2", "p1"], ["p2"])
-        scan(T.lek[:], T.hold[:, 0:SH], T.le[:, 0:SH], A.add, A.min, ["hold", "le"], ["lek"])
-        ts(T.offn[:], p2, om, 1.0 / ETA, A.add, A.mult, ["p2", "sums"], ["offn"])
-        ts(T.el[:], T.lek[:, 15:SH:16], -1.0, None, A.add, None, ["lek"], ["el"])
+        came = [[("af%d" % rnd, len(eng))]]
+
+        def arrived():
+            return came.pop() if came else []
+
+        steps = {
+            "a": lambda: tt(hh, gl, thr, A.is_gt, ["thr"], ["hh"], ext=arrived()),
+            "b": lambda: tt(mm_, gm, gl, A.min, [G], ["mm"], ext=arrived()),
+            "c": lambda: tt(t1, gl, thr, A.is_le, ["thr"], ["t1"], ext=arrived()),
+            "d": lambda: tt(nq, gl, gm, A.is_ge, [G], ["nq"], ext=arrived()),
+            "e": lambda: scan(ex[:, 47::-1], T.stay[:], w[:, 32:80], A.mult, A.add, ["stay", "hh"], ["ex"]),
+            "f": lambda: scan(p1, dk, w[:, 1:18], A.add, A.add, ["dk", "mm"], ["p1"]),
+            "g": lambda: tt(t1, t1, far, A.mult, ["t1", "far"], ["t1"]),
+            "h": lambda: scan(p2, gb, w[:, 0:16], A.add, A.subtract, [G, "mm", "of"], ["p2"], of),
+            "i": lambda: tr(ex[:, 64:96], ex[:, 0:32], ["ex"], ["ext"]),
+            "j": lambda: ts(mx[:, 0:64], T.m32[:, 0:64], w[:, 112:113], None, A.mult, None, ["lt", "sl", "p1"], ["mx"]),
+            "k": lambda: tt(t1, t1, ex[:, 47:31:-1], A.add, ["t1", "ex"], ["t1"]),
+            "l": lambda: tt(p2, p2, nq, A.subtract, ["p2", "nq"], ["p2"]),
+            "m": lambda: scan(ex[:, 96:128], T.k32[:, 64:96], ex[:, 64:96], A.mult, A.add, ["k32", "k16", "ext"], ["oh"]),
+            "n": lambda: tr(mx[:, 64:128], mx[:, 0:64], ["mx"], ["mxt"]),
+            "o": lambda: ts(T.offe[:], t1, oh, -1.0, A.add, A.add, ["t1", "oh"], ["offe"]),
+            "p": lambda: scan(mx[:, 128:192], T.k32[:, 0:64], mx[:, 64:128], A.mult, A.add, ["k32", "mxt"], ["sums"]),
+            "q": lambda: ts(p2, p2, sc, 768 * ETA, A.add, A.add, ["p2", "sums"], ["p2"]),
+            "r": lambda: cp(T.le[:].indirect(T.offe[:]), T.up[:], ["offe", "up"], ["le"]),
+            "s": lambda: tt(p2, p2, w[:, 96:112], A.max, ["p2", "p1"], ["p2"]),
+            "t": lambda: scan(T.lek[:], T.hold[:, 0:SH], T.le[:, 0:SH], A.add, A.min, ["hold", "le"], ["lek"]),
+            "u": lambda: ts(T.offn[:], p2, om, 1.0 / ETA, A.add, A.mult, ["p2", "sums"], ["offn"]),
+            "v": lambda: ts(T.el[:], T.lek[:, 15:SH:16], -1.0, None, A.add, None, ["lek"], ["el"])}
+        for x in OPT["lists"]:
+            (steps if x.islower() else waiting)[x.lower()]()
         if last:
             for k in range(2):
                 lin("a", T.idw[:, k:ZO:2], T.le[:, 0:SH], 1.0, -1.0, ["le"], ["id%d" % (k + 1)])
@@ -508,20 +561,20 @@ def rank_program(g, core, T, topo):
         zv = OPT["slots"].count("z")
         for b in range(zv, 4):
             act(T.zt[:, b:512:4], win(b, ZO, TO).indirect(T.el[:, 0:8]), AF.Copy, ["zf%d" % b, "el"], ["zt%d" % b])
-        mine = list(range(zv))
+        here = list(range(zv))
 
         def chosen():
-            b = mine.pop()
+            b = here.pop()
             cp(T.zt[:, b:512:4], win(b, ZO, TO).indirect(T.el[:, 0:8]), ["zf%d" % b, "el"], ["zt%d" % b])
 
-        for b in OPT["forder"]:
+        for b in range(4):
             act(win(b, 1, ZO, 2), win(b, TO, WN).indirect(T.el[:]), AF.Copy, ["wt%d" % b, "el"], ["wf%d" % b])
             op("g", lambda b=b: g.affine_select(win(b, C, ZO, 2), win(b, C + 1, ZO, 2), [[0, SH - 128]], A.is_ge, 0.0, 0, 0),
                ["wf%d" % b], ["we%d" % b])
 
         def layer():
             quant(T.zq[:], T.zs[:], T.zt[:], ["zt0", "zt1", "zt2", "zt3"], ["zq"])
-            for b in OPT["forder"]:
+            for b in range(4):
                 mm(3 + b, 128, T.wq[:, 128 * b:128 * b + 128], T.wsc[:, 128 * b:128 * b + 128], T.zq[:], T.zs[:], ["wq", "wsc", "zq"])
 
         def made(b):
@@ -538,48 +591,24 @@ def rank_program(g, core, T, topo):
             "q": layer, "z": chosen}
         for x in OPT["slots"]:
             if x in "0123":
-                made(OPT["forder"][int(x)])
+                made(int(x))
             else:
                 steps[x]()
 
-        def take(q, b, a, e):
-            rd = ["wt%d" % b, "wf%d" % b, "we%d" % b, "wm%d" % b, "zf%d" % b, "nlist"]
-            out, src = T.xt[:, 64 * a + b:64 * e:4], win(b, 0, WN).indirect(T.nlist[:, a:e])
-            wr = ["xt%d_%d" % (b, k) for k in range(a // 2, e // 2)]
-            if q == "a":
-                act(out, src, AF.Copy, rd, wr, scale=1.0 / 64)
-            else:
-                ts(out, src, 1.0 / 64, None, A.mult, None, rd, wr)
-
-        def state(a, e):
-            n = rnd + 1
-            quant(T["xq%d" % n][:, 16 * a:16 * e], T["xs%d" % n][:, 16 * a:16 * e], T.xt[:, 64 * a:64 * e],
-                  ["xt%d_%d" % (b, k) for b in range(4) for k in range(a // 2, e // 2)], ["xq%d" % n if e == 16 else "xh"])
-
-        if last and OPT["tail"]:
-            for a in (0, 8):
-                for q, b in OPT["ftail"]:
-                    take(q, b, a, a + 8)
-                state(a, a + 8)
+    for x in OPT["end"].split():
+        if x[0] == "Q":
+            state(3, x[1])
         else:
-            for q, b, a, e in OPT["final"]:
-                take(q, b, a, e)
-            state(0, 16)
-
-    whole = ["xq3", "xh"]
-    if OPT["tail"]:
-        for k, tag in enumerate(["xh", "xq3"]):
-            mm(3 + k, 128, T.vq[:], T.vs[:], T.xq3[:, 128 * k:128 * k + 128], T.xs3[:, 128 * k:128 * k + 128], ["vq", tag])
-        dma("s", T.oc[:], T.xq3[:].bitcast(dt.uint8), whole, [])
-        act(T.yo[:, 0:128], bank(3, 0, 128), AF.Copy, ["P3"], ["yo0"])
-        dma("a", T.y[:, 0:128], T.yo[:, 0:128], ["yo0"], [])
-        act(T.yo[:, 128:C], bank(4, 0, 128), AF.Copy, ["P4"], ["yo1"])
-        dma("a", T.y[:, 128:C], T.yo[:, 128:C], ["yo1"], [])
-    else:
-        mm(3, C, T.vq[:], T.vs[:], T.xq3[:], T.xs3[:], ["vq", "xq3"])
-        dma("s", T.oc[:], T.xq3[:].bitcast(dt.uint8), ["xq3"], [])
-        act(T.yo[:], bank(3, 0, C), AF.Copy, ["P3"], ["yo"])
-        dma("a", T.y[:], T.yo[:], ["yo"], [])
+            take(x[0], int(x[2]), x[1])
+    whole = ["xq3U", "xq3L"]
+    for k, s in enumerate("UL"):
+        a, e = half[s]
+        mm(3 + k, H, T.vq[:], T.vs[:], T.xq3[:, a:e], T.xs3[:, a:e], ["vq", "xq3" + s])
+        dma("s", T.oc[:, 4 * a:4 * e], T.xq3[:, a:e].bitcast(dt.uint8), ["xq3" + s], [])
+    for k, s in enumerate("UL"):
+        a, e = half[s]
+        act(T.yo[:, a:e], bank(3 + k, 0, H), AF.Copy, ["P%d" % (3 + k)], ["yo" + s])
+        dma("a", T.y[:, a:e], T.yo[:, a:e], ["yo" + s], [])
     cp(T.nlo[:], T.idw[:].indirect(T.nlist[:]), ["id0", "id1", "id2", "nlist"], ["nlo"])
     for k in range(4):
         dma("s", T.osc[4 * k:4 * k + 4, :], T.xs3[32 * k:32 * k + 4, :], whole, [])

from concourse.bass import DstId, RemoteDMATransfer
from concourse.mybir import dt, AluOpType, ActivationFunctionType

A = AluOpType
AF = ActivationFunctionType
C = 256
H = 128
SH = 192
ZO, TO, WN = 384, 640, 896
STEPS = [1, 2, 4]
BIG = 2.0 ** 88
ETA = 2.0 ** -16
GAP = 191
CODE = "float8_e4m3fn_x4"
OPT = dict(lists="VTBKSMRQDbacOfegdjikhnmlpoqrstuv", slots="szuqpbk01n23", tfirst=1, padv=(0, 2), c0=9, su=(15, 14, 13), sx=(15, 14, 13), eq=4,
           end="aU0 vU1 aU2 vU3 aL0 aL2 vL1 QU vL3 QL", head="",
           order="aU0 vU1 aU2 vU3 aL0 aL2 vL1 QU vL3 QL o nU pU nL SU x10 u10 u9 x12 iU pL u12 x11 x9 iL u11 c5 c7 x8 q0l c6 q0u c4 c2 q2 c1 c3 q3u q3l q1 SR l1 l3 l0 r9 l2 d eU eL b")


def sb(n, d):
    return ("sbuf", [128, n], d)


SCRATCH = {
    "xin": sb(1024, "bfloat16"), "ut": sb(512, "bfloat16"), "vt": sb(512, "bfloat16"),
    "xt": sb(1024, "bfloat16"),
    "wq": sb(512, CODE), "wsc": sb(512, "uint8"),
    "uq": sb(128, CODE), "us": sb(128, "uint8"), "uq2": sb(128, CODE), "us2": sb(128, "uint8"),
    "vq": sb(128, CODE), "vs": sb(128, "uint8"),
    "eq": sb(512, CODE), "es": sb(512, "uint8"), "oq": sb(128, CODE), "osb": sb(128, "uint8"),
    "mq": sb(768, CODE), "ms": sb(768, "uint8"), "mt": sb(4 * 768, "bfloat16"),
    "fq": sb(256, CODE), "fs": sb(256, "uint8"), "zq": sb(128, CODE), "zs": sb(128, "uint8"),
    "zt": sb(512, "bfloat16"), "win": sb(4 * WN, "bfloat16"), "tp": sb(1024, "bfloat16"), "idw": sb(WN, "float32"),
    "et": sb(528, "bfloat16"), "ot": sb(512, "bfloat16"), "one": sb(128, "bfloat16"),
    "pi": sb(4, "int32"), "pf": sb(16, "float32"),
    "yy": sb(256, "bfloat16"), "g16": sb(128, "bfloat16"), "up": sb(256, "bfloat16"),
    "bigm": sb(256, "float32"), "hold": sb(256, "bfloat16"), "drop": sb(256, "bfloat16"),
    "kd": sb(256, "bfloat16"), "k2": sb(256, "bfloat16"),
    "m32": sb(96, "bfloat16"), "k32": sb(96, "bfloat16"),
    "cidx": sb(96, "float32"), "uoff": sb(8, "uint16"),
    "m1": sb(256, "float32"), "tq": sb(256, "float32"), "sg": sb(2048, "bfloat16"), "junk": sb(2048, "bfloat16"),
    "r1": sb(32, "float32"), "rs": sb(2944, "bfloat16"), "dsc": sb(256, "bfloat16"), "csc": sb(256, "float32"),
    "ua": sb(32, "float32"), "i32": sb(32, "bfloat16"), "o32": sb(96, "bfloat16"),
    "gm": sb(192, "bfloat16"), "fx": sb(128, "bfloat16"), "gl": sb(96, "bfloat16"),
    "own": sb(96, "float32"), "w": sb(192, "float32"), "mx": sb(192, "bfloat16"), "ex": sb(128, "bfloat16"), "stay": sb(48, "bfloat16"),
    "offe": sb(16, "uint16"), "le": sb(768, "bfloat16"), "lek": sb(SH, "bfloat16"), "el": sb(12, "uint16"),
    "offn": sb(16, "uint16"), "ln": sb(1024, "bfloat16"), "un": sb(272, "bfloat16"), "ks": sb(3 * C, "float16"),
    "nlist": sb(16, "uint16"),
    "nlo": sb(256, "float32"), "yo": sb(256, "float32"),
    "ps": ("psum", [128, 4096], "float32"),
}
for _k in range(4):
    SCRATCH["xq%d" % _k] = sb(256, CODE)
    SCRATCH["xs%d" % _k] = sb(256, "uint8")
for _k in range(3):
    SCRATCH["pq%d" % _k] = sb(256, CODE)
    SCRATCH["pz%d" % _k] = sb(256, "uint8")

POOL = {"v": 60, "a": 30, "p": 20, "g": 10}
NDMA = 16
SEMAPHORES = (["%s%d" % (q, k) for q in POOL for k in range(POOL[q])] + ["d%d" % k for k in range(NDMA)]
              + ["aq0", "aq1", "aq2", "af0", "af1", "af2", "gone"])


def emit(g, T, ops):
    queue = {"v": g.vector, "a": g.scalar, "p": g.tensor, "g": g, "s": g.sync}
    writer, readers = {}, {}
    deps = []
    for n, (q, fn, rd, wr, ext, dma) in enumerate(ops):
        d = set()
        for t in rd:
            if t in writer:
                d.add(writer[t])
            if t[0] == "P":
                d.update(k for k in readers.get(t, []) if ops[k][0] != q)
        for t in wr:
            if t in writer and not (q == "p" and ops[writer[t]][0] == "p"):
                d.add(writer[t])
            d.update(readers.get(t, []))
        d.discard(n)
        deps.append(d)
        for t in rd:
            readers.setdefault(t, []).append(n)
        for t in wr:
            writer[t] = n
            readers[t] = []
    known = {q: 0 for q in queue}
    issued = {q: 0 for q in queue}
    closure, waits, needed = [], [], set()
    for n, op in enumerate(ops):
        q = op[0]
        mine = []
        for k in sorted(deps[n], reverse=True):
            if not known[q] >> k & 1:
                mine.append(k)
                known[q] |= closure[k]
                needed.add(k)
        waits.append(mine)
        if op[5] == "dma" or op[5] == "far":
            closure.append(known[q] | 1 << n)
        else:
            issued[q] |= 1 << n
            closure.append(known[q] | issued[q])
    count = {q: 0 for q in POOL}
    mark, ndma, open_dma = {}, 0, []
    for n, (q, fn, rd, wr, ext, dma) in enumerate(ops):
        for k in waits[n]:
            queue[q].wait_ge(*mark[k])
        for s, val in ext:
            queue[q].wait_ge(T.sem[s], val)
        ins = fn()
        if dma == "dma":
            mark[n] = (T.sem["d%d" % ndma], 16)
            ndma += 1
            ins.then_inc(*mark[n])
            if n not in needed:
                open_dma.append((q, mark[n]))
        elif n in needed:
            k = count[q]
            count[q] += 1
            sem = T.sem["%s%d" % (q, k % POOL[q])]
            mark[n] = (sem, k // POOL[q] + 1)
            ins.then_inc(sem, 1)
    for q, m in open_dma:
        queue[q].wait_ge(*m)


def rank_program(g, core, T, topo):
    rank = T.rank_of(core)
    if rank is None:
        return
    V, S, PE = g.vector, g.scalar, g.tensor
    ops = []

    def op(q, fn, rd, wr, ext=(), dma=""):
        ops.append((q, fn, list(rd), list(wr), list(ext), dma))

    def ts(out, in0, s1, s2, o0, o1, rd, wr, ext=()):
        if o1 is None:
            op("v", lambda: V.tensor_scalar(out, in0, s1, None, o0), rd, wr, ext)
        else:
            op("v", lambda: V.tensor_scalar(out, in0, s1, s2, o0, o1), rd, wr, ext)

    def tt(out, a, b, o, rd, wr, ext=()):
        op("v", lambda: V.tensor_tensor(out, a, b, o), rd, wr, ext)

    def cp(out, a, rd, wr):
        op("v", lambda: V.tensor_copy(out, a), rd, wr)

    def scan(out, d0, d1, o0, o1, rd, wr, first=0.0):
        op("v", lambda: V.tensor_tensor_scan(out, d0, d1, first, o0, o1), rd, wr)

    def tr(out, a, rd, wr):
        op("v", lambda: V.transpose(out, a), rd, wr)

    def fill(ap, val, wr):
        op("v", lambda: V.memset(ap, val), [], wr)

    def quant(qo, so, a, rd, wr):
        op("v", lambda: V.quantize_mx(qo, so, a), rd, wr)

    def act(out, a, fn, rd, wr, **kw):
        op("a", lambda: S.activation(out, a, fn, **kw), rd, wr)

    def lin(q, out, a, scale, bias, rd, wr):
        if q == "a":
            act(out, a, AF.Identity, rd, wr, scale=scale, bias=bias)
        else:
            ts(out, a, scale, bias, A.mult, A.add, rd, wr)

    def mm(bank, n, lq, ls, rq, rs, rd, start=True, stop=True, ext=()):
        op("p", lambda: PE.matmul_mx(T.ps[:, 512 * bank:512 * bank + n], lq, ls, rq, rs, start, stop),
           rd, ["P%d" % bank], ext)

    def unpack(bank, b, rq, rs, rd, start=True, stop=True, ext=()):
        mm(bank, C, T.eq[:, 128 * b:128 * b + 128], T.es[:, 128 * b:128 * b + 128], rq, rs, ["eq%d" % b] + rd, start, stop, ext)

    def bank(k, a, b):
        return T.ps[:, 512 * k + a:512 * k + b]

    def dma(q, out, a, rd, wr):
        eng = {"s": g.sync, "a": g.scalar}[q]
        op(q, lambda: eng.dma_start(out, a), rd, wr, (), "dma")

    def iota(out, pat, base, mult, wr, small=True):
        if small:
            op("g", lambda: g.iota(out, pat, base, mult, allow_small_or_imprecise_dtypes=True), [], wr)
        else:
            op("g", lambda: g.iota(out, pat, base, mult), [], wr)

    def win(b, a, e, step=1):
        return T.win[:, WN * b + a:WN * b + e:step]

    c0, su, sx = OPT["c0"], OPT["su"], OPT["sx"]
    lanes = [[0, 11, 10, 9], [1, 2, 3, 4], [5, 6, 7, 8], [15, 14, 13, 12]]
    MW = [256, 128, 128, 256]
    MO = [0, 256, 384, 512]
    half = {"U": (H, C), "L": (0, H)}

    def slot(c, a, e):
        k = [c in x for x in lanes].index(True)
        t = lanes[k].index(c)
        return T.mt[:, 4 * (MO[k] + a) + t:4 * (MO[k] + e):4]

    def pad(k):
        a = 16 * min(c if c else 16 for c in lanes[k])
        out = T.mt[:, 4 * (MO[k] + a):4 * (MO[k] + MW[k])]
        wr = ["m%s%d" % ("U" if MW[k] == C else "L", c) for c in lanes[k]]
        if k in OPT["padv"]:
            fill(out, 0.0, wr)
        else:
            act(out, T.et[:, 0:4 * (MW[k] - a)], AF.Copy, ["et"], wr, scale=0.0)

    def summed(c):
        return C + GAP * (c - 1)

    def maskof(es):
        return sum(1 << e for e in es)

    gone = [0]

    dma("s", T.ut[:], T.u[:], [], ["ut"])
    dma("s", T.xin[:, 4 * H:4 * C], T.x[:, 4 * H:4 * C], [], ["xU"])
    dma("s", T.xin[:, 0:4 * H], T.x[:, 0:4 * H], [], ["xL"])
    dma("s", T.wq[:].bitcast(dt.uint8), T.wc[:], ["xU", "xL"], ["wq"])
    dma("s", T.wsc[:], T.ws[:], [], ["wsc"])
    dma("s", T.vt[:], T.v[:], [], ["vt"])

    iota(T.pi[:, 0:1], [[0, 1]], 0, 1, ["pi0"], False)
    iota(T.yy[:], [[0, 16], [1, 16]], 0, 0, ["yy"])
    fill(T.one[:], 1.0, ["one"])
    fill(T.et[:], 0.0, ["et"])
    op("g", lambda: g.affine_select(T.et[:, 3:515:4], T.one[:], [[-1, 128]], A.is_equal, 0.0, 0, 1), ["one"], ["et"])
    iota(T.g16[:], [[16, 8], [0, 16]], 0, 0, ["g16"])
    iota(T.kd[:], [[-16, 16], [4096, 16]], 0, 0, ["kd"])
    for k, bits in enumerate([15, 112, 16]):
        ts(T.pi[:, 1 + k:2 + k], T.pi[:, 0:1], bits, None, A.bitwise_and, None, ["pi0"], ["pi%d" % (k + 1)])
    fill(T.rs[:, summed(0):summed(0) + 1], 0.0, ["r0"])
    fill(T.gm[:], 0.0, ["gm0", "gm1", "gm2"])
    cp(T.pf[:, 0:3], T.pi[:, 1:4], ["pi1", "pi2", "pi3"], ["pf"])
    rr, gp, par = T.pf[:, 0:1], T.pf[:, 1:2], T.pf[:, 2:3]

    def column(q, k, src, scale, bias, rd=()):
        lin(q, T.pf[:, k:k + 1], src, scale, bias, ["pf"] + list(rd), ["pf%d" % k])
        return T.pf[:, k:k + 1]

    pad(0)
    nbig = column("v", 3, rr, -BIG, 0.0)
    hbias = column("v", 4, rr, 64 * BIG, 64 * BIG)
    ts(T.uoff[:], T.yy[:, 0:8], 16.0, None, A.mult, None, ["yy"], ["uoff"])
    unit = ETA / 128
    scale = [column("a", 6, par, -unit / 16, unit), column("a", 7, par, unit / 16, 0.0)]
    column("a", 5, rr, -1025.0, 15375.5 + 32768)
    act(T.bigm[:], T.yy[:], AF.Abs, ["yy", "pf3"], ["bigm"], scale=BIG, bias=nbig)
    shift = [column("a", 8 + k, T.pf[:, 5:6], scale[k], -128 * ETA, ["pf5", "pf%d" % (6 + k)]) for k in range(2)]
    act(T.hold[:], T.yy[:], AF.Relu, ["yy", "pf4"], ["hold"], scale=-64 * BIG, bias=hbias)
    pad(2)
    pad(3)

    def packed_unit(b):
        quant(T.eq[:, 128 * b:128 * b + 128], T.es[:, 128 * b:128 * b + 128], T.et[:, 3 - b:515 - b], ["et"], ["eq%d" % b])

    def state(n, s):
        a, e = half[s]
        src, rd = (T.xin, ["x" + s]) if n == 0 else (T.xt, ["xt%s%d" % (s, b) for b in range(4)])
        quant(T["xq%d" % n][:, a:e], T["xs%d" % n][:, a:e], src[:, 4 * a:4 * e], rd, ["xq%d%s" % (n, s)])

    for b in range(OPT["eq"]):
        packed_unit(b)
    quant(T.uq[:], T.us[:], T.ut[:], ["ut"], ["uq"])
    state(0, "U")
    op("v", lambda: V.tensor_copy(T.uq2[:].bitcast(dt.uint32), T.uq[:].bitcast(dt.uint32).indirect(T.uoff[:])),
       ["uq", "uoff"], ["uq2"])
    state(0, "L")
    for b in range(OPT["eq"], 4):
        packed_unit(b)
    act(T.us2[:], T.us[:].indirect(T.uoff[:]), AF.Copy, ["uq", "uoff"], ["us2"])
    pad(1)
    act(T.drop[:], T.hold[:], AF.Identity, ["hold"], ["drop"], scale=2.0 ** -76, bias=-1024.0)

    def ones():
        for t in range(4):
            ts(T.ot[:, t:512:4], T.g16[:], gp, None, A.is_equal, None, ["g16", "pf"], ["ot%d" % t])
        quant(T.oq[:], T.osb[:], T.ot[:], ["ot0", "ot1", "ot2", "ot3"], ["oq"])

    lt, same, far, ieta = T.m32[:, 0:32], T.m32[:, 64:96], T.cidx[:, 48:64], T.cidx[:, 64:80]

    def later_constants():
        first = column("a", 10, rr, 16.0, 256.0)
        column("a", 11, rr, -1.0, 47.0)
        act(T.k32[:], T.k32[:], AF.Sign, ["k32"], ["k32"])
        lin("a", far, T.yy[:, 0:16], 1.0, first, ["yy", "pf10"], ["far"])
        lin("a", T.pf[:, 12:13], par, -1.0, T.pf[:, 11:12], ["pf", "pf11"], ["pf12"])
        lin("a", T.k32[:, 80:81], par, -1.0 / 16, 1.0, ["pf", "k32"], ["k16"])
        lin("a", ieta, far, ETA, -256 * ETA, ["far"], ["ieta"])

    masks = [lambda: ts(same, T.g16[:, 0:32], par, None, A.is_equal, None, ["g16", "pf"], ["same"]),
             lambda: ts(lt, T.yy[:, 0:32], rr, None, A.is_gt, None, ["yy", "pf"], ["lt"]),
             lambda: tt(lt, lt, same, A.mult, ["lt", "same"], ["lt"]),
             lambda: ts(T.stay[:], T.stay[:], T.pf[:, 12:13], None, A.is_lt, None, ["stay", "pf12"], ["stay"]),
             lambda: lin("v", T.m32[:, 32:64], lt, -2.0, 0.0, ["lt"], ["sl"]),
             lambda: tt(T.m32[:, 32:64], T.m32[:, 32:64], same, A.add, ["sl", "same"], ["sl"])]

    def beside():
        if masks:
            masks.pop(0)()

    def take(q, b, s):
        a, e = half[s]
        rd = ["wt%d" % b, "wf%d" % b, "we%d" % b, "wm%d" % b, "zf%d" % b, "nlist"]
        out, src = T.xt[:, 4 * a + b:4 * e:4], win(b, 0, WN).indirect(T.nlist[:, a // 16:e // 16])
        if q == "a":
            act(out, src, AF.Copy, rd, ["xt%s%d" % (s, b)], scale=1.0 / 64)
        else:
            ts(out, src, 1.0 / 64, None, A.mult, None, rd, ["xt%s%d" % (s, b)])

    mine, theirs, sums = {"U": 2, "L": 0}, {"U": 1, "L": 7}, {"U": 2, "L": 1}
    tb = [7, 2, 0, 1]

    for rnd, h in enumerate(STEPS):
        mate = T.cores[rank ^ h]
        rid, pid, _ = topo.addr(mate)
        eng = topo.engines(core, mate)
        xq, xs, pq, pz = T["xq%d" % rnd], T["xs%d" % rnd], T["pq%d" % rnd], T["pz%d" % rnd]
        X = ["xq%dU" % rnd, "xq%dL" % rnd]
        last = rnd == len(STEPS) - 1

        def send(out, a, sem, rd, pid=pid, rid=rid, eng=eng):
            op("g", lambda: g.remote_dma(out, a, T.sem[sem], T.sem.gone, pid, rid, maskof(eng)), rd, [], (), "far")
            gone[0] += len(eng)

        def scores(s):
            a, e = half[s]
            if rnd > 0:
                state(rnd, s)
            for k in (mine[s], theirs[s]):
                if k == mine[s] or s == "U" or sx:
                    mm(k, H, T.uq2[:], T.us2[:], xq[:, a:e], xs[:, a:e], ["uq2", "us2", "xq%d%s" % (rnd, s)])
            if s == "U":
                return
            for b in range(4):
                unpack(3 + b, b, xq[:], xs[:], X)
            send(pq[:].bitcast(dt.uint8), xq[:].bitcast(dt.uint8), "aq%d" % rnd, X)
            send(pz[:], xs[:], "aq%d" % rnd, X)
            if rnd == 0:
                iota(T.k2[:, 0:128], [[-4096, 128]], 127 * 4096, 0, ["k2a"])
                iota(T.k2[:, 128:256], [[0, 128]], 4096, 0, ["k2b"])
                iota(T.stay[:], [[1, 48]], 0, 0, ["stay"])
                iota(T.k32[:], [[0, 3], [1, 32]], 0, 0, ["k32"])
                iota(T.own[:, 0:18], [[0, 18]], 0, 0, ["kb"])
                iota(T.w[:, 0:80], [[0, 80]], 0, 0, ["mm", "hh"])
                iota(T.un[:, 0:1], [[0, 1]], 1, 0, ["un0"])
            iota(T.le[:, 128:SH], [[0, SH - 128]], C, 0, ["le"])
            if rnd > 0:
                iota(T.ln[:, 2 * C:4 * C], [[0, 2 * C]], -1024, 0, ["ln"])
            if last:
                iota(T.idw[:, ZO:WN], [[1, WN - ZO]], ZO - TO, 0, ["id0"])

        def masked(s):
            a, e = half[s]
            tt(T.m1[:, a:e], bank(mine[s], 0, H), T.bigm[:, a:e], A.add, ["P%d" % mine[s], "bigm"], ["m1" + s])

        def pivots(s):
            a, e = half[s]
            scan(T.tq[:, a:e], T.hold[:, a:e], T.m1[:, a:e], A.add, A.min, ["hold", "m1" + s], ["tq" + s])

        def inside(s):
            a, e = half[s]
            tt(slot(0, a, e), bank(mine[s], 0, H), T.tq[:, a:e], A.is_gt, ["P%d" % mine[s], "tq" + s], ["m%s0" % s])

        def pivot(c):
            return T.tq[:, 16 * c + 15:16 * c + 16], "tqU" if c >= 8 else "tqL"

        def rows(c, s):
            return half[s][0], min(half[s][1], 16 * c)

        def compare(c, s):
            a, e = rows(c, s)
            ts(slot(c, a, e), bank(mine[s], 0, e - a), pivot(c)[0], None, A.is_ge, None, ["P%d" % mine[s], pivot(c)[1]], ["m%s%d" % (s, c)])

        def signs(c, s):
            a, e = rows(c, s)
            act(T.sg[:, C * (15 - c) + a:C * (15 - c) + e], bank(theirs[s], 0, e - a), AF.Sign, ["P%d" % theirs[s], pivot(c)[1]],
                ["sg%s%d" % (s, c)], bias=pivot(c)[0], scale=-1.0)

        def beaten(c):
            a, e, ss = (0, 16 * c, "UL") if c in sx else (H, 16 * c, "U")
            more = dict(accum_out=T.r1[:, c:c + 1]) if c in sx else {}
            act(slot(c, a, e), T.sg[:, C * (15 - c) + a:C * (15 - c) + e], AF.Sign, ["sg%s%d" % (s, c) for s in ss],
                ["m%s%d" % (s, c) for s in ss] + ["q%d" % c], bias=1.0, scale=-1.0, **more)

        def by_scalar():
            for c in su:
                signs(c, "U")
            for c in su:
                if c not in sx:
                    beaten(c)
            for c in sx:
                signs(c, "L")
            for c in sx:
                beaten(c)

        def scalar_sums():
            for c in range(15, c0 - 1, -1):
                if c not in sx:
                    act(T.junk[:, 8 * c * (c - 1):8 * c * (c + 1)], slot(c, 0, 16 * c), AF.Copy, ["mL%d" % c, "mU%d" % c], ["q%d" % c],
                        accum_out=T.r1[:, c:c + 1])
            act(T.rs[:, summed(c0):summed(15) + 1:GAP], T.r1[:, c0:16], AF.Copy, ["q%d" % c for c in range(c0, 16)],
                ["r%d" % c for c in range(c0, 16)])

        def rowsum(c):
            if c < c0:
                scan(T.rs[:, summed(c) + 1 - 16 * c:summed(c) + 1], slot(c, 0, 16 * c), slot(c, 0, 16 * c), A.add, A.max,
                     ["mL%d" % c, "mU%d" % c], ["r%d" % c])

        def rowsums(t):
            if 5 + t >= c0:
                return rowsum(1 + t)
            scan(T.rs[:, GAP * t:GAP * t + 4 * C - 3:4], T.mt[:, 4 * MO[1] + t:4 * MO[3]:4], T.k2[:], A.add, A.min,
                 ["mL%d" % (1 + t), "mL%d" % (5 + t), "k2a", "k2b"], ["r%d" % (1 + t), "r%d" % (5 + t)])

        done = {"U": 0, "L": 0}

        def packed(k, s):
            a = MO[k] + half[s][0]
            quant(T.mq[:, a:a + H], T.ms[:, a:a + H], T.mt[:, 4 * a:4 * (a + H)], ["m%s%d" % (s, c) for c in lanes[k]], ["mq%d%s" % (k, s)])
            done[s] += 1
            mm(sums[s], H, T.oq[:], T.osb[:], T.mq[:, a:a + H], T.ms[:, a:a + H], ["oq", "mq%d%s" % (k, s)],
               done[s] == 1, done[s] == (2 if s == "U" else 4))

        def own_copy(b):
            act(win(b, TO, WN), bank(3 + b, 0, C), AF.Copy, ["P%d" % (3 + b)], ["wt%d" % b], scale=64.0)

        def column_sums(s):
            a, e = half[s]
            scan(T.csc[:, a:e], T.drop[:, a:e], bank(sums[s], 0, H), A.add, A.min, ["drop", "P%d" % sums[s]], ["csc" + s])

        ub, rk = T.ua[:, 0:16], T.ua[:, 16:32]
        for x in OPT["head"].split() + OPT["order"].split():
            if x[0] in "av":
                if rnd > 0:
                    take(x[0], int(x[2]), x[1])
            elif x[0] in "Qnpie":
                {"Q": scores, "n": masked, "p": pivots, "i": inside, "e": column_sums}[x[0]](x[1])
            elif x[0] in "xc":
                if int(x[1:]) not in sx:
                    compare(int(x[1:]), "L")
            elif x[0] == "u":
                if int(x[1:]) not in su:
                    compare(int(x[1:]), "U")
            elif x[0] == "q":
                packed(int(x[1]), x[2:].upper() or "L")
            elif x[0] == "r":
                rowsum(int(x[1:]))
            elif x[0] == "l":
                rowsums(int(x[1:]))
            elif x == "d":
                scan(T.dsc[:], slot(0, 0, C), T.kd[:], A.add, A.min, ["kd", "mU0", "mL0"], ["dsc"])
            elif x == "b":
                tt(ub, T.dsc[:, 15:C:16], T.rs[:, summed(0):summed(15) + 1:GAP], A.add, ["dsc"] + ["r%d" % c for c in range(16)], ["ub"])
            elif x == "o":
                if rnd == 0:
                    ones()
            elif x == "SU":
                by_scalar()
            elif x == "SR":
                scalar_sums()
        for b in range(OPT["tfirst"]):
            own_copy(b)
        if rnd == 0:
            later_constants()
        beside()
        tt(rk, T.csc[:, 15:C:16], ub, A.subtract, ["cscU", "cscL", "ub"], ["rk"])
        beside()
        for k in range(2):
            ts(T.i32[:, 16 * k:16 * k + 16], rk, scale[k], shift[k], A.mult, A.add, ["rk", "pf6", "pf7", "pf8", "pf9"], ["i32%d" % k])
        beside()
        tr(T.o32[:, 32 * rnd:32 * rnd + 32], T.i32[:], ["i320", "i321"], ["o%d" % rnd])
        beside()
        gm, gb, gl = T.gm[:, 64 * rnd + 8:64 * rnd + 24], T.gm[:, 64 * rnd + 7:64 * rnd + 23], T.gl[:, 32 * rnd:32 * rnd + 16]
        G = "gm%d" % rnd
        lo, hi = T.o32[:, 32 * rnd:32 * rnd + 16], T.o32[:, 32 * rnd + 16:32 * rnd + 32]
        tt(gm, lo, hi, A.add, ["o%d" % rnd], [G])
        beside()
        fold = RemoteDMATransfer(dst_ids=[DstId(rid=rid, pnc=pid)], dma_engine_mask=maskof(eng), remote_sem=T.sem["af%d" % rnd],
                                 srcs=[lo, hi], dsts=[gl], alu_op=1)
        op("g", lambda fold=fold: g.remote_dma_fused([fold], local_sem=T.sem.gone), ["o%d" % rnd], [], (), "far")
        gone[0] += len(eng)
        if rnd == 0:
            iota(T.up[:], [[1, 16], [16, 16]], 1, 0, ["up"])
            iota(T.ln[:, 2 * C:4 * C], [[0, 2 * C]], -1024, 0, ["ln"])

        o, fx = T.own, T.fx
        kb, dk, thr, of = o[:, 1:17], T.cidx[:, 0:17], o[:, 64:80], fx[:, 127:128]
        for b in range(4):
            unpack(tb[b], b, pq[:], pz[:], [], ext=[("aq%d" % rnd, 2 * len(eng))] if b == 0 else [])
        for b in range(4):
            act(T.tp[:, b:1024:4], bank(tb[b], 0, C), AF.Copy, ["P%d" % tb[b]], ["tp%d" % b], scale=-1.0)
        for b in range(4):
            unpack(tb[b], b, xq[:], xs[:], X, True, False)
        for b in range(OPT["tfirst"], 4):
            own_copy(b)

        def difference():
            quant(T.fq[:], T.fs[:], T.tp[:], ["tp0", "tp1", "tp2", "tp3"], ["fq"])
            for b in range(4):
                unpack(tb[b], b, T.fq[:], T.fs[:], ["fq"], False, True)
            for b in range(4):
                act(win(b, ZO, TO), bank(tb[b], 0, C), AF.Copy, ["P%d" % tb[b]], ["zf%d" % b])

        steps = {
            "k": lambda: ts(kb, gm, 1.5 * ETA, 511 * ETA, A.is_gt, A.mult, [G], ["kb"]),
            "t": lambda: ts(thr, gm, 0.5 * ETA, None, A.is_lt, None, [G], ["thr"]),
            "s": lambda: scan(fx[:, 47::-1], T.stay[:], T.gm[:, 64 * rnd + 8:64 * rnd + 56], A.mult, A.add, ["stay", G], ["fx"]),
            "m": lambda: tt(kb, kb, ieta, A.max, ["kb", "ieta"], ["kb"]),
            "r": lambda: tr(fx[:, 64:96], fx[:, 0:32], ["fx"], ["fxt"]),
            "d": lambda: tt(dk, o[:, 1:18], o[:, 0:17], A.subtract, ["kb"], ["dk"]),
            "o": lambda: scan(fx[:, 96:128], T.k32[:, 64:96], fx[:, 64:96], A.mult, A.add, ["k32", "k16", "fxt"], ["of"]),
            "v": lambda: rnd == 1 and quant(T.vq[:], T.vs[:], T.vt[:], ["vt"], ["vq"]),
            "b": beside, "q": difference}
        waiting = steps

        w, mx, ex = T.w, T.mx, T.ex
        mm_, hh = w[:, 1:17], w[:, 32:48]
        t1, nq, p2, p1 = w[:, 128:144], w[:, 144:160], w[:, 160:176], w[:, 96:113]
        oh, om, sc = ex[:, 127:128], mx[:, 159:160], mx[:, 191:192]
        came = [[("af%d" % rnd, len(eng))]]

        def arrived():
            return came.pop() if came else []

        steps = {
            "a": lambda: tt(hh, gl, thr, A.is_gt, ["thr"], ["hh"], ext=arrived()),
            "b": lambda: tt(mm_, gm, gl, A.min, [G], ["mm"], ext=arrived()),
            "c": lambda: tt(t1, gl, thr, A.is_le, ["thr"], ["t1"], ext=arrived()),
            "d": lambda: tt(nq, gl, gm, A.is_ge, [G], ["nq"], ext=arrived()),
            "e": lambda: scan(ex[:, 47::-1], T.stay[:], w[:, 32:80], A.mult, A.add, ["stay", "hh"], ["ex"]),
            "f": lambda: scan(p1, dk, w[:, 1:18], A.add, A.add, ["dk", "mm"], ["p1"]),
            "g": lambda: tt(t1, t1, far, A.mult, ["t1", "far"], ["t1"]),
            "h": lambda: scan(p2, gb, w[:, 0:16], A.add, A.subtract, [G, "mm", "of"], ["p2"], of),
            "i": lambda: tr(ex[:, 64:96], ex[:, 0:32], ["ex"], ["ext"]),
            "j": lambda: ts(mx[:, 0:64], T.m32[:, 0:64], w[:, 112:113], None, A.mult, None, ["lt", "sl", "p1"], ["mx"]),
            "k": lambda: tt(t1, t1, ex[:, 47:31:-1], A.add, ["t1", "ex"], ["t1"]),
            "l": lambda: tt(p2, p2, nq, A.subtract, ["p2", "nq"], ["p2"]),
            "m": lambda: scan(ex[:, 96:128], T.k32[:, 64:96], ex[:, 64:96], A.mult, A.add, ["k32", "k16", "ext"], ["oh"]),
            "n": lambda: tr(mx[:, 64:128], mx[:, 0:64], ["mx"], ["mxt"]),
            "o": lambda: ts(T.offe[:], t1, oh, -1.0, A.add, A.add, ["t1", "oh"], ["offe"]),
            "p": lambda: scan(mx[:, 128:192], T.k32[:, 0:64], mx[:, 64:128], A.mult, A.add, ["k32", "mxt"], ["sums"]),
            "q": lambda: ts(p2, p2, sc, 768 * ETA, A.add, A.add, ["p2", "sums"], ["p2"]),
            "r": lambda: cp(T.le[:].indirect(T.offe[:]), T.up[:], ["offe", "up"], ["le"]),
            "s": lambda: tt(p2, p2, w[:, 96:112], A.max, ["p2", "p1"], ["p2"]),
            "t": lambda: scan(T.lek[:], T.hold[:, 0:SH], T.le[:, 0:SH], A.add, A.min, ["hold", "le"], ["lek"]),
            "u": lambda: ts(T.offn[:], p2, om, 1.0 / ETA, A.add, A.mult, ["p2", "sums"], ["offn"]),
            "v": lambda: ts(T.el[:], T.lek[:, 15:SH:16], -1.0, None, A.add, None, ["lek"], ["el"])}
        for x in OPT["lists"]:
            (steps if x.islower() else waiting)[x.lower()]()
        if last:
            for k in range(2):
                lin("a", T.idw[:, k:ZO:2], T.le[:, 0:SH], 1.0, -1.0, ["le"], ["id%d" % (k + 1)])

        zv = OPT["slots"].count("z")
        for b in range(zv, 4):
            act(T.zt[:, b:512:4], win(b, ZO, TO).indirect(T.el[:, 0:8]), AF.Copy, ["zf%d" % b, "el"], ["zt%d" % b])
        here = list(range(zv))

        def chosen():
            b = here.pop()
            cp(T.zt[:, b:512:4], win(b, ZO, TO).indirect(T.el[:, 0:8]), ["zf%d" % b, "el"], ["zt%d" % b])

        for b in range(4):
            act(win(b, 1, ZO, 2), win(b, TO, WN).indirect(T.el[:]), AF.Copy, ["wt%d" % b, "el"], ["wf%d" % b])
            op("g", lambda b=b: g.affine_select(win(b, C, ZO, 2), win(b, C + 1, ZO, 2), [[0, SH - 128]], A.is_ge, 0.0, 0, 0),
               ["wf%d" % b], ["we%d" % b])

        def layer():
            quant(T.zq[:], T.zs[:], T.zt[:], ["zt0", "zt1", "zt2", "zt3"], ["zq"])
            for b in range(4):
                mm(3 + b, 128, T.wq[:, 128 * b:128 * b + 128], T.wsc[:, 128 * b:128 * b + 128], T.zq[:], T.zs[:], ["wq", "wsc", "zq"])

        def made(b):
            tt(win(b, 0, C, 2), bank(3 + b, 0, 128), win(b, 1, C, 2), A.add, ["P%d" % (3 + b), "wf%d" % b], ["wm%d" % b])

        pair, best, kept = T.ks[:, 0:C], T.ks[:, C:2 * C], T.ks[:, 2 * C:3 * C]
        steps = {
            "s": lambda: cp(T.ln[:].indirect(T.offn[:]), T.up[:], ["offn", "up"], ["ln"]),
            "u": lambda: ts(T.un[:, 1:C + 1], T.ln[:, 2 * C:3 * C], 0.0, None, A.is_lt, None, ["ln"], ["un"]),
            "p": lambda: scan(pair, T.un[:, 1:C + 1], T.un[:, 0:C], A.add, A.add, ["un", "un0"], ["pair"], -1.0 - TO),
            "b": lambda: scan(best, pair, T.ln[:, 3 * C:4 * C], A.max, A.max, ["pair", "ln"], ["best"], -1024.0),
            "k": lambda: scan(kept, T.hold[:], best, A.add, A.min, ["hold", "best"], ["kept"]),
            "n": lambda: ts(T.nlist[:], T.ks[:, 2 * C + 15:3 * C:16], TO - 1.0, None, A.add, None, ["kept"], ["nlist"]),
            "q": layer, "z": chosen}
        for x in OPT["slots"]:
            if x in "0123":
                made(int(x))
            else:
                steps[x]()

    for x in OPT["end"].split():
        if x[0] == "Q":
            state(3, x[1])
        else:
            take(x[0], int(x[2]), x[1])
    whole = ["xq3U", "xq3L"]
    for k, s in enumerate("UL"):
        a, e = half[s]
        mm(3 + k, H, T.vq[:], T.vs[:], T.xq3[:, a:e], T.xs3[:, a:e], ["vq", "xq3" + s])
        dma("s", T.oc[:, 4 * a:4 * e], T.xq3[:, a:e].bitcast(dt.uint8), ["xq3" + s], [])
    for k, s in enumerate("UL"):
        a, e = half[s]
        act(T.yo[:, a:e], bank(3 + k, 0, H), AF.Copy, ["P%d" % (3 + k)], ["yo" + s])
        dma("a", T.y[:, a:e], T.yo[:, a:e], ["yo" + s], [])
    cp(T.nlo[:], T.idw[:].indirect(T.nlist[:]), ["id0", "id1", "id2", "nlist"], ["nlo"])
    for k in range(4):
        dma("s", T.osc[4 * k:4 * k + 4, :], T.xs3[32 * k:32 * k + 4, :], whole, [])
    dma("s", T.nl[:], T.nlo[0:128:16, :], ["nlo"], [])
    emit(g, T, ops)
    g.wait_ge(T.sem.gone, gone[0])
